import numpy as np, ml_dtypes
CORES = [10,34,74,98]
N = 4
BF = ml_dtypes.bfloat16
def gentries(a):
    return np.ascontiguousarray(a.reshape(8, 16, -1).transpose(0, 2, 1)).reshape(8, -1)
def gtable(e):
    e = np.asarray(e); return np.ascontiguousarray(e.reshape(8, -1, 16).transpose(0, 2, 1)).reshape(128, -1).astype(np.int32)
V, H, Q, ST = 4096, 512, 4, 3
MOST, SAME = 2 ** (Q + 1) - 1, 7
def sizes(w):
    return 1 + np.minimum((w * (V - 1 - H)) // np.add.reduce(w, axis=-1, keepdims=True), MOST - 1)
def usual(rng):
    return sizes((1000 * rng.standard_exponential((N, 8, H))).astype(np.int64) + 1)
def forest(rng, n, stale, last):
    pool = rng.permutation(V - 1) + 1; r = np.zeros((Q + 1, H), np.int64)
    if last: pool = np.concatenate([pool[pool == V - 1], pool[pool != V - 1]])
    c = rng.integers(0, V, (Q, V)) if stale else np.zeros((Q, V), np.int64)
    high = pool[:0]; at = 0
    for o in range(Q, -1, -1):
        hs = np.nonzero((n >> o) & 1)[0]
        a = pool[at:at + hs.size]; at += hs.size; r[o, hs] = a
        k = pool[at:at + high.size]; at += high.size
        if o < Q: c[o, high] = k
        high = np.concatenate([high, a, k])
    return r, c
def forests(rng, n, stale=False, last=False):
    p = [[forest(rng, n[q, g], stale, last) for g in range(8)] for q in range(N)]
    return np.array([[x[0] for x in a] for a in p]), np.array([[x[1] for x in a] for a in p])
def records(rng):
    v = rng.integers(0, 256, (N, 8, 16, V))
    lev = np.clip(rng.integers(0, 256, (N, 8, 1, V)) + rng.integers(-40, 41, (N, 8, 16, V)), 0, 255)
    return np.where(rng.random((N, 8, 1, V)) < 0.5, v, lev)
def pack(v, r, c):
    return {"rec": np.ascontiguousarray(v.reshape(N, 128, V)).astype(np.float32).astype(BF), "rt": np.stack([gtable(a.reshape(8, -1)) for a in r]),
            "ch": np.ascontiguousarray(c.reshape(N, 8, Q * V)).astype(np.int32)}
def setup_inputs(rng):
    r, c = forests(rng, usual(rng)); return pack(records(rng), r, c)
def setup_inputs_alike(rng):
    n = usual(rng); n[:, 0] = 1; n[:, 2] = SAME
    for q in range(N):
        n[q, 4] = rng.permutation(2 ** (np.arange(H) % (Q + 1)))
        room = MOST - n[q, 6]; before = np.add.accumulate(room) - room
        n[q, 6] = n[q, 6] + np.clip(V - 1 - np.add.reduce(n[q, 6]) - before, 0, room)
        for g in (5, 7):
            more = 2 ** (1 + (q + g // 2) % Q) - 1; many = min(H, (V - 1 - H) // more)
            n[q, g] = rng.permutation(1 + more * (np.arange(H) < many).astype(np.int64))
    r, c = forests(rng, n, last=True); v = records(rng)
    for q in range(N):
        for g in (1, 3): v[q, g] = v[q, g][:, rng.integers(0, 8, V)]
    return pack(v, r, c)
def setup_inputs_ties(rng):
    r, c = forests(rng, usual(rng))
    base = np.array([1, 128, 254, 128, 1, 254, 128, 128])[rng.permutation(8)].reshape(1, 8, 1, 1)
    k = rng.choice(np.array([0, 7, 8, 9, 16]), (N, 8, 1, V)); low = rng.integers(0, 2, (N, 8, 1, V))
    up = np.argsort(rng.random((N, 8, 16, V), dtype=np.float32), axis=2) < k
    return pack(base + np.where(up, 1, -low), r, c)
def setup_inputs_tall(rng):
    n = np.ones((N, 8, H), np.int64)
    run = [np.full((V - 1 - H) // (MOST - 1), MOST), 2 ** Q + 1 - (np.arange(2 * ((V - 1 - H) // MOST)) & 1)]
    st = np.stack([rng.integers(1, H - run[g & 1].size + 1, N) for g in range(8)], axis=1)
    for q in range(N):
        for g in range(8): n[q, g, st[q, g]:st[q, g] + run[g & 1].size] = run[g & 1]
    r, c = forests(rng, n); v = rng.integers(100, 256, (N, 8, 16, V))
    for q in range(N):
        for g in range(8):
            k = np.arange(run[g & 1].size); h = st[q, g] + k
            o = np.where((k + (0 if g & 1 else int(rng.integers(0, 2)))) & 1 == 1, Q, 0)
            v[q, g][:, r[q, g, o, h]] = rng.integers(0, 100, (16, k.size))
            v[q, g][:, r[q, g, 0, 0]] = (np.arange(16) == rng.integers(0, 16)).astype(np.int64)
    return pack(v, r, c)
def setup_inputs_stale(rng):
    n = usual(rng); n[:, :, 0] = 1
    r, c = forests(rng, n, True); v = records(rng); v[..., 0] = 0
    for q in range(N):
        for g in range(8):
            t = (0, 1, H - 1, H, 4080, H // 2)[(q + g) % 6]
            v[q, g][:, r[q, g, 0, 0]] = rng.permutation(np.clip(t - 255 * np.arange(16), 0, 255))
    return pack(v, r, c)
def setup_inputs_spread(rng):
    r, c = forests(rng, sizes(np.exp2(12 * rng.random((N, 8, H))).astype(np.int64)))
    v = (np.exp2(8 * rng.random((N, 8, 1, V))) * rng.random((N, 8, 16, V))).astype(np.int64); u = rng.random((N, 8, 1, V))
    return pack(np.where(u < 0.0625, 0, np.where(u > 0.9375, 255, np.minimum(v, 255))), r, c)
def check_inputs(d):
    bad = []
    x = np.asarray(d["rec"]).astype(np.float32)
    if not np.all((x >= 0) & (x <= 255) & (x == np.floor(x))): bad.append("whole numbers from 0 to 255 in rec")
    for k in ("rt", "ch"):
        if np.min(d[k]) < 0 or np.max(d[k]) > V - 1: bad.append("range of " + k)
    if "range of rt" in bad or "range of ch" in bad: return bad
    empty, lack, twice = False, False, False
    for q in range(N):
        rr = gentries(d["rt"][q]).reshape(8, Q + 1, H); cc = np.asarray(d["ch"][q]).reshape(8, Q, V)
        for g in range(8):
            if not np.all(np.max(rr[g], axis=0) > 0): empty = True
            high = np.zeros(0, np.int64)
            for o in range(Q, -1, -1):
                a = rr[g, o][rr[g, o] > 0].astype(np.int64); k = cc[g, o][high].astype(np.int64) if o < Q else high
                if np.any(k == 0): lack = True
                high = np.concatenate([high, a, k])
            if np.unique(high).size != high.size: twice = True
    if empty: bad.append("every heap has a root")
    if lack: bad.append("every child that counts is a node")
    if twice: bad.append("no node stands twice")
    return bad
def pick(v, ix):
    return np.take_along_axis(v, ix[:, :, None, :], 3)
def beats(x, y):
    return np.add.reduce((x < y).astype(np.int64), axis=2) >= 9
def reference(rec, rt, ch):
    v = rec.astype(np.float32).astype(np.int64).reshape(N, 8, 16, V); kid = ch.astype(np.int64).reshape(N, 8, Q, V)
    root = np.stack([gentries(a) for a in rt]).astype(np.int64).reshape(N, 8, Q + 1, H)
    for step in range(ST):
        m = root[:, :, 0].copy(); order = np.zeros_like(m)
        for o in range(1, Q + 1):
            a = root[:, :, o]; w = (a > 0) & ((m == 0) | beats(pick(v, a), pick(v, m)))
            m = np.where(w, a, m); order = np.where(w, o, order)
        for o in range(Q + 1): root[:, :, o] = np.where(order == o, 0, root[:, :, o])
        z = pick(v, m); got = np.roll(z, 1, axis=0)
        s = np.add.reduce(got[:, :, :, 0], axis=2) & (H - 1)
        np.put_along_axis(v, m[:, :, None, :], (z + got) >> 1, 3)
        j = (np.arange(H) + s[:, :, None]) & (H - 1)
        mj = np.take_along_axis(m, j, 2); oj = np.take_along_axis(order, j, 2)
        c = m
        for o in range(Q):
            a = root[:, :, o].copy(); b = np.where(o < oj, np.take_along_axis(kid[:, :, o], mj, 2), 0)
            n = (a > 0).astype(np.int64) + (b > 0) + (c > 0); link = n >= 2
            x = np.where((n == 2) & (a > 0), a, b); y = np.where(c > 0, c, b)
            win = beats(pick(v, y), pick(v, x)); wn = np.where(win, y, x); ls = np.where(win, x, y)
            rl = pick(v, ls); new = rl + np.clip(pick(v, wn) - rl, -1, 1)
            i = np.nonzero(link)
            v[i[0], i[1], :, ls[i]] = new.transpose(0, 1, 3, 2)[i]
            kid[i[0], i[1], o, wn[i]] = ls[i]
            root[:, :, o] = np.where(n == 1, a + b + c, np.where(n == 3, a, 0))
            c = np.where(link, wn, 0)
        root[:, :, Q] = np.where(root[:, :, Q] > 0, root[:, :, Q], c)
    return {"yrec": v.reshape(N, 128, V).astype(np.float32).astype(BF), "yrt": np.stack([gtable(a.reshape(8, -1)) for a in root]).astype(np.float32)}

@@ -1,0 +1,656 @@
+from concourse.mybir import AluOpType, ActivationFunctionType
+
+V, H, ST = 4096, 512, 3
+CW = [4096, 2560, 2560]
+NB = [V]
+for _t in range(ST):
+    NB.append(NB[-1] + 16 + CW[_t] + 4608 + 2048)
+BIG = 60000.0
+MAGIC = 12582912.0
+MAGIC16 = 201326592.0
+EXACT = True
+MF = ()
+CF = (2, 3, 4)
+MPA = True
+SPLIT = 2
+LOOK, WAKE, TRIES = 0.5, 0.12, 1500
+NDMA = 12
+
+SCRATCH = {
+    "G": ("sbuf", [128, NB[ST]], "bfloat16"),
+    "O": ("sbuf", [128, V + H], "bfloat16"),
+    "TB": ("sbuf", [128, V], "bfloat16"),
+    "CHI": ("sbuf", [128, 1024], "int32"),
+    "HI": ("sbuf", [128, 1024], "bfloat16"),
+    "LO": ("sbuf", [128, 1024], "bfloat16"),
+    "RT": ("sbuf", [128, 160], "int32"),
+    "YR": ("sbuf", [128, 160], "float32"),
+    "WB": ("sbuf", [128, 24576], "bfloat16"),
+    "F": ("sbuf", [128, 18432], "float32"),
+    "IP": ("sbuf", [128, 1024], "int32"),
+    "U": ("sbuf", [128, 2560], "uint16"),
+}
+for _t in range(ST):
+    SCRATCH["Z%d" % _t] = ("sbuf", [128, H], "bfloat16")
+    SCRATCH["W%d" % _t] = ("sbuf", [128, H], "bfloat16")
+    SCRATCH["ZT%d" % _t] = ("sbuf", [128, 16], "bfloat16")
+    SCRATCH["WT%d" % _t] = ("sbuf", [128, 16], "bfloat16")
+for _b in range(8):
+    SCRATCH["ps%d" % _b] = ("psum", [128, 512], "float32")
+SEMAPHORES = (["cv", "ca", "cp", "cg", "sent"] + ["d%d" % k for k in range(NDMA)]
+              + ["aw%d" % k for k in range(ST)] + ["at%d" % k for k in range(ST)])
+
+A = AluOpType
+ACT = ActivationFunctionType
+CY = 0.83e-3 * 1.25
+PC = 0.42e-3 * 1.25
+WIDE2 = ("G", "O", "TB", "HI", "LO", "WB", "U")
+PLAN = {}
+
+
+def sub(a, lo, n, st=1):
+    return (a[0], a[1] + lo * a[3], n, a[3] * st)
+
+
+def meet(a, b):
+    alo, ahi = a[1], a[1] + (a[2] - 1) * a[3]
+    blo, bhi = b[1], b[1] + (b[2] - 1) * b[3]
+    if ahi < blo or bhi < alo:
+        return False
+    if EXACT and a[3] == b[3] and a[3] > 1 and (alo - blo) % a[3] != 0:
+        return False
+    return True
+
+
+def two(a):
+    return a[0] in WIDE2 or a[0][0] in "ZW"
+
+
+def build(g, T, nxt_addr, nxt_mask, neng):
+    ops = []
+    fill = {"WB": 0, "F": 0, "IP": 0, "U": 0, "d": 0}
+
+    def R(a):
+        if a[3] == 1:
+            return T[a[0]][:, a[1]:a[1] + a[2]]
+        return T[a[0]][:, a[1]:a[1] + (a[2] - 1) * a[3] + 1:a[3]]
+
+    def new(pool, n):
+        lo = fill[pool]
+        fill[pool] = lo + (n + 15) // 16 * 16
+        return (pool, lo, n, 1)
+
+    def f(n=32):
+        return new("F", n)
+
+    def vp(lo, n):
+        return ("ps3", lo, n, 1)
+
+    def op(eng, fn, rd, wr, cost, lat=0.0, sem=None, acc=False, after=()):
+        ops.append({"eng": eng, "fn": fn, "rd": rd, "wr": wr, "cost": cost, "lat": lat, "sem": sem, "acc": acc, "after": list(after)})
+        return len(ops) - 1
+
+    def S(x):
+        return R(x) if isinstance(x, tuple) else x
+
+    def aps(*xs):
+        return [x for x in xs if isinstance(x, tuple)]
+
+    def cp(o, i):
+        op("v", lambda: g.vector.tensor_copy(R(o), R(i)), [i], [o], CY * max(64, o[2] * (0.5 if two(o) and two(i) else 1)))
+        return o
+
+    def ts(o, i, s1, o0, s2=None, o1=None):
+        c = CY * max(64, o[2] * (0.5 if two(o) and two(i) else 1))
+        if o1 is None:
+            op("v", lambda: g.vector.tensor_scalar(R(o), R(i), S(s1), None, o0), aps(i, s1), [o], c)
+        else:
+            op("v", lambda: g.vector.tensor_scalar(R(o), R(i), S(s1), S(s2), o0, o1), aps(i, s1, s2), [o], c)
+        return o
+
+    def tt(o, a, b, alu):
+        k = 1 if a[0][:2] == "ps" or b[0][:2] == "ps" else 2
+        op("v", lambda: g.vector.tensor_tensor(R(o), R(a), R(b), alu), [a, b], [o], CY * max(64, o[2] * k))
+        return o
+
+    def mset(o, c):
+        op("v", lambda: g.vector.memset(R(o), c), [], [o], CY * max(64, o[2] * (0.5 if two(o) else 1)))
+        return o
+
+    def act(o, i, fn, bias=0.0, scale=1.0):
+        op("a", lambda: g.scalar.activation(R(o), R(i), fn, bias=S(bias), scale=S(scale)), aps(i, bias, scale), [o], CY * max(64, o[2]))
+        return o
+
+    def IND(win, off):
+        return R(win).indirect(R(off))
+
+    def agat(o, win, off, rd=None):
+        op("a", lambda: g.scalar.activation(R(o), IND(win, off), ACT.Copy), (rd or [win]) + [off], [o], 0.065 + 1.6 * 0.83e-3 * o[2])
+        return o
+
+    def vgat(o, win, off):
+        op("v", lambda: g.vector.tensor_copy(R(o), IND(win, off)), [win, off], [o], 0.05 + 1.6 * 0.83e-3 * o[2])
+        return o
+
+    def fused(o, win, off, b, alu):
+        op("v", lambda: g.vector.tensor_tensor(R(o), IND(win, off), R(b), alu), [win, off, b], [o], 0.05 + 1.8 * 0.83e-3 * o[2])
+        return o
+
+    def scat(off, src):
+        win = ("O", 0, V + H, 1)
+        n = H // SPLIT
+        for k in range(SPLIT):
+            o2, s2 = sub(off, k * n // 16, n // 16), sub(src, k * n, n)
+            op("v", lambda o2=o2, s2=s2: g.vector.tensor_copy(IND(win, o2), R(s2)), [o2, s2], [win], 0.05 + 3.8 * 0.83e-3 * n)
+
+    def mm(o, terms, start, stop):
+        if len(terms) > 1 and o[2] >= 256:
+            for k, x in enumerate(terms):
+                mm(o, [x], start and k == 0, stop and k == len(terms) - 1)
+            return o
+
+        def fn():
+            last = None
+            for k, (l, r) in enumerate(terms):
+                last = g.tensor.matmul(R(o), R(l), R(r), start and k == 0, stop and k == len(terms) - 1)
+            return last
+        c = sum(PC * max(64, r[2]) * (4 if r[0] == "F" else 1) for l, r in terms)
+        op("p", fn, [x for t in terms for x in t], [o], c, lat=0.05, acc=not start)
+        return o
+
+    def iota(o, pat, base, cm):
+        if o[0] == "IP":
+            op("g", lambda: g.iota(R(o), pat, base, cm), [], [o], 0.13 + 2 * CY * o[2])
+        else:
+            op("g", lambda: g.iota(R(o), pat, base, cm, allow_small_or_imprecise_dtypes=True), [], [o], 0.13 + 2 * CY * o[2])
+        return o
+
+    def asel(o, pat, cmp, fl, base, cm):
+        op("g", lambda: g.affine_select(R(o), R(o), pat, cmp, fl, base, cm), [o], [o], 0.17 + 2 * CY * o[2])
+        return o
+
+    def dma(q, out, in_, rd, wr, nbytes, after=()):
+        name = "d%d" % fill["d"]
+        fill["d"] += 1
+        e = g.sync if q == "s" else g.scalar
+        return op(q, lambda: e.dma_start(out, in_), rd, wr, 0.06, lat=1.8 + nbytes / 180e3, sem=(name, 16), after=after)
+
+    def send(dst, src, sem, nbytes):
+        k = op("g", lambda: g.remote_dma(R(dst), R(src), T.sem[sem], T.sem.sent, nxt_addr[1], nxt_addr[0], nxt_mask),
+               [src], [], 0.4, sem=("", 0))
+        op("x", None, [], [dst], 0.0, lat=2.2 + nbytes / 60e3, sem=(sem, neng), after=[k])
+
+    dma("a", T.RT[:], T.rt[:], [], [("RT", 0, 160, 1)], 80e3)
+    dma("a", T.G[:, 0:16], T.rec[:, 0:16], [], [("G", 0, 16, 1)], 20e3)
+    big = dma("s", T.G[:, 16:V], T.rec[:, 16:V], [], [("G", 16, V - 16, 1)], 1050e3)
+    dma("s", T.CHI[:], T.ch[:], [], [("CHI", 0, 1024, 1)], 520e3, after=[big])
+    pi = iota(new("IP", 1), [[0, 1]], 0, 1)
+    ri = ts(new("IP", 1), pi, 15, A.bitwise_and)
+    RF = cp(f(1), ri)
+    RF2 = ts(f(1), ri, 2.0, A.mult)
+    RF8 = ts(f(1), ri, 8.0, A.mult)
+    PP = ts(f(1), ri, 2.0, A.mult, 13.0 / 128, A.add)
+    PP2 = ts(f(1), ri, 2.0, A.mult, 13.0 / 128 + 0.375, A.add)
+    E8 = iota(f(8), [[0, 8]], 1, 0)
+    asel(E8, [[-16, 8]], A.is_ge, 0.0, 0, 1)
+    asel(E8, [[16, 8]], A.is_ge, 0.0, 15, -1)
+    EB = mset(new("WB", 144), 0.0)
+    ts(sub(EB, 16, 8, 16), E8, 3.0 / 64, A.mult)
+    EK = mset(new("WB", 144), 0.0)
+    ts(sub(EK, 16, 8, 16), E8, 65536.0, A.mult)
+    KU = mset(new("WB", 32), -8.5 * 65536)
+    KS = mset(new("WB", 32), -65536.0)
+    ID = iota(new("WB", 128), [[0, 128]], 1, 0)
+    asel(ID, [[-1, 128]], A.is_equal, 0.0, 0, 1)
+    IDN = ts(new("WB", 128), ID, -1.0, A.mult)
+    C32 = iota(new("WB", 32), [[32, 32]], 0, 0)
+    C64 = iota(new("WB", 32), [[64, 32]], 0, 0)
+    TH32 = ts(f(), C32, 0.4, A.add)
+    TH64 = ts(f(), C64, 0.05, A.add)
+    mset(("G", 0, 1, 1), 256.0)
+    for t in range(ST):
+        mset(("G", NB[t], 16, 1), 256.0)
+    IDH = ts(new("WB", 128), ID, 0.5, A.mult)
+    IDM2 = ts(new("WB", 128), ID, -2.0, A.mult)
+    KE = []
+    for o in range(4):
+        m1 = ts(f(1), ri, 4 * o + 0.5, A.subtract)
+        m2 = tt(f(1), m1, m1, A.mult)
+        m3 = ts(f(1), m2, 0.5, A.is_lt)
+        k = mset(new("WB", 144), 0.0)
+        ts(sub(k, 16, 8, 16), E8, m3, A.mult)
+        KE.append(k)
+    BD = iota(new("WB", 128), [[0, 128]], 1, 0)
+    asel(BD, [[-16, 8], [0, 16]], A.is_ge, 0.0, 0, 1)
+    asel(BD, [[16, 8], [0, 16]], A.is_ge, 0.0, 15, -1)
+    J = iota(f(256), [[16, 2], [-16, 8], [-1, 16]], 0, 1)
+    asel(J, [[0, 2], [-16, 8], [0, 16]], A.is_ge, 999.0, 0, 1)
+    asel(J, [[0, 2], [16, 8], [0, 16]], A.is_ge, 999.0, 15, -1)
+    ts(J, J, 7.5, A.subtract)
+    J8 = ts(f(6), iota(f(6), [[128, 6]], 0, 0), RF8, A.add)
+    NH = mset(new("WB", H), -0.5)
+    M75 = mset(new("WB", 2), -7.5)
+    AP0, AP1, YP1 = f(160), f(160), f(160)
+    act(sub(AP0, 0, 32), iota(f(), [[32, 32]], 16, 0), ACT.Identity, bias=RF2)
+    act(sub(AP0, 32, 128), iota(f(128), [[1024, 4], [32, 32]], 17, 0), ACT.Identity, bias=RF2)
+    act(AP1, iota(f(160), [[512, 5], [16, 32]], 16, 0), ACT.Identity, bias=RF)
+    act(sub(YP1, 0, 128), iota(f(128), [[1024, 4], [32, 32]], 16 + CW[1] + 1, 0), ACT.Identity, bias=RF2)
+    act(sub(YP1, 128, 32), iota(f(), [[16, 32]], 16 + CW[1] + 4096, 0), ACT.Identity, bias=RF)
+    APN = [AP0, AP1, AP1]
+    YPN = [ts(f(160), YP1, float(CW[0] - CW[1]), A.add), YP1, YP1]
+    DUM = act(f(128), iota(f(128), [[0, 4], [16, 32]], V, 0), ACT.Identity, bias=RF)
+    POS = act(f(128), iota(f(128), [[512, 4], [16, 32]], 0, 0), ACT.Identity, bias=RF)
+    lbase = [NB[t + 1] - 2048 for t in range(ST)]
+    LPOS = [ts(f(128), POS, float(lbase[t]), A.add) for t in range(ST - 1)]
+    CODE = ts(f(128), POS, 1.0, A.add, 4096.0, A.mult)
+    APA = [ts(f(128), sub(APN[t], 0, 128), float(NB[t]), A.add) for t in range(ST)]
+    hi, lo, chi = ("HI", 0, 1024, 1), ("LO", 0, 1024, 1), ("CHI", 0, 1024, 1)
+    for k in range(4):
+        h = cp(sub(hi, 256 * k, 256), sub(chi, 256 * k, 256))
+        tt(sub(lo, 256 * k, 256), mm(("ps%d" % (6 + k % 2), 0, 256, 1), [(IDN, h)], True, True), sub(chi, 256 * k, 256), A.add)
+    TBW, tbl = [], []
+    for k in range(4):
+        TBW.append(("TB%d" % k, 0, 1, 1))
+        tbl.append(dma("s", T.TB[k:128:4, :], T.HI[:] if k % 2 == 0 else T.LO[:], [hi if k % 2 == 0 else lo], [TBW[k]], 260e3))
+    dma("s", T.O[:, 0:V], T.rec[:], [], [("O", 0, V, 1)], 1050e3, after=tbl)
+    mset(("O", V, H, 1), 0.0)
+
+    def count(bank, cmpt, signed, p, w, c0=0):
+        n = p[2]
+        o = (bank, 0, n, 1)
+        mm(o, [(ID, sub(C64 if signed else C32, c0, n))], True, False)
+        mm(o, [(sub(EB, 16 - r, 128), sub(cmpt, r, n, 16)) for r in range(16)], False, True)
+        if signed:
+            ts(p, o, 0.5, A.mult, PP2, A.add)
+        else:
+            ts(p, o, PP, A.add)
+        tt(w, o, sub(TH64 if signed else TH32, c0, n), A.is_gt)
+        return p, w
+
+    def rotate(bank, win, off, PM):
+        rg = agat(f(80), win, off)
+        return mm((bank, 0, 64, 1), [(sub(PM, 0, 128), sub(rg, 0, 64)), (sub(PM, 128, 128), sub(rg, 2, 64))], True, True)
+
+    def regions(t):
+        p0 = NB[t] + 16 + CW[t]
+        P = [("G", p0 + 1024 * o, 1024, 1) for o in range(4)]
+        X = [sub(p, 0, H, 2) for p in P]
+        Y = [sub(p, 1, H, 2) for p in P] + [("G", p0 + 4096, H, 1)]
+        if t == 0:
+            AA = [("G", NB[t] + 16, H, 2)] + [("G", NB[t] + 17 + 1024 * o, H, 2) for o in range(4)]
+        else:
+            AA = [("G", NB[t] + 16 + H * o, H, 1) for o in range(5)]
+        return NB[t], P, X, Y, AA
+
+    def champion_level(t, o, st, RR):
+        nb, P, X, Y, AA = regions(t)
+        cm = new("WB", H)
+        win = ("G", nb, 16 + H * o, 1)
+        signed = not (o >= 2 and o in CF)
+        if not signed:
+            fused(cm, win, st["p16"], AA[o], A.is_gt)
+        else:
+            c = AA[0] if o == 1 else agat(new("WB", H), win, st["p16"])
+            d = mm(("ps5", 0, H, 1), [(IDN, AA[o]), (ID, c)], True, True)
+            act(cm, d, ACT.Sign, bias=-0.5)
+        ac = act(f(), sub(RR, 32 * o, 32), ACT.Identity, bias=4096.0 * o)
+        st["ac"].append(ac)
+        k = ("ps1", 0, 32, 1)
+        mm(k, [(ID, KS if signed else KU)], True, False)
+        mm(k, [(sub(EK, 16 - r, 128), sub(cm, r, 32, 16)) for r in range(16)], False, True)
+        st["p"] = tt(f(), tt(f(), k, sub(APN[t], 32 * o, 32), A.min), st["p"], A.max)
+        st["p16"] = cp(new("U", 32), st["p"])
+        st["cur"] = tt(new("IP", 32) if o == 4 else f(), tt(f(), k, ac, A.min), st["cur"], A.max)
+        st["win"] = ("G", nb, 16 + CW[t], 1)
+
+    rt = ("RT", 0, 160, 1)
+    r16 = cp(new("U", 160), rt)
+    RR = cp(f(160), rt)
+    nb, P, X, Y, AA = regions(0)
+    for o in range(5):
+        for k in range(2):
+            (vgat if o in (0, 2) else agat)(sub(AA[o], 256 * k, 256), ("G", 0, V, 1), sub(r16, 32 * o + 16 * k, 16))
+    st = {"cur": sub(RR, 0, 32), "ac": [sub(RR, 0, 32)]}
+    C = [None] + [("G", nb + 16 + 1024 * o, 1024, 1) for o in range(4)]
+    p = None
+    for o in range(1, 5):
+        p2, w, cm = new("U", 32), f(), new("WB", H)
+        for k in range(2):
+            ck, ak = sub(cm, 256 * k, 256), sub(AA[o], 256 * k, 256)
+            if o == 1:
+                d = mm((("ps5", "ps2")[k], 0, 256, 1), [(IDN, ak), (ID, sub(AA[0], 256 * k, 256))], True, True)
+                act(ck, d, ACT.Sign, bias=-0.5)
+            else:
+                wk, pk = sub(C[o - 1], 0, 512 * k + 512), sub(p, 16 * k, 16)
+                fused(ck, wk, pk, ak, A.is_gt)
+                agat(sub(C[o], 512 * k, 256, 2), wk, pk)
+            count(("ps1", "ps0")[k], ck, o == 1, sub(p2, 16 * k, 16), sub(w, 16 * k, 16), 16 * k)
+        p = p2
+        ac = act(f(), sub(RR, 32 * o, 32), ACT.Identity, bias=4096.0 * o)
+        st["ac"].append(ac)
+        st["cur"] = tt(new("IP", 32) if o == 4 else f(), tt(f(), w, ac, A.mult), st["cur"], A.max)
+    st["p16"], st["win"] = p, C[4]
+
+    keys, losers, rotd, code1 = [], [], None, None
+    for t in range(ST):
+        nb, P, X, Y, AA = regions(t)
+        last = t == ST - 1
+        Z, W = ("Z%d" % t, 0, H, 1), ("W%d" % t, 0, H, 1)
+        ZT, WT = ("ZT%d" % t, 0, 16, 1), ("WT%d" % t, 0, 16, 1)
+        cur = st["cur"]
+        agat(ZT, sub(st["win"], 0, 512) if t == 0 else st["win"], sub(st["p16"], 0, 1))
+        send(WT, ZT, "at%d" % t, 30e3)
+        agat(Z, st["win"], st["p16"])
+        send(W, Z, "aw%d" % t, 131e3)
+        m = ts(new("IP", 32), cur, 4095, A.bitwise_and)
+        m16 = cp(new("U", 32), m)
+        G1 = agat(new("WB", H), ("TB", 0, V, 1), m16, TBW)
+        MB = ("ps4", 0, H, 1)
+        mm(MB, [(IDH, NH), (IDH, Z)], True, False)
+        pq = f(128)
+        for o in range(4):
+            ts(sub(pq, 32 * o, 32), cur, 4096.0 * (o + 1), A.is_ge)
+        npq = act(f(128), pq, ACT.Identity, bias=BIG, scale=-BIG)
+        if t == 0:
+            gm, ei, ep = pq, None, npq
+        else:
+            e = vp(0, 128)
+            for o in range(4):
+                tt(sub(e, 32 * o, 32), sub(keys[t - 1], 32 * o, 32), m, A.is_equal)
+            hm = tt(f(128), pq, e, A.subtract)
+            ei = tt(f(128), e, losers[t - 1], A.mult)
+            ep = tt(f(128), tt(vp(128, 128), e, LPOS[t - 1], A.mult), npq, A.add)
+            gm = hm
+            if t == 2:
+                e1 = vp(256, 128)
+                for o in range(4):
+                    tt(sub(e1, 32 * o, 32), sub(keys[0], 32 * o, 32), m, A.is_equal)
+                c1 = tt(f(128), e1, code1, A.mult)
+                e2 = vp(384, 96)
+                for o in range(3):
+                    tt(sub(e2, 32 * o, 32), sub(rotd, 64 * o, 32, 2), m, A.is_equal)
+                tt(e2, e2, sub(rotd, 1, 96, 2), A.mult)
+                tt(sub(e1, 0, 96), e2, sub(c1, 0, 96), A.max)
+                cp(sub(e1, 96, 32), sub(c1, 96, 32))
+                ci = tt(new("IP", 128), e1, hm, A.mult)
+                i1 = ts(new("IP", 128), ci, 4095, A.bitwise_and)
+                p1 = ts(new("IP", 128), ci, 12, A.arith_shift_right)
+                a1 = ts(vp(0, 128), p1, 0.0, A.is_gt)
+                gm = tt(f(128), hm, a1, A.subtract)
+                u1 = ts(vp(128, 128), p1, 0.0, A.is_gt, float(lbase[0] - 1), A.mult)
+                tt(u1, u1, p1, A.add)
+                ep = tt(f(128), u1, ep, A.add)
+                ei = tt(f(128), i1, ei, A.add)
+        sb = ("ps5", 0, 1, 1)
+        mm(sb, [(ID, sub(M75, 0, 1)), (BD, sub(WT, 0, 1))], True, True)
+        f16 = ts(f(1), sb, MAGIC16, A.add, MAGIC16, A.subtract)
+        s0m = tt(f(1), f16, sb, A.subtract)
+        j1 = ts(new("IP", 6), J8, f16, A.add)
+        j2 = ts(new("IP", 6), j1, 3, A.arith_shift_right, 63, A.bitwise_and)
+        off = sub(cp(new("U", 6), j2), 0, 5)
+        PM = act(f(256), act(f(256), J, ACT.Abs, bias=s0m), ACT.Relu, bias=1.0, scale=-1.0)
+        ne = vp(256, 160)
+        for o in range(5):
+            tt(sub(ne, 32 * o, 32), st["ac"][o], cur, A.not_equal)
+        Ra = tt(f(160), ne, RR, A.mult)
+        Bi = f(128)
+        rws = []
+        for o in range(4):
+            kd = mm(("ps6", 32 * o, 32, 1), [(sub(KE[o], 16 - r, 128), sub(G1, r, 32, 16)) for r in range(16)], True, True)
+            rw = f(64)
+            if ei is None:
+                chm = tt(sub(rw, 0, 32, 2), kd, sub(gm, 32 * o, 32), A.mult)
+            else:
+                chm = tt(f(), kd, sub(gm, 32 * o, 32), A.mult)
+                tt(sub(rw, 0, 32, 2), chm, sub(ei, 32 * o, 32), A.add)
+            tt(sub(rw, 1, 32, 2), chm, sub(ep, 32 * o, 32), A.add)
+            rws.append(rw)
+        for o in range(4):
+            rb = rotate(("ps7", "ps1")[o % 2], rws[o], off, PM)
+            xp = tt(f(), sub(rb, 1, 32, 2), sub(APA[t], 32 * o, 32), A.min)
+            x16 = cp(new("U", 32), xp)
+            act(sub(Bi, 32 * o, 32), sub(rb, 0, 32, 2), ACT.Copy)
+            agat(X[o], ("G", 0, nb + 16 + CW[t], 1), x16)
+            if o == 0:
+                D0 = ("ps5", 0, H, 1)
+                mm(D0, [(ID, Z), (ID, W), (IDM2, X[0])], True, True)
+                mm(MB, [(IDH, W)], False, True)
+                cm0 = act(new("WB", H), D0, ACT.Sign, bias=-0.5, scale=-1.0)
+                if MPA:
+                    act(Y[0], act(MB, MB, ACT.Identity, bias=MAGIC), ACT.Identity, bias=-MAGIC)
+                else:
+                    ts(Y[0], MB, MAGIC, A.add, MAGIC, A.subtract)
+        if t == 1:
+            code1 = tt(f(128), losers[0], CODE, A.add)
+            rotd = f(192)
+            for o in range(3):
+                rw = f(64)
+                act(sub(rw, 0, 32, 2), sub(keys[0], 32 * o, 32), ACT.Copy)
+                act(sub(rw, 1, 32, 2), sub(code1, 32 * o, 32), ACT.Copy)
+                act(sub(rotd, 64 * o, 64), rotate("ps7", rw, off, PM), ACT.Copy)
+        LK = f(192)
+        mset(sub(LK, 0, 32), 1.0)
+        xa, usey, nd, kp = vp(128, 128), vp(256, 160), vp(0, 128), vp(416, 96)
+        xi, xd, a16 = f(128), f(128), new("U", 160)
+        for lo, n in ((0, 64), (64, 64)):
+            n5 = n + 32 * (lo > 0)
+            xa_, xi_, nd_, lk_, ra_ = sub(xa, lo, n), sub(xi, lo, n), sub(nd, lo, n), sub(LK, lo + 32, n), sub(Ra, lo, n)
+            ts(xa_, sub(Bi, lo, n), 0.0, A.is_le)
+            tt(xa_, xa_, ra_, A.mult)
+            tt(xi_, xa_, sub(Bi, lo, n), A.add)
+            for o in range(lo // 32, (lo + n5) // 32):
+                tt(sub(LK, 32 * o + 32, 32), sub(xi, 32 * o, 32) if o < 4 else sub(Ra, 128, 32), sub(LK, 32 * o, 32), A.min)
+            tt(xa_, xa_, lk_, A.mult)
+            tt(ra_, ra_, xa_, A.subtract)
+            us_ = tt(sub(usey, lo, n5), sub(LK, lo, n5), sub(LK, lo + 32, n5), A.subtract)
+            if not last:
+                kp_ = ts(sub(kp, 0, n5), sub(Ra, lo, n5), 0.0, A.is_gt)
+                q1 = tt(f(n5), kp_, sub(APN[t], lo, n5), A.mult)
+                tt(kp_, us_, sub(YPN[t], lo, n5), A.mult)
+                cp(sub(a16, lo, n5), tt(kp_, kp_, q1, A.add))
+            ts(nd_, lk_, -8192.0, A.mult)
+            tt(nd_, nd_, sub(DUM, lo, n), A.add)
+            tt(sub(xd, lo, n), nd_, xi_, A.max)
+        RN = ("YR", 0, 160, 1) if last else f(160)
+        ky, ls = f(128), f(128)
+        st2 = {"cur": sub(RN, 0, 32), "ac": [sub(RN, 0, 32)], "p": sub(AP1, 0, 32)}
+
+        def root(o, y):
+            tt(sub(RN, 32 * o, 32), tt(f(), sub(usey, 32 * o, 32), y, A.mult), sub(Ra, 32 * o, 32), A.add)
+            if not last:
+                agat(regions(t + 1)[4][o], ("G", nb, (Y[o][1] + Y[o][2] * Y[o][3] - nb) // 2 * 2, 1), sub(a16, 32 * o, 32))
+                if o >= 1:
+                    champion_level(t + 1, o, st2, RN)
+
+        scat(m16, Y[0])
+        y = m
+        p = None
+        pend = []
+        for o in range(4):
+            if o == 0:
+                cm = cm0
+            elif o in MF:
+                cm = fused(new("WB", H), P[o - 1], p, X[o], A.is_lt)
+                agat(Y[o], P[o - 1], p)
+            else:
+                agat(Y[o], P[o - 1], p)
+                dd = mm(("ps6", 0, H, 1), [(ID, X[o]), (IDN, Y[o])], True, True)
+                cm = act(new("WB", H), dd, ACT.Sign, bias=-0.5)
+            p, w = count("ps0", cm, o not in MF, new("U", 32), f())
+            if o == 3 and not last:
+                agat(Y[4], P[3], p)
+            root(o, y)
+            yd = tt(f(), y, sub(nd, 32 * o, 32), A.max)
+            d = tt(f(), yd, sub(xd, 32 * o, 32), A.subtract)
+            x = tt(f(), w, d, A.mult)
+            y = tt(sub(ky, 32 * o, 32), sub(xd, 32 * o, 32), x, A.add)
+            pend.append(cp(new("U", 32), tt(sub(ls, 32 * o, 32), yd, x, A.subtract)))
+        root(4, y)
+        for o in range(4):
+            bank = ("ps2" if o % 2 else "ps4", 0, H, 1)
+            nw = ("G", lbase[t] + H * o, H, 1)
+            if last and o == 3:
+                pn = new("WB", 2 * H)
+                mm(bank, [(ID, Y[o]), (IDN, X[o])], True, True)
+                sg = act(new("WB", H), bank, ACT.Sign)
+                act(sub(pn, 0, H, 2), mm(bank, [(ID, Y[o]), (IDN, sg)], True, True), ACT.Copy)
+                act(sub(pn, 1, H, 2), mm(("ps7", 0, H, 1), [(ID, X[o]), (ID, sg)], True, True), ACT.Copy)
+                for k in range(2):
+                    agat(sub(nw, 256 * k, 256), pn, sub(p, 16 * k, 16))
+            else:
+                mm(bank, [(ID, X[o]), (ID, Y[o]), (IDM2, Y[o + 1])], True, True)
+                sg = act(new("WB", H), bank, ACT.Sign, scale=-1.0)
+                mm(bank, [(ID, X[o]), (ID, Y[o]), (IDN, Y[o + 1]), (ID, sg)], True, True)
+                act(nw, bank, ACT.Copy)
+            scat(pend[o], nw)
+        keys.append(ky)
+        losers.append(ls)
+        st, RR = st2, RN
+    dma("a", T.yrt[:], T.YR[:], [("YR", 0, 160, 1)], [], 80e3)
+    dma("s", T.yrec[:], T.O[:, 0:V], [("O", 0, V, 1)], [], 1050e3)
+    return ops
+
+
+def place(ops, deps, succ, tail):
+    n = len(ops)
+    left = [len(deps[k]) for k in range(n)]
+    start, done, rdy = [0.0] * n, [0.0] * n, [0.0] * n
+    free = {e: 0.0 for e in "vapgsx"}
+    avail = {e: [] for e in "vapgsx"}
+    for k in range(n):
+        if left[k] == 0:
+            avail[ops[k]["eng"]].append(k)
+    order = []
+    while len(order) < n:
+        best = None
+        for e in "xgspav":
+            if not avail[e]:
+                continue
+            now = max(free[e], min(rdy[k] for k in avail[e]))
+            c = max((k for k in avail[e] if rdy[k] <= now), key=lambda k: tail[k])
+            for k in avail[e]:
+                if now < rdy[k] < now + LOOK * ops[c]["cost"] and tail[k] > tail[c] + 1.0:
+                    c, now = k, rdy[k]
+            if best is None or now < best[0]:
+                best = (now, c)
+        now, c = best
+        e = ops[c]["eng"]
+        avail[e].remove(c)
+        start[c] = now
+        free[e] = now + ops[c]["cost"]
+        done[c] = free[e] + ops[c]["lat"]
+        order.append(c)
+        for s in succ[c]:
+            if deps[s][c]:
+                rdy[s] = max(rdy[s], done[c] + WAKE)
+            elif ops[s]["eng"] == "s":
+                rdy[s] = max(rdy[s], done[c] - 1.8)
+            else:
+                rdy[s] = max(rdy[s], free[e])
+            left[s] -= 1
+            if left[s] == 0:
+                avail[ops[s]["eng"]].append(s)
+    return order, start, done
+
+
+def schedule(ops):
+    n = len(ops)
+    deps = [dict() for _ in range(n)]
+    seen = {}
+    for k, o in enumerate(ops):
+        for j in o["after"]:
+            deps[k][j] = o["eng"] != ops[j]["eng"] and o["eng"] != "x"
+        for a, wr in [(a, False) for a in o["rd"]] + [(a, True) for a in o["wr"]]:
+            for j, b, bw in seen.get(a[0], []):
+                if j == k:
+                    continue
+                other = ops[j]["eng"] != o["eng"]
+                if a[0][:2] == "ps" and other:
+                    deps[k][j] = True
+                elif (wr or bw) and meet(a, b):
+                    if o["acc"] and not other and a[0][:2] == "ps":
+                        deps[k].setdefault(j, False)
+                    else:
+                        deps[k][j] = True
+        for a in o["rd"]:
+            seen.setdefault(a[0], []).append((k, a, False))
+        for a in o["wr"]:
+            seen.setdefault(a[0], []).append((k, a, True))
+    succ = [[] for _ in range(n)]
+    for k in range(n):
+        for j in deps[k]:
+            succ[j].append(k)
+    base = [0.0] * n
+    for k in range(n - 1, -1, -1):
+        base[k] = ops[k]["cost"] + ops[k]["lat"] + max([base[s] + WAKE for s in succ[k]] + [0.0])
+    best = place(ops, deps, succ, base)
+    seed = 12345
+    for it in range(TRIES):
+        pr = list(base)
+        for r in range(3):
+            seed = (seed * 1103515245 + 12345) % 2147483648
+            lo = (seed >> 8) % n
+            seed = (seed * 1103515245 + 12345) % 2147483648
+            w = 1 + (seed >> 8) % 12
+            seed = (seed * 1103515245 + 12345) % 2147483648
+            dv = ((seed >> 8) % 2001 - 1000) / 1000.0
+            for k in range(lo, min(n, lo + w)):
+                pr[k] += 6.0 * dv * dv * dv
+        got = place(ops, deps, succ, pr)
+        if max(got[2]) <= max(best[2]):
+            best, base = got, pr
+    return best[0], deps, best[1], best[2]
+
+
+def rank_program(g, core, T, topo):
+    rank = T.rank_of(core)
+    if rank is None:
+        return
+    nxt = T.cores[(rank + 1) % len(T.cores)]
+    neng = len(topo.engines(core, nxt))
+    ops = build(g, T, topo.addr(nxt), topo.mask(core, nxt), neng)
+    if "plan" not in PLAN:
+        PLAN["plan"] = schedule(ops)
+    order, deps, start, done = PLAN["plan"]
+    queue = {"v": g.vector, "a": g.scalar, "p": g.tensor, "g": g, "s": g.sync}
+    total, mark, clock = {}, {}, {}
+    known = {e: {} for e in queue}
+    sends = 0
+    for k in order:
+        o = ops[k]
+        e = o["eng"]
+        if e == "x":
+            mark[k] = o["sem"]
+            clock[k] = {o["sem"][0]: o["sem"][1]}
+            total[o["sem"][0]] = o["sem"][1]
+            continue
+        need = {}
+        for j in deps[k]:
+            if deps[k][j]:
+                s, c = mark[j]
+                if c > need.get(s, (0, 0))[0]:
+                    need[s] = (c, j)
+        for s, (c, j) in sorted(need.items(), key=lambda x: -done[x[1][1]]):
+            if known[e].get(s, 0) < c:
+                queue[e].wait_ge(T.sem[s], c)
+                for s2, c2 in clock[j].items():
+                    known[e][s2] = max(known[e].get(s2, 0), c2)
+        ins = o["fn"]()
+        if o["sem"] is None:
+            s = "c" + e
+            total[s] = total.get(s, 0) + 1
+            ins.then_inc(T.sem[s], 1)
+            mark[k] = (s, total[s])
+        elif o["sem"][0] == "":
+            sends += neng
+            continue
+        else:
+            s = o["sem"][0]
+            ins.then_inc(T.sem[s], 16)
+            total[s] = 16
+            mark[k] = (s, 16)
+        clock[k] = dict(known[e])
+        clock[k][s] = total[s]
+    total["sent"] = sends
+    for s in total:
+        g.wait_ge(T.sem[s], total[s])

@@ -8,13 +8,11 @@ for _t in range(ST):
 BIG = 60000.0
 MAGIC = 12582912.0
 MAGIC16 = 201326592.0
-EXACT = True
-MF = ()
-CF = (2, 3, 4)
-MPA = True
+MF = ((1, 2, 3), (1,), ())
 SPLIT = 2
-LOOK, WAKE, TRIES = 0.5, 0.12, 1500
-NDMA = 12
+LOOK, WAKE, TRIES = 0.5, 0.14, 6000
+VIEWS = (((1.0, 1.0, 1.0), 0.12, 0.0), ((0.88, 0.88, 0.74), 0.17, 0.5), ((1.16, 1.2, 1.45), 0.15, 0.4), ((1.16, 1.0, 0.8), 0.15, 0.4))
+NDMA = 10
 
 SCRATCH = {
     "G": ("sbuf", [128, NB[ST]], "bfloat16"),
@@ -57,9 +55,7 @@ def meet(a, b):
     blo, bhi = b[1], b[1] + (b[2] - 1) * b[3]
     if ahi < blo or bhi < alo:
         return False
-    if EXACT and a[3] == b[3] and a[3] > 1 and (alo - blo) % a[3] != 0:
-        return False
-    return True
+    return not (a[3] == b[3] and a[3] > 1 and (alo - blo) % a[3] != 0)
 
 
 def two(a):
@@ -87,7 +83,8 @@ def build(g, T, nxt_addr, nxt_mask, neng):
         return ("ps3", lo, n, 1)
 
     def op(eng, fn, rd, wr, cost, lat=0.0, sem=None, acc=False, after=()):
-        ops.append({"eng": eng, "fn": fn, "rd": rd, "wr": wr, "cost": cost, "lat": lat, "sem": sem, "acc": acc, "after": list(after)})
+        ops.append({"eng": eng, "fn": fn, "rd": rd, "wr": wr, "cost": cost, "lat": lat, "sem": sem, "acc": acc, "after": list(after),
+                    "kind": 0 if not any(a[0] == "U" for a in rd) else 2 if wr[0][0] == "O" else 1})
         return len(ops) - 1
 
     def S(x):
@@ -183,7 +180,8 @@ def build(g, T, nxt_addr, nxt_mask, neng):
     dma("a", T.RT[:], T.rt[:], [], [("RT", 0, 160, 1)], 80e3)
     dma("a", T.G[:, 0:16], T.rec[:, 0:16], [], [("G", 0, 16, 1)], 20e3)
     big = dma("s", T.G[:, 16:V], T.rec[:, 16:V], [], [("G", 16, V - 16, 1)], 1050e3)
-    dma("s", T.CHI[:], T.ch[:], [], [("CHI", 0, 1024, 1)], 520e3, after=[big])
+    chl = dma("s", T.CHI[:], T.ch[:], [], [("CHI", 0, 1024, 1)], 520e3, after=[big])
+    dma("s", T.O[:, 0:V], T.rec[:], [], [("O", 0, V, 1)], 1050e3, after=[chl])
     pi = iota(new("IP", 1), [[0, 1]], 0, 1)
     ri = ts(new("IP", 1), pi, 15, A.bitwise_and)
     RF = cp(f(1), ri)
@@ -244,15 +242,17 @@ def build(g, T, nxt_addr, nxt_mask, neng):
     LPOS = [ts(f(128), POS, float(lbase[t]), A.add) for t in range(ST - 1)]
     CODE = ts(f(128), POS, 1.0, A.add, 4096.0, A.mult)
     APA = [ts(f(128), sub(APN[t], 0, 128), float(NB[t]), A.add) for t in range(ST)]
+    LKS = [f(192) for t in range(ST)]
+    for t in range(ST):
+        mset(sub(LKS[t], 0, 32), 1.0)
     hi, lo, chi = ("HI", 0, 1024, 1), ("LO", 0, 1024, 1), ("CHI", 0, 1024, 1)
     for k in range(4):
         h = cp(sub(hi, 256 * k, 256), sub(chi, 256 * k, 256))
         tt(sub(lo, 256 * k, 256), mm(("ps%d" % (6 + k % 2), 0, 256, 1), [(IDN, h)], True, True), sub(chi, 256 * k, 256), A.add)
-    TBW, tbl = [], []
-    for k in range(4):
-        TBW.append(("TB%d" % k, 0, 1, 1))
-        tbl.append(dma("s", T.TB[k:128:4, :], T.HI[:] if k % 2 == 0 else T.LO[:], [hi if k % 2 == 0 else lo], [TBW[k]], 260e3))
-    dma("s", T.O[:, 0:V], T.rec[:], [], [("O", 0, V, 1)], 1050e3, after=tbl)
+    TBW = [("TB0", 0, 1, 1), ("TB1", 0, 1, 1)]
+    op("v", lambda: g.vector.memset(T.TB[:], 0.0), [], TBW, CY * V / 2)
+    dma("s", T.TB[0:128:4, :], T.HI[:], [hi], [TBW[0]], 260e3)
+    dma("s", T.TB[1:128:4, :], T.LO[:], [lo], [TBW[1]], 260e3)
     mset(("O", V, H, 1), 0.0)
 
     def count(bank, cmpt, signed, p, w, c0=0):
@@ -285,18 +285,14 @@ def build(g, T, nxt_addr, nxt_mask, neng):
     def champion_level(t, o, st, RR):
         nb, P, X, Y, AA = regions(t)
         cm = new("WB", H)
-        win = ("G", nb, 16 + H * o, 1)
-        signed = not (o >= 2 and o in CF)
-        if not signed:
-            fused(cm, win, st["p16"], AA[o], A.is_gt)
+        if o >= 2:
+            fused(cm, ("G", nb, 16 + H * o, 1), st["p16"], AA[o], A.is_gt)
         else:
-            c = AA[0] if o == 1 else agat(new("WB", H), win, st["p16"])
-            d = mm(("ps5", 0, H, 1), [(IDN, AA[o]), (ID, c)], True, True)
-            act(cm, d, ACT.Sign, bias=-0.5)
+            act(cm, mm(("ps5", 0, H, 1), [(IDN, AA[1]), (ID, AA[0])], True, True), ACT.Sign, bias=-0.5)
         ac = act(f(), sub(RR, 32 * o, 32), ACT.Identity, bias=4096.0 * o)
         st["ac"].append(ac)
         k = ("ps1", 0, 32, 1)
-        mm(k, [(ID, KS if signed else KU)], True, False)
+        mm(k, [(ID, KS if o == 1 else KU)], True, False)
         mm(k, [(sub(EK, 16 - r, 128), sub(cm, r, 32, 16)) for r in range(16)], False, True)
         st["p"] = tt(f(), tt(f(), k, sub(APN[t], 32 * o, 32), A.min), st["p"], A.max)
         st["p16"] = cp(new("U", 32), st["p"])
@@ -365,13 +361,11 @@ def build(g, T, nxt_addr, nxt_mask, neng):
                 e1 = vp(256, 128)
                 for o in range(4):
                     tt(sub(e1, 32 * o, 32), sub(keys[0], 32 * o, 32), m, A.is_equal)
-                c1 = tt(f(128), e1, code1, A.mult)
+                tt(e1, e1, code1, A.mult)
                 e2 = vp(384, 96)
                 for o in range(3):
                     tt(sub(e2, 32 * o, 32), sub(rotd, 64 * o, 32, 2), m, A.is_equal)
-                tt(e2, e2, sub(rotd, 1, 96, 2), A.mult)
-                tt(sub(e1, 0, 96), e2, sub(c1, 0, 96), A.max)
-                cp(sub(e1, 96, 32), sub(c1, 96, 32))
+                tt(sub(e1, 0, 96), sub(e1, 0, 96), tt(f(96), e2, sub(rotd, 1, 96, 2), A.mult), A.max)
                 ci = tt(new("IP", 128), e1, hm, A.mult)
                 i1 = ts(new("IP", 128), ci, 4095, A.bitwise_and)
                 p1 = ts(new("IP", 128), ci, 12, A.arith_shift_right)
@@ -410,16 +404,16 @@ def build(g, T, nxt_addr, nxt_mask, neng):
             xp = tt(f(), sub(rb, 1, 32, 2), sub(APA[t], 32 * o, 32), A.min)
             x16 = cp(new("U", 32), xp)
             act(sub(Bi, 32 * o, 32), sub(rb, 0, 32, 2), ACT.Copy)
-            agat(X[o], ("G", 0, nb + 16 + CW[t], 1), x16)
+            (vgat if (t, o) == (0, 1) else agat)(X[o], ("G", 0, nb + 16 + CW[t], 1), x16)
             if o == 0:
                 D0 = ("ps5", 0, H, 1)
                 mm(D0, [(ID, Z), (ID, W), (IDM2, X[0])], True, True)
                 mm(MB, [(IDH, W)], False, True)
                 cm0 = act(new("WB", H), D0, ACT.Sign, bias=-0.5, scale=-1.0)
-                if MPA:
-                    act(Y[0], act(MB, MB, ACT.Identity, bias=MAGIC), ACT.Identity, bias=-MAGIC)
-                else:
+                if t == 0:
                     ts(Y[0], MB, MAGIC, A.add, MAGIC, A.subtract)
+                else:
+                    act(Y[0], act(MB, MB, ACT.Identity, bias=MAGIC), ACT.Identity, bias=-MAGIC)
         if t == 1:
             code1 = tt(f(128), losers[0], CODE, A.add)
             rotd = f(192)
@@ -428,8 +422,7 @@ def build(g, T, nxt_addr, nxt_mask, neng):
                 act(sub(rw, 0, 32, 2), sub(keys[0], 32 * o, 32), ACT.Copy)
                 act(sub(rw, 1, 32, 2), sub(code1, 32 * o, 32), ACT.Copy)
                 act(sub(rotd, 64 * o, 64), rotate("ps7", rw, off, PM), ACT.Copy)
-        LK = f(192)
-        mset(sub(LK, 0, 32), 1.0)
+        LK = LKS[t]
         xa, usey, nd, kp = vp(128, 128), vp(256, 160), vp(0, 128), vp(416, 96)
         xi, xd, a16 = f(128), f(128), new("U", 160)
         for lo, n in ((0, 64), (64, 64)):
@@ -469,14 +462,14 @@ def build(g, T, nxt_addr, nxt_mask, neng):
         for o in range(4):
             if o == 0:
                 cm = cm0
-            elif o in MF:
+            elif o in MF[t]:
                 cm = fused(new("WB", H), P[o - 1], p, X[o], A.is_lt)
                 agat(Y[o], P[o - 1], p)
             else:
                 agat(Y[o], P[o - 1], p)
                 dd = mm(("ps6", 0, H, 1), [(ID, X[o]), (IDN, Y[o])], True, True)
                 cm = act(new("WB", H), dd, ACT.Sign, bias=-0.5)
-            p, w = count("ps0", cm, o not in MF, new("U", 32), f())
+            p, w = count("ps0", cm, o not in MF[t], new("U", 32), f())
             if o == 3 and not last:
                 agat(Y[4], P[3], p)
             root(o, y)
@@ -553,6 +546,25 @@ def place(ops, deps, succ, tail):
     return order, start, done
 
 
+def replay(ops, dl, order, k, wake, far):
+    free = {e: 0.0 for e in "vapgsx"}
+    n = len(ops)
+    done, fr = [0.0] * n, [0.0] * n
+    for c in order:
+        o = ops[c]
+        e = o["eng"]
+        t = free[e]
+        for j, w in dl[c]:
+            x = done[j] + wake if w else (done[j] - 1.8 if e == "s" else fr[j])
+            if x > t:
+                t = x
+        fr[c] = t + k[o["kind"]] * o["cost"]
+        done[c] = fr[c] + o["lat"] + (far if e == "x" else 0.0)
+        if e != "x":
+            free[e] = fr[c]
+    return max(done)
+
+
 def schedule(ops):
     n = len(ops)
     deps = [dict() for _ in range(n)]
@@ -583,7 +595,11 @@ def schedule(ops):
     base = [0.0] * n
     for k in range(n - 1, -1, -1):
         base[k] = ops[k]["cost"] + ops[k]["lat"] + max([base[s] + WAKE for s in succ[k]] + [0.0])
+    dl = []
+    for k in range(n):
+        dl.append([(j, w) for j, w in deps[k].items() if not (w and any(deps[i].get(j) for i in deps[k] if i > j))])
     best = place(ops, deps, succ, base)
+    score = sum(replay(ops, dl, best[0], k, w, x) for k, w, x in VIEWS)
     seed = 12345
     for it in range(TRIES):
         pr = list(base)
@@ -597,8 +613,9 @@ def schedule(ops):
             for k in range(lo, min(n, lo + w)):
                 pr[k] += 6.0 * dv * dv * dv
         got = place(ops, deps, succ, pr)
-        if max(got[2]) <= max(best[2]):
-            best, base = got, pr
+        sc = sum(replay(ops, dl, got[0], k, w, x) for k, w, x in VIEWS)
+        if sc <= score:
+            best, base, score = got, pr, sc
     return best[0], deps, best[1], best[2]
 
 

@@ -1,32 +1,37 @@
 from concourse.mybir import AluOpType, ActivationFunctionType
 
 V, H, ST = 4096, 512, 3
-CW = [4096, 2560, 2560]
-NB = [V]
+CW = [4096, 4096, 4096]
+NB = [V + H]
 for _t in range(ST):
-    NB.append(NB[-1] + 16 + CW[_t] + 4608 + 2048)
-BIG = 60000.0
+    NB.append(NB[-1] + 16 + CW[_t] + 4096)
 MAGIC = 12582912.0
 MAGIC16 = 201326592.0
-MF = ((1, 2, 3), (1,), ())
+HOW = ("sfss", "sfss", "sfss")
+XV = ("avav", "avav", "avav")
+PMV = (1, 1, 1)
+STAGES = ((0, 64), (64, 64))
+PARTS = (2, 1, 1)
+CH = ("sfff", "ssff", "ssff")
+LG = ("cccg", "cccg", "cccg")
+LASTPN = 1
 SPLIT = 2
-LOOK, WAKE, TRIES = 0.5, 0.14, 6000
-VIEWS = (((1.0, 1.0, 1.0), 0.12, 0.0), ((0.88, 0.88, 0.74), 0.17, 0.5), ((1.16, 1.2, 1.45), 0.15, 0.4), ((1.16, 1.0, 0.8), 0.15, 0.4))
-NDMA = 10
+WAKE, TRIES, SHAKE, SPAN = 0.14, 5000, 2.0, 6.0
+VIEWS = (((1.0, 1.0, 1.0, 1.0), 0.14, 0.0), ((0.88, 0.88, 0.74, 1.1), 0.2, 0.5), ((1.16, 1.2, 1.45, 1.16), 0.15, 0.4), ((0.9, 0.9, 0.8, 0.9), 0.3, 0.4))
+NDMA = 8
 
 SCRATCH = {
     "G": ("sbuf", [128, NB[ST]], "bfloat16"),
-    "O": ("sbuf", [128, V + H], "bfloat16"),
     "TB": ("sbuf", [128, V], "bfloat16"),
     "CHI": ("sbuf", [128, 1024], "int32"),
     "HI": ("sbuf", [128, 1024], "bfloat16"),
     "LO": ("sbuf", [128, 1024], "bfloat16"),
     "RT": ("sbuf", [128, 160], "int32"),
     "YR": ("sbuf", [128, 160], "float32"),
-    "WB": ("sbuf", [128, 24576], "bfloat16"),
-    "F": ("sbuf", [128, 18432], "float32"),
-    "IP": ("sbuf", [128, 1024], "int32"),
-    "U": ("sbuf", [128, 2560], "uint16"),
+    "WB": ("sbuf", [128, 36864], "bfloat16"),
+    "F": ("sbuf", [128, 14336], "float32"),
+    "IP": ("sbuf", [128, 2048], "int32"),
+    "U": ("sbuf", [128, 3072], "uint16"),
 }
 for _t in range(ST):
     SCRATCH["Z%d" % _t] = ("sbuf", [128, H], "bfloat16")
@@ -42,7 +47,8 @@ A = AluOpType
 ACT = ActivationFunctionType
 CY = 0.83e-3 * 1.25
 PC = 0.42e-3 * 1.25
-WIDE2 = ("G", "O", "TB", "HI", "LO", "WB", "U")
+WIDE2 = ("G", "TB", "HI", "LO", "WB", "U")
+REC = ("G", 0, V + H, 1)
 PLAN = {}
 
 
@@ -60,6 +66,10 @@ def meet(a, b):
 
 def two(a):
     return a[0] in WIDE2 or a[0][0] in "ZW"
+
+
+def swap(o):
+    o["eng"], o["fn"], o["alt"] = "v" if o["eng"] == "a" else "a", o["alt"], o["fn"]
 
 
 def build(g, T, nxt_addr, nxt_mask, neng):
@@ -84,7 +94,7 @@ def build(g, T, nxt_addr, nxt_mask, neng):
 
     def op(eng, fn, rd, wr, cost, lat=0.0, sem=None, acc=False, after=()):
         ops.append({"eng": eng, "fn": fn, "rd": rd, "wr": wr, "cost": cost, "lat": lat, "sem": sem, "acc": acc, "after": list(after),
-                    "kind": 0 if not any(a[0] == "U" for a in rd) else 2 if wr[0][0] == "O" else 1})
+                    "kind": 3 if eng == "p" else 0 if not any(a[0] == "U" for a in rd) else 2 if wr[0] == REC else 1})
         return len(ops) - 1
 
     def S(x):
@@ -122,23 +132,29 @@ def build(g, T, nxt_addr, nxt_mask, neng):
         return R(win).indirect(R(off))
 
     def agat(o, win, off, rd=None):
-        op("a", lambda: g.scalar.activation(R(o), IND(win, off), ACT.Copy), (rd or [win]) + [off], [o], 0.065 + 1.6 * 0.83e-3 * o[2])
+        k = op("a", lambda: g.scalar.activation(R(o), IND(win, off), ACT.Copy), (rd or [win]) + [off], [o], 0.065 + 1.6 * 0.83e-3 * o[2])
+        ops[k]["alt"] = lambda: g.vector.tensor_copy(R(o), IND(win, off))
         return o
 
     def vgat(o, win, off):
-        op("v", lambda: g.vector.tensor_copy(R(o), IND(win, off)), [win, off], [o], 0.05 + 1.6 * 0.83e-3 * o[2])
+        agat(o, win, off)
+        swap(ops[-1])
         return o
 
     def fused(o, win, off, b, alu):
-        op("v", lambda: g.vector.tensor_tensor(R(o), IND(win, off), R(b), alu), [win, off, b], [o], 0.05 + 1.8 * 0.83e-3 * o[2])
+        op("v", lambda: g.vector.tensor_tensor(R(o), IND(win, off), R(b), alu), [win, off, b], [o], 0.05 + 1.6 * 0.83e-3 * o[2])
         return o
 
-    def scat(off, src):
-        win = ("O", 0, V + H, 1)
+    def scat(off, src, add=None):
         n = H // SPLIT
+        c = 0.05 + 3.8 * 0.83e-3 * n
         for k in range(SPLIT):
             o2, s2 = sub(off, k * n // 16, n // 16), sub(src, k * n, n)
-            op("v", lambda o2=o2, s2=s2: g.vector.tensor_copy(IND(win, o2), R(s2)), [o2, s2], [win], 0.05 + 3.8 * 0.83e-3 * n)
+            if add is None:
+                op("v", lambda o2=o2, s2=s2: g.vector.tensor_copy(IND(REC, o2), R(s2)), [o2, s2], [REC], c)
+            else:
+                a2 = sub(add, k * n, n)
+                op("v", lambda o2=o2, s2=s2, a2=a2: g.vector.tensor_tensor(IND(REC, o2), R(s2), R(a2), A.add), [o2, s2, a2], [REC], c)
 
     def mm(o, terms, start, stop):
         if len(terms) > 1 and o[2] >= 256:
@@ -178,46 +194,64 @@ def build(g, T, nxt_addr, nxt_mask, neng):
         op("x", None, [], [dst], 0.0, lat=2.2 + nbytes / 60e3, sem=(sem, neng), after=[k])
 
     dma("a", T.RT[:], T.rt[:], [], [("RT", 0, 160, 1)], 80e3)
-    dma("a", T.G[:, 0:16], T.rec[:, 0:16], [], [("G", 0, 16, 1)], 20e3)
-    big = dma("s", T.G[:, 16:V], T.rec[:, 16:V], [], [("G", 16, V - 16, 1)], 1050e3)
-    chl = dma("s", T.CHI[:], T.ch[:], [], [("CHI", 0, 1024, 1)], 520e3, after=[big])
-    dma("s", T.O[:, 0:V], T.rec[:], [], [("O", 0, V, 1)], 1050e3, after=[chl])
+    big = dma("s", T.G[:, 0:V], T.rec[:], [], [("G", 0, V, 1)], 1050e3)
+    dma("s", T.CHI[:], T.ch[:], [], [("CHI", 0, 1024, 1)], 520e3, after=[big])
     pi = iota(new("IP", 1), [[0, 1]], 0, 1)
     ri = ts(new("IP", 1), pi, 15, A.bitwise_and)
     RF = cp(f(1), ri)
     RF2 = ts(f(1), ri, 2.0, A.mult)
-    RF8 = ts(f(1), ri, 8.0, A.mult)
-    PP = ts(f(1), ri, 2.0, A.mult, 13.0 / 128, A.add)
-    PP2 = ts(f(1), ri, 2.0, A.mult, 13.0 / 128 + 0.375, A.add)
+    RF16 = ts(f(1), ri, 16.0, A.mult, 7.5, A.add)
+    PQ = ts(f(1), ri, 2.0, A.mult, 0.5, A.add)
     E8 = iota(f(8), [[0, 8]], 1, 0)
     asel(E8, [[-16, 8]], A.is_ge, 0.0, 0, 1)
     asel(E8, [[16, 8]], A.is_ge, 0.0, 15, -1)
-    EB = mset(new("WB", 144), 0.0)
-    ts(sub(EB, 16, 8, 16), E8, 3.0 / 64, A.mult)
-    EK = mset(new("WB", 144), 0.0)
-    ts(sub(EK, 16, 8, 16), E8, 65536.0, A.mult)
-    KU = mset(new("WB", 32), -8.5 * 65536)
-    KS = mset(new("WB", 32), -65536.0)
+
+    def summing(scale, twice=True):
+        k = mset(new("WB", 144), 0.0)
+        ts(sub(k, 16, 8, 16), E8, scale, A.mult)
+        if twice:
+            ts(sub(k, 24, 8, 16), E8, scale, A.mult)
+        return k
+
+    def wrap(bank, lhs, tile, n, pre):
+        o = (bank, 0, 2 * n, 1)
+        mm(o, pre, True, False)
+        mm(o, [(sub(lhs, 16 - r, 128), sub(tile, r, 2 * n, 8)) for r in range(8)], False, True)
+        s = f(2 * n)
+        op("v", lambda: g.vector.tensor_tensor_scan(R(s), R(sub(RS, 0, 2 * n)), R(o), 0.0, A.add, A.max), [RS, o], [s], CY * 64)
+        return sub(s, 1, n, 2)
+    EB = {False: summing(1.0 / 32), True: summing(1.0 / 64)}
     ID = iota(new("WB", 128), [[0, 128]], 1, 0)
     asel(ID, [[-1, 128]], A.is_equal, 0.0, 0, 1)
-    IDN = ts(new("WB", 128), ID, -1.0, A.mult)
+    ids = {1.0: ID}
+
+    def I(x):
+        if x not in ids:
+            ids[x] = ts(new("WB", 128), ID, x, A.mult)
+        return ids[x]
+    IDN = I(-1.0)
     C32 = iota(new("WB", 32), [[32, 32]], 0, 0)
-    C64 = iota(new("WB", 32), [[64, 32]], 0, 0)
-    TH32 = ts(f(), C32, 0.4, A.add)
-    TH64 = ts(f(), C64, 0.05, A.add)
-    mset(("G", 0, 1, 1), 256.0)
+    C64 = iota(new("WB", 64), [[32, 32], [0, 2]], 0, 0)
+    RS = mset(f(64), 0.0)
+    mset(sub(RS, 0, 32, 2), -2.0 ** 50)
+    ONE = mset(new("WB", 160), 1.0)
+    OUT = new("WB", 64)
+    ts(sub(OUT, 0, 32, 2), sub(ONE, 0, 32), ts(f(1), ri, 7.5, A.is_gt), A.mult)
+    ts(sub(OUT, 1, 32, 2), sub(ONE, 0, 32), ts(f(1), ri, 7.5, A.is_lt), A.mult)
+    OUTS = {False: ts(new("WB", 64), OUT, -4096.0, A.mult, -8.5 / 32, A.add), True: ts(new("WB", 64), OUT, -4096.0, A.mult, -0.5 / 32, A.add)}
+    CQ = ts(f(), C32, 2.0, A.mult, PQ, A.add)
+    C32M = iota(new("WB", 64), [[0, 2], [32, 32]], -4096, 0)
+    DC = iota(new("WB", 64), [[0, 2], [1, 32]], 0, 0)
+    DR = ts(new("WB", 64), sub(ONE, 0, 64), ts(f(1), ri, 32.0, A.mult, 4096.0, A.add), A.mult)
+    mset(("G", V, H, 1), 0.0)
     for t in range(ST):
         mset(("G", NB[t], 16, 1), 256.0)
-    IDH = ts(new("WB", 128), ID, 0.5, A.mult)
-    IDM2 = ts(new("WB", 128), ID, -2.0, A.mult)
+    KO = iota(new("WB", 256), [[1, 8], [0, 32]], 1, 0)
+    LR = ts(new("WB", 32), sub(ONE, 0, 32), RF, A.mult)
     KE = []
     for o in range(4):
         m1 = ts(f(1), ri, 4 * o + 0.5, A.subtract)
-        m2 = tt(f(1), m1, m1, A.mult)
-        m3 = ts(f(1), m2, 0.5, A.is_lt)
-        k = mset(new("WB", 144), 0.0)
-        ts(sub(k, 16, 8, 16), E8, m3, A.mult)
-        KE.append(k)
+        KE.append(summing(ts(f(1), tt(f(1), m1, m1, A.mult), 0.5, A.is_lt), False))
     BD = iota(new("WB", 128), [[0, 128]], 1, 0)
     asel(BD, [[-16, 8], [0, 16]], A.is_ge, 0.0, 0, 1)
     asel(BD, [[16, 8], [0, 16]], A.is_ge, 0.0, 15, -1)
@@ -225,325 +259,300 @@ def build(g, T, nxt_addr, nxt_mask, neng):
     asel(J, [[0, 2], [-16, 8], [0, 16]], A.is_ge, 999.0, 0, 1)
     asel(J, [[0, 2], [16, 8], [0, 16]], A.is_ge, 999.0, 15, -1)
     ts(J, J, 7.5, A.subtract)
-    J8 = ts(f(6), iota(f(6), [[128, 6]], 0, 0), RF8, A.add)
+    J16 = ts(f(4), iota(f(4), [[256, 4]], 0, 0), RF16, A.add)
     NH = mset(new("WB", H), -0.5)
     M75 = mset(new("WB", 2), -7.5)
-    AP0, AP1, YP1 = f(160), f(160), f(160)
-    act(sub(AP0, 0, 32), iota(f(), [[32, 32]], 16, 0), ACT.Identity, bias=RF2)
-    act(sub(AP0, 32, 128), iota(f(128), [[1024, 4], [32, 32]], 17, 0), ACT.Identity, bias=RF2)
-    act(AP1, iota(f(160), [[512, 5], [16, 32]], 16, 0), ACT.Identity, bias=RF)
-    act(sub(YP1, 0, 128), iota(f(128), [[1024, 4], [32, 32]], 16 + CW[1] + 1, 0), ACT.Identity, bias=RF2)
-    act(sub(YP1, 128, 32), iota(f(), [[16, 32]], 16 + CW[1] + 4096, 0), ACT.Identity, bias=RF)
-    APN = [AP0, AP1, AP1]
-    YPN = [ts(f(160), YP1, float(CW[0] - CW[1]), A.add), YP1, YP1]
-    DUM = act(f(128), iota(f(128), [[0, 4], [16, 32]], V, 0), ACT.Identity, bias=RF)
-    POS = act(f(128), iota(f(128), [[512, 4], [16, 32]], 0, 0), ACT.Identity, bias=RF)
-    lbase = [NB[t + 1] - 2048 for t in range(ST)]
-    LPOS = [ts(f(128), POS, float(lbase[t]), A.add) for t in range(ST - 1)]
-    CODE = ts(f(128), POS, 1.0, A.add, 4096.0, A.mult)
-    APA = [ts(f(128), sub(APN[t], 0, 128), float(NB[t]), A.add) for t in range(ST)]
-    LKS = [f(192) for t in range(ST)]
+    IF8 = ts(f(128), ID, -8192.0, A.mult)
+    HA0, LA0, HY, LY = new("WB", 160), new("WB", 160), new("WB", 160), new("WB", 160)
+    iota(sub(HA0, 0, 32), [[32, 32]], 0, 0)
+    iota(sub(HA0, 32, 128), [[1024, 4], [32, 32]], 0, 0)
+    iota(sub(HY, 0, 128), [[1024, 4], [32, 32]], 0, 0)
+    ts(sub(LA0, 0, 32), sub(ONE, 0, 32), RF2, A.mult, 16.0, A.add)
+    ts(sub(LA0, 32, 128), sub(ONE, 0, 128), RF2, A.mult, 17.0, A.add)
+    ts(sub(LY, 0, 128), sub(ONE, 0, 128), RF2, A.mult, 17.0, A.add)
+    HA, LA = [HA0] * ST, [LA0] * ST
+    APA = [act(f(128), mm(("ps7", 0, 128, 1), [(ID, sub(HA[t], 0, 128)), (ID, sub(LA[t], 0, 128))], True, True), ACT.Identity,
+               bias=float(NB[t])) for t in range(ST)]
+    LKS = [new("WB", 192) for t in range(ST)]
+    SGS = [new("WB", 192) for t in range(ST)]
     for t in range(ST):
         mset(sub(LKS[t], 0, 32), 1.0)
+        mset(sub(SGS[t], 0, 32), 1.0)
+        mset(sub(SGS[t], 160, 32), -1.0)
     hi, lo, chi = ("HI", 0, 1024, 1), ("LO", 0, 1024, 1), ("CHI", 0, 1024, 1)
     for k in range(4):
         h = cp(sub(hi, 256 * k, 256), sub(chi, 256 * k, 256))
-        tt(sub(lo, 256 * k, 256), mm(("ps%d" % (6 + k % 2), 0, 256, 1), [(IDN, h)], True, True), sub(chi, 256 * k, 256), A.add)
+        tt(sub(lo, 256 * k, 256), mm(("ps%d" % (6, 4)[k % 2], 0, 256, 1), [(IDN, h)], True, True), sub(chi, 256 * k, 256), A.add)
     TBW = [("TB0", 0, 1, 1), ("TB1", 0, 1, 1)]
     op("v", lambda: g.vector.memset(T.TB[:], 0.0), [], TBW, CY * V / 2)
     dma("s", T.TB[0:128:4, :], T.HI[:], [hi], [TBW[0]], 260e3)
     dma("s", T.TB[1:128:4, :], T.LO[:], [lo], [TBW[1]], 260e3)
-    mset(("O", V, H, 1), 0.0)
 
-    def count(bank, cmpt, signed, p, w, c0=0):
+    def count(bank, cmpt, signed, p, w, th, c0=0):
         n = p[2]
-        o = (bank, 0, n, 1)
-        mm(o, [(ID, sub(C64 if signed else C32, c0, n))], True, False)
-        mm(o, [(sub(EB, 16 - r, 128), sub(cmpt, r, n, 16)) for r in range(16)], False, True)
-        if signed:
-            ts(p, o, 0.5, A.mult, PP2, A.add)
-        else:
-            ts(p, o, PP, A.add)
-        tt(w, o, sub(TH64 if signed else TH32, c0, n), A.is_gt)
-        return p, w
+        o = wrap(bank, EB[signed], cmpt, n, [(ID, sub(C64, 2 * c0, 2 * n)), (ID, sub(OUTS[signed], 0, 2 * n))])
+        if p[0] == "U":
+            ts(p, o, PQ, A.add)
+        tt(w, o, th, A.is_gt)
+        return o
 
-    def rotate(bank, win, off, PM):
-        rg = agat(f(80), win, off)
-        return mm((bank, 0, 64, 1), [(sub(PM, 0, 128), sub(rg, 0, 64)), (sub(PM, 128, 128), sub(rg, 2, 64))], True, True)
+    def rotate(out, win, off, PM):
+        rg = agat(f(48), win, off)
+        return mm(out, [(sub(PM, 0, 128), sub(rg, 0, 32)), (sub(PM, 128, 128), sub(rg, 1, 32))], True, True)
 
     def regions(t):
         p0 = NB[t] + 16 + CW[t]
         P = [("G", p0 + 1024 * o, 1024, 1) for o in range(4)]
         X = [sub(p, 0, H, 2) for p in P]
-        Y = [sub(p, 1, H, 2) for p in P] + [("G", p0 + 4096, H, 1)]
-        if t == 0:
-            AA = [("G", NB[t] + 16, H, 2)] + [("G", NB[t] + 17 + 1024 * o, H, 2) for o in range(4)]
-        else:
-            AA = [("G", NB[t] + 16 + H * o, H, 1) for o in range(5)]
+        Y = [sub(p, 1, H, 2) for p in P]
+        AA = [("G", NB[t] + 16, H, 2)] + [("G", NB[t] + 17 + 1024 * o, H, 2) for o in range(4)]
         return NB[t], P, X, Y, AA
 
-    def champion_level(t, o, st, RR):
+    def champion_level(t, o, st, AC):
         nb, P, X, Y, AA = regions(t)
-        cm = new("WB", H)
-        if o >= 2:
-            fused(cm, ("G", nb, 16 + H * o, 1), st["p16"], AA[o], A.is_gt)
-        else:
-            act(cm, mm(("ps5", 0, H, 1), [(IDN, AA[1]), (ID, AA[0])], True, True), ACT.Sign, bias=-0.5)
-        ac = act(f(), sub(RR, 32 * o, 32), ACT.Identity, bias=4096.0 * o)
-        st["ac"].append(ac)
-        k = ("ps1", 0, 32, 1)
-        mm(k, [(ID, KS if o == 1 else KU)], True, False)
-        mm(k, [(sub(EK, 16 - r, 128), sub(cm, r, 32, 16)) for r in range(16)], False, True)
-        st["p"] = tt(f(), tt(f(), k, sub(APN[t], 32 * o, 32), A.min), st["p"], A.max)
-        st["p16"] = cp(new("U", 32), st["p"])
-        st["cur"] = tt(new("IP", 32) if o == 4 else f(), tt(f(), k, ac, A.min), st["cur"], A.max)
-        st["win"] = ("G", nb, 16 + CW[t], 1)
+        C = [None] + [("G", nb + 16 + 1024 * k, 1024, 1) for k in range(4)]
+        p2, w, cm = new("U", 32), f(), new("WB", H)
+        parts = PARTS[t]
+        n = H // parts
+        for k in range(parts):
+            ck, ak = sub(cm, n * k, n), sub(AA[o], n * k, n)
+            signed = CH[t][o - 1] == "s"
+            if o > 1:
+                wk, pk = sub(C[o - 1], 0, 2 * n * (k + 1)), sub(st["p16"], n // 16 * k, n // 16)
+                if not signed:
+                    fused(ck, wk, pk, ak, A.is_gt)
+                agat(sub(C[o], 2 * n * k, n, 2), wk, pk)
+            if signed:
+                d = mm((("ps5", "ps2")[k], 0, n, 1), [(IDN, ak), (ID, sub(C[o], 2 * n * k, n, 2))], True, True)
+                act(ck, d, ACT.Sign, bias=-0.5)
+            c0, cn = n // 16 * k, n // 16
+            count(("ps1", "ps0")[k], ck, signed, sub(p2, c0, cn), sub(w, c0, cn), sub(C32, c0, cn), c0)
+        u = tt(f(), w, sub(AC, 32 * o, 32), A.mult)
+        old = st["cur"]
+        st["cur"] = tt(f(), u, old, A.max)
+        if o == 4:
+            st["curi"] = tt(new("IP", 32), u, old, A.max)
+        st["p16"], st["win"] = p2, C[o]
 
     rt = ("RT", 0, 160, 1)
-    r16 = cp(new("U", 160), rt)
-    RR = cp(f(160), rt)
+    r16 = cp(new("U", 160), tt(f(160), ts(vp(0, 160), rt, 0.5, A.is_lt, float(NB[0]), A.mult), rt, A.add))
+    AC = tt(f(160), mm(vp(160, 160), [(I(4096.0), sub(KO, 0, 160))], True, True), rt, A.add)
     nb, P, X, Y, AA = regions(0)
     for o in range(5):
         for k in range(2):
-            (vgat if o in (0, 2) else agat)(sub(AA[o], 256 * k, 256), ("G", 0, V, 1), sub(r16, 32 * o + 16 * k, 16))
-    st = {"cur": sub(RR, 0, 32), "ac": [sub(RR, 0, 32)]}
-    C = [None] + [("G", nb + 16 + 1024 * o, 1024, 1) for o in range(4)]
-    p = None
+            (vgat if o in (0, 2) else agat)(sub(AA[o], 256 * k, 256), ("G", 0, NB[0] + 16, 1), sub(r16, 32 * o + 16 * k, 16))
+    st = {"cur": sub(AC, 0, 32)}
     for o in range(1, 5):
-        p2, w, cm = new("U", 32), f(), new("WB", H)
-        for k in range(2):
-            ck, ak = sub(cm, 256 * k, 256), sub(AA[o], 256 * k, 256)
-            if o == 1:
-                d = mm((("ps5", "ps2")[k], 0, 256, 1), [(IDN, ak), (ID, sub(AA[0], 256 * k, 256))], True, True)
-                act(ck, d, ACT.Sign, bias=-0.5)
-            else:
-                wk, pk = sub(C[o - 1], 0, 512 * k + 512), sub(p, 16 * k, 16)
-                fused(ck, wk, pk, ak, A.is_gt)
-                agat(sub(C[o], 512 * k, 256, 2), wk, pk)
-            count(("ps1", "ps0")[k], ck, o == 1, sub(p2, 16 * k, 16), sub(w, 16 * k, 16), 16 * k)
-        p = p2
-        ac = act(f(), sub(RR, 32 * o, 32), ACT.Identity, bias=4096.0 * o)
-        st["ac"].append(ac)
-        st["cur"] = tt(new("IP", 32) if o == 4 else f(), tt(f(), w, ac, A.mult), st["cur"], A.max)
-    st["p16"], st["win"] = p, C[4]
+        champion_level(0, o, st, AC)
 
-    keys, losers, rotd, code1 = [], [], None, None
+    keys, losers, rotd = [], [], None
     for t in range(ST):
         nb, P, X, Y, AA = regions(t)
         last = t == ST - 1
         Z, W = ("Z%d" % t, 0, H, 1), ("W%d" % t, 0, H, 1)
         ZT, WT = ("ZT%d" % t, 0, 16, 1), ("WT%d" % t, 0, 16, 1)
         cur = st["cur"]
-        agat(ZT, sub(st["win"], 0, 512) if t == 0 else st["win"], sub(st["p16"], 0, 1))
+        agat(ZT, sub(st["win"], 0, 32), sub(st["p16"], 0, 1))
         send(WT, ZT, "at%d" % t, 30e3)
         agat(Z, st["win"], st["p16"])
         send(W, Z, "aw%d" % t, 131e3)
-        m = ts(new("IP", 32), cur, 4095, A.bitwise_and)
+        ky, ls = f(160), f(128)
+        m = ts(new("IP", 32), st["curi"], 4095, A.bitwise_and)
         m16 = cp(new("U", 32), m)
         G1 = agat(new("WB", H), ("TB", 0, V, 1), m16, TBW)
-        MB = ("ps4", 0, H, 1)
-        mm(MB, [(IDH, NH), (IDH, Z)], True, False)
-        pq = f(128)
-        for o in range(4):
-            ts(sub(pq, 32 * o, 32), cur, 4096.0 * (o + 1), A.is_ge)
-        npq = act(f(128), pq, ACT.Identity, bias=BIG, scale=-BIG)
-        if t == 0:
-            gm, ei, ep = pq, None, npq
-        else:
-            e = vp(0, 128)
-            for o in range(4):
-                tt(sub(e, 32 * o, 32), sub(keys[t - 1], 32 * o, 32), m, A.is_equal)
-            hm = tt(f(128), pq, e, A.subtract)
-            ei = tt(f(128), e, losers[t - 1], A.mult)
-            ep = tt(f(128), tt(vp(128, 128), e, LPOS[t - 1], A.mult), npq, A.add)
-            gm = hm
-            if t == 2:
-                e1 = vp(256, 128)
-                for o in range(4):
-                    tt(sub(e1, 32 * o, 32), sub(keys[0], 32 * o, 32), m, A.is_equal)
-                tt(e1, e1, code1, A.mult)
-                e2 = vp(384, 96)
-                for o in range(3):
-                    tt(sub(e2, 32 * o, 32), sub(rotd, 64 * o, 32, 2), m, A.is_equal)
-                tt(sub(e1, 0, 96), sub(e1, 0, 96), tt(f(96), e2, sub(rotd, 1, 96, 2), A.mult), A.max)
-                ci = tt(new("IP", 128), e1, hm, A.mult)
-                i1 = ts(new("IP", 128), ci, 4095, A.bitwise_and)
-                p1 = ts(new("IP", 128), ci, 12, A.arith_shift_right)
-                a1 = ts(vp(0, 128), p1, 0.0, A.is_gt)
-                gm = tt(f(128), hm, a1, A.subtract)
-                u1 = ts(vp(128, 128), p1, 0.0, A.is_gt, float(lbase[0] - 1), A.mult)
-                tt(u1, u1, p1, A.add)
-                ep = tt(f(128), u1, ep, A.add)
-                ei = tt(f(128), i1, ei, A.add)
+        MB = ("ps1", 0, H, 1)
+        mm(MB, [(I(0.5), NH), (I(0.5), Z)], True, False)
+        SG, LK = SGS[t], LKS[t]
+        for o in range(1, 5):
+            act(sub(SG, 32 * o, 32), cur, ACT.Sign, bias=-4096.0 * (o + 1))
+        Ta = mm(vp(288, 160), [(I(4096.0), sub(KO, 64, 160)), (I(-4096.0), sub(SG, 0, 160)), (I(4096.0), sub(SG, 32, 160))], True, True)
+        ACa = tt(new("IP", 160), Ta, AC, A.min)
+        xi = new("IP", 160)
+        ts(sub(xi, 128, 32), sub(ACa, 128, 32), 4095, A.bitwise_and)
+
+        def found(e, ks):
+            for o in range(e[2] // 32):
+                tt(sub(e, 32 * o, 32), sub(ks, 32 * o, 32), m, A.is_equal)
+            return e
+        el = None
+        if t == 1:
+            el = tt(f(128), found(vp(0, 128), keys[0]), losers[0], A.mult)
+        if t == 2:
+            lb = tt(vp(128, 128), found(vp(0, 128), keys[0]), losers[0], A.mult)
+            lc = tt(f(96), found(vp(256, 96), sub(rotd, 0, 96)), sub(rotd, 96, 96), A.mult)
+            tt(sub(lb, 0, 96), sub(lb, 0, 96), lc, A.max)
+            ea = found(vp(0, 128), keys[1])
+            el = tt(f(128), lb, tt(f(128), ea, tt(f(128), losers[1], lb, A.subtract), A.mult), A.add)
         sb = ("ps5", 0, 1, 1)
         mm(sb, [(ID, sub(M75, 0, 1)), (BD, sub(WT, 0, 1))], True, True)
+        j1 = ts(new("IP", 4), J16, sb, A.add)
         f16 = ts(f(1), sb, MAGIC16, A.add, MAGIC16, A.subtract)
-        s0m = tt(f(1), f16, sb, A.subtract)
-        j1 = ts(new("IP", 6), J8, f16, A.add)
-        j2 = ts(new("IP", 6), j1, 3, A.arith_shift_right, 63, A.bitwise_and)
-        off = sub(cp(new("U", 6), j2), 0, 5)
-        PM = act(f(256), act(f(256), J, ACT.Abs, bias=s0m), ACT.Relu, bias=1.0, scale=-1.0)
-        ne = vp(256, 160)
-        for o in range(5):
-            tt(sub(ne, 32 * o, 32), st["ac"][o], cur, A.not_equal)
-        Ra = tt(f(160), ne, RR, A.mult)
-        Bi = f(128)
-        rws = []
+        j2 = ts(new("IP", 4), j1, 4, A.arith_shift_right, 31, A.bitwise_and)
+        off = sub(cp(new("U", 4), j2), 0, 3)
+        if PMV[t]:
+            PM = ts(f(256), J, tt(f(1), sb, f16, A.subtract), A.is_equal)
+        else:
+            PM = act(f(256), act(f(256), J, ACT.Abs, bias=tt(f(1), f16, sb, A.subtract)), ACT.Relu, bias=1.0, scale=-1.0)
+        rw = f(128)
         for o in range(4):
-            kd = mm(("ps6", 32 * o, 32, 1), [(sub(KE[o], 16 - r, 128), sub(G1, r, 32, 16)) for r in range(16)], True, True)
-            rw = f(64)
-            if ei is None:
-                chm = tt(sub(rw, 0, 32, 2), kd, sub(gm, 32 * o, 32), A.mult)
-            else:
-                chm = tt(f(), kd, sub(gm, 32 * o, 32), A.mult)
-                tt(sub(rw, 0, 32, 2), chm, sub(ei, 32 * o, 32), A.add)
-            tt(sub(rw, 1, 32, 2), chm, sub(ep, 32 * o, 32), A.add)
-            rws.append(rw)
-        for o in range(4):
-            rb = rotate(("ps7", "ps1")[o % 2], rws[o], off, PM)
-            xp = tt(f(), sub(rb, 1, 32, 2), sub(APA[t], 32 * o, 32), A.min)
-            x16 = cp(new("U", 32), xp)
-            act(sub(Bi, 32 * o, 32), sub(rb, 0, 32, 2), ACT.Copy)
-            (vgat if (t, o) == (0, 1) else agat)(X[o], ("G", 0, nb + 16 + CW[t], 1), x16)
-            if o == 0:
-                D0 = ("ps5", 0, H, 1)
-                mm(D0, [(ID, Z), (ID, W), (IDM2, X[0])], True, True)
-                mm(MB, [(IDH, W)], False, True)
-                cm0 = act(new("WB", H), D0, ACT.Sign, bias=-0.5, scale=-1.0)
-                if t == 0:
-                    ts(Y[0], MB, MAGIC, A.add, MAGIC, A.subtract)
-                else:
-                    act(Y[0], act(MB, MB, ACT.Identity, bias=MAGIC), ACT.Identity, bias=-MAGIC)
-        if t == 1:
-            code1 = tt(f(128), losers[0], CODE, A.add)
-            rotd = f(192)
-            for o in range(3):
-                rw = f(64)
-                act(sub(rw, 0, 32, 2), sub(keys[0], 32 * o, 32), ACT.Copy)
-                act(sub(rw, 1, 32, 2), sub(code1, 32 * o, 32), ACT.Copy)
-                act(sub(rotd, 64 * o, 64), rotate("ps7", rw, off, PM), ACT.Copy)
-        LK = LKS[t]
-        xa, usey, nd, kp = vp(128, 128), vp(256, 160), vp(0, 128), vp(416, 96)
-        xi, xd, a16 = f(128), f(128), new("U", 160)
-        for lo, n in ((0, 64), (64, 64)):
-            n5 = n + 32 * (lo > 0)
-            xa_, xi_, nd_, lk_, ra_ = sub(xa, lo, n), sub(xi, lo, n), sub(nd, lo, n), sub(LK, lo + 32, n), sub(Ra, lo, n)
-            ts(xa_, sub(Bi, lo, n), 0.0, A.is_le)
-            tt(xa_, xa_, ra_, A.mult)
-            tt(xi_, xa_, sub(Bi, lo, n), A.add)
-            for o in range(lo // 32, (lo + n5) // 32):
-                tt(sub(LK, 32 * o + 32, 32), sub(xi, 32 * o, 32) if o < 4 else sub(Ra, 128, 32), sub(LK, 32 * o, 32), A.min)
-            tt(xa_, xa_, lk_, A.mult)
-            tt(ra_, ra_, xa_, A.subtract)
-            us_ = tt(sub(usey, lo, n5), sub(LK, lo, n5), sub(LK, lo + 32, n5), A.subtract)
+            kd = (("ps6", "ps0")[o // 2], 32 * (o % 2), 32, 1)
+            pre = [(I(2.0 ** 26), sub(ONE, 0, 32)), (I(-2.0 ** 26), sub(SG, 32 * o + 32, 32))]
+            mm(kd, pre + ([(IF8, sub(el, 32 * o, 32))] if el else []) + [(sub(KE[o], 16 - r, 128), sub(G1, r, 32, 16)) for r in range(16)], True, True)
+            if o % 2 and el:
+                tt(sub(rw, 32 * o - 32, 64), (kd[0], 0, 64, 1), sub(el, 32 * o - 32, 64), A.max)
+            elif o % 2:
+                act(sub(rw, 32 * o - 32, 64), (kd[0], 0, 64, 1), ACT.Copy)
+        x16, xa, bp = new("U", 128), new("IP", 128), new("WB", 128)
+        US, ACk, xd, a16 = vp(0, 160), f(160), f(128), new("U", 160)
+        for lo, n in STAGES:
+            rb = ("ps7", lo, n, 1)
+            for o in range(lo // 32, (lo + n) // 32):
+                rotate(sub(rb, 32 * o - lo, 32), sub(rw, 32 * o, 32), off, PM)
+            cp(sub(x16, lo, n), tt(f(n), rb, sub(APA[t], lo, n), A.min))
+            tt(sub(xa, lo, n), rb, sub(ACa, lo, n), A.min)
+            act(sub(bp, lo, n), rb, ACT.Sign, bias=8192.0, scale=-1.0)
+            ts(sub(xi, lo, n), sub(xa, lo, n), 4095, A.bitwise_and)
+            for o in range(lo // 32, (lo + n) // 32):
+                (vgat if XV[t][o] == "v" else agat)(X[o], ("G", 0, nb + 16 + CW[t], 1), sub(x16, 32 * o, 32))
+                tt(sub(LK, 32 * o + 32, 32), sub(xi, 32 * o, 32), sub(LK, 32 * o, 32), A.min)
+                if o == 0:
+                    D0 = ("ps5", 0, H, 1)
+                    mm(D0, [(ID, Z), (ID, W), (I(-2.0), X[0])], True, True)
+                    mm(MB, [(I(0.5), W), (I(-2 * MAGIC), NH)], False, True)
+                    cm0 = act(new("WB", H), D0, ACT.Sign, bias=-0.5, scale=-1.0)
+                    act(Y[0], MB, ACT.Identity, bias=-MAGIC)
+        tt(sub(LK, 160, 32), sub(xi, 128, 32), sub(LK, 128, 32), A.min)
+        for lo, n in ((0, 64), (64, 64), (128, 32)):
+            lk0, lk1, one = sub(LK, lo, n), sub(LK, lo + 32, n), sub(ONE, 0, n)
+            mm(sub(US, lo, n), [(ID, lk0), (IDN, lk1)], True, True)
+            gone = []
+            if lo < 128:
+                gone = [(I(-8192.0), lk1), (I(4096.0), sub(bp, lo, n))]
+                tk = mm(vp(288, n), [(I(4096.0), sub(KO, 96 + lo, n))] + gone, True, True)
+                tt(sub(ACk, lo, n), tk, sub(ACa, lo, n), A.min)
+                nd = mm(vp(352, n), [(ID, DC), (ID, DR), (I(-8192.0), lk1)], True, True)
+                tt(sub(xd, lo, n), nd, sub(xi, lo, n), A.max)
+                mm(vp(160 + lo, n), [(ID, C32M), (I(4096.0), lk1)], True, True)
             if not last:
-                kp_ = ts(sub(kp, 0, n5), sub(Ra, lo, n5), 0.0, A.is_gt)
-                q1 = tt(f(n5), kp_, sub(APN[t], lo, n5), A.mult)
-                tt(kp_, us_, sub(YPN[t], lo, n5), A.mult)
-                cp(sub(a16, lo, n5), tt(kp_, kp_, q1, A.add))
-            ts(nd_, lk_, -8192.0, A.mult)
-            tt(nd_, nd_, sub(DUM, lo, n), A.add)
-            tt(sub(xd, lo, n), nd_, xi_, A.max)
-        RN = ("YR", 0, 160, 1) if last else f(160)
-        ky, ls = f(128), f(128)
-        st2 = {"cur": sub(RN, 0, 32), "ac": [sub(RN, 0, 32)], "p": sub(AP1, 0, 32)}
+                pre = [(ID, sub(HY, lo, n)), (ID, sub(LY, lo, n))] if lo < 128 else [(I(2.0), LR)]
+                t2 = mm(("ps7", 0, n, 1), pre + [(I(16384.0), lk0), (I(-16384.0), lk1)], True, True)
+                r2 = act(f(n), t2, ACT.Identity, bias=CW[t] - 16384.0 + (-4096.0 if lo < 128 else 16.5 + 3072))
+                t1 = mm(vp(416, n), [(ID, sub(HA[t], lo, n)), (ID, sub(LA[t], lo, n)), (I(-4096.0), sub(SG, lo, n)),
+                                     (I(4096.0), sub(SG, lo + 32, n))] + gone, True, True)
+                if lo < 128:
+                    ts(sub(a16, lo, n), tt(f(n), t1, r2, A.max), 4096.0, A.add)
+        if t == 1:
+            rotd = f(192)
+            for k, src in enumerate((keys[0], losers[0])):
+                for o in range(3):
+                    rotate(("ps7", 32 * o, 32, 1), sub(src, 32 * o, 32), off, PM)
+                act(sub(rotd, 96 * k, 96), ("ps7", 0, 96, 1), ACT.Copy)
+        AN = f(160)
+        st2 = {"cur": sub(AN, 0, 32)}
 
         def root(o, y):
-            tt(sub(RN, 32 * o, 32), tt(f(), sub(usey, 32 * o, 32), y, A.mult), sub(Ra, 32 * o, 32), A.add)
             if not last:
-                agat(regions(t + 1)[4][o], ("G", nb, (Y[o][1] + Y[o][2] * Y[o][3] - nb) // 2 * 2, 1), sub(a16, 32 * o, 32))
+                tt(sub(AN, 32 * o, 32), tt(f(), sub(US, 32 * o, 32), y, A.mult), sub(ACk if o < 4 else ACa, 32 * o, 32), A.add)
+                agat(regions(t + 1)[4][o], ("G", nb, 16 + CW[t] + 1024 * min(o + 1, 4), 1), sub(a16, 32 * o, 32))
                 if o >= 1:
-                    champion_level(t + 1, o, st2, RN)
+                    champion_level(t + 1, o, st2, AN)
 
         scat(m16, Y[0])
-        y = m
+        y = cp(sub(ky, 0, 32), m) if last else m
         p = None
-        pend = []
+        pend, q16 = [], []
         for o in range(4):
+            how = HOW[t][o]
             if o == 0:
                 cm = cm0
-            elif o in MF[t]:
+            elif how == "f":
                 cm = fused(new("WB", H), P[o - 1], p, X[o], A.is_lt)
                 agat(Y[o], P[o - 1], p)
             else:
                 agat(Y[o], P[o - 1], p)
                 dd = mm(("ps6", 0, H, 1), [(ID, X[o]), (IDN, Y[o])], True, True)
                 cm = act(new("WB", H), dd, ACT.Sign, bias=-0.5)
-            p, w = count("ps0", cm, o not in MF[t], new("U", 32), f())
+            p, w = new("U", 32) if o < 3 or (last and LASTPN) else f(), f()
+            sc = count("ps0", cm, how == "s", p, w, vp(160 + 32 * o, 32))
             if o == 3 and not last:
-                agat(Y[4], P[3], p)
+                cp(sub(a16, 128, 32), tt(f(), t1, tt(f(), sc, r2, A.add), A.max))
+            q16.append(cp(new("U", 32), tt(f(), CQ, sc, A.subtract)) if LG[t][o] == "g" and not (last and o == 3 and LASTPN) else None)
             root(o, y)
-            yd = tt(f(), y, sub(nd, 32 * o, 32), A.max)
-            d = tt(f(), yd, sub(xd, 32 * o, 32), A.subtract)
+            d = tt(f(), y, sub(xd, 32 * o, 32), A.subtract)
             x = tt(f(), w, d, A.mult)
-            y = tt(sub(ky, 32 * o, 32), sub(xd, 32 * o, 32), x, A.add)
-            pend.append(cp(new("U", 32), tt(sub(ls, 32 * o, 32), yd, x, A.subtract)))
+            lsr = tt(sub(ls, 32 * o, 32), y, x, A.subtract)
+            y = tt(sub(ky, 32 * o + 32, 32), sub(xd, 32 * o, 32), x, A.add)
+            pend.append(cp(new("U", 32), lsr))
         root(4, y)
+        if last:
+            cp(sub(ACk, 128, 32), sub(ACa, 128, 32))
+            rk = tt(f(160), ACk, mm(("ps1", 0, 160, 1), [(I(4096.0), sub(KO, 0, 160))], True, True), A.subtract)
+            tt(("YR", 0, 160, 1), tt(US, US, ky, A.mult), rk, A.add)
         for o in range(4):
-            bank = ("ps2" if o % 2 else "ps4", 0, H, 1)
-            nw = ("G", lbase[t] + H * o, H, 1)
-            if last and o == 3:
-                pn = new("WB", 2 * H)
-                mm(bank, [(ID, Y[o]), (IDN, X[o])], True, True)
-                sg = act(new("WB", H), bank, ACT.Sign)
-                act(sub(pn, 0, H, 2), mm(bank, [(ID, Y[o]), (IDN, sg)], True, True), ACT.Copy)
+            b1, b2 = (("ps2", "ps4")[o % 2], 0, H, 1), ("ps5", 0, H, 1)
+            if last and o == 3 and LASTPN:
+                pn, nw = new("WB", 2 * H), new("WB", H)
+                mm(b1, [(ID, Y[o]), (IDN, X[o])], True, True)
+                sg = act(new("WB", H), b1, ACT.Sign)
+                act(sub(pn, 0, H, 2), mm(b2, [(ID, Y[o]), (IDN, sg)], True, True), ACT.Copy)
                 act(sub(pn, 1, H, 2), mm(("ps7", 0, H, 1), [(ID, X[o]), (ID, sg)], True, True), ACT.Copy)
                 for k in range(2):
                     agat(sub(nw, 256 * k, 256), pn, sub(p, 16 * k, 16))
+                scat(pend[o], nw)
+            elif LG[t][o] == "g":
+                old, sg = new("WB", H), new("WB", H)
+                parts = 2 if last and o == 3 else 1
+                n = H // parts
+                for k in range(parts):
+                    bk, ok = ((b1[0], b2[0])[k], 0, n, 1), sub(old, n * k, n)
+                    agat(ok, P[o], sub(q16[o], n // 16 * k, n // 16))
+                    if o < 3:
+                        mm(bk, [(ID, Y[o + 1]), (IDN, ok)], True, True)
+                    else:
+                        mm(bk, [(ID, sub(X[o], n * k, n)), (ID, sub(Y[o], n * k, n)), (I(-2.0), ok)], True, True)
+                    act(sub(sg, n * k, n), bk, ACT.Sign)
+                scat(pend[o], old, sg)
             else:
-                mm(bank, [(ID, X[o]), (ID, Y[o]), (IDM2, Y[o + 1])], True, True)
-                sg = act(new("WB", H), bank, ACT.Sign, scale=-1.0)
-                mm(bank, [(ID, X[o]), (ID, Y[o]), (IDN, Y[o + 1]), (ID, sg)], True, True)
-                act(nw, bank, ACT.Copy)
-            scat(pend[o], nw)
-        keys.append(ky)
+                mm(b1, [(ID, X[o]), (ID, Y[o]), (IDN, Y[o + 1])], True, True)
+                old = act(new("WB", H), b1, ACT.Copy)
+                mm(b1, [(IDN, Y[o + 1]), (ID, old)], True, True)
+                scat(pend[o], old, act(new("WB", H), b1, ACT.Sign, scale=-1.0))
+        keys.append(sub(ky, 32, 128))
         losers.append(ls)
-        st, RR = st2, RN
+        st, AC = st2, AN
     dma("a", T.yrt[:], T.YR[:], [("YR", 0, 160, 1)], [], 80e3)
-    dma("s", T.yrec[:], T.O[:, 0:V], [("O", 0, V, 1)], [], 1050e3)
+    dma("s", T.yrec[:], T.G[:, 0:V], [("G", 0, V, 1)], [], 1050e3)
     return ops
 
 
-def place(ops, deps, succ, tail):
+def sweep(ops, after, key, first):
     n = len(ops)
-    left = [len(deps[k]) for k in range(n)]
-    start, done, rdy = [0.0] * n, [0.0] * n, [0.0] * n
-    free = {e: 0.0 for e in "vapgsx"}
-    avail = {e: [] for e in "vapgsx"}
-    for k in range(n):
-        if left[k] == 0:
-            avail[ops[k]["eng"]].append(k)
-    order = []
-    while len(order) < n:
-        best = None
-        for e in "xgspav":
-            if not avail[e]:
-                continue
-            now = max(free[e], min(rdy[k] for k in avail[e]))
-            c = max((k for k in avail[e] if rdy[k] <= now), key=lambda k: tail[k])
-            for k in avail[e]:
-                if now < rdy[k] < now + LOOK * ops[c]["cost"] and tail[k] > tail[c] + 1.0:
-                    c, now = k, rdy[k]
-            if best is None or now < best[0]:
-                best = (now, c)
-        now, c = best
-        e = ops[c]["eng"]
-        avail[e].remove(c)
-        start[c] = now
-        free[e] = now + ops[c]["cost"]
-        done[c] = free[e] + ops[c]["lat"]
-        order.append(c)
-        for s in succ[c]:
-            if deps[s][c]:
-                rdy[s] = max(rdy[s], done[c] + WAKE)
-            elif ops[s]["eng"] == "s":
-                rdy[s] = max(rdy[s], done[c] - 1.8)
-            else:
-                rdy[s] = max(rdy[s], free[e])
-            left[s] -= 1
-            if left[s] == 0:
-                avail[ops[s]["eng"]].append(s)
-    return order, start, done
+    rdy = list(first)
+    start = [0.0] * n
+    busy = {e: [] for e in "vapgs"}
+    for k in sorted(range(n), key=lambda k: key[k]):
+        t, c, e = rdy[k], ops[k]["cost"], ops[k]["eng"]
+        if e != "x":
+            b = busy[e]
+            i = len(b)
+            while i > 0 and b[i - 1][1] > t:
+                i -= 1
+            while i < len(b) and b[i][0] < t + c - 1e-9:
+                t = max(t, b[i][1])
+                i += 1
+            b.insert(i, (t, t + c))
+        start[k] = t
+        for s, lag in after[k]:
+            if t + lag > rdy[s]:
+                rdy[s] = t + lag
+    return start
+
+
+def justify(ops, suc, rsuc, key):
+    n = len(ops)
+    fw = sweep(ops, suc, key, [0.0] * n)
+    bw = sweep(ops, rsuc, [(-fw[k] - ops[k]["cost"], -k) for k in range(n)], [o["lat"] for o in ops])
+    return sweep(ops, suc, [(-bw[k] - ops[k]["cost"], k) for k in range(n)], [0.0] * n)
 
 
 def replay(ops, dl, order, k, wake, far):
@@ -584,39 +593,58 @@ def schedule(ops):
                         deps[k].setdefault(j, False)
                     else:
                         deps[k][j] = True
-        for a in o["rd"]:
-            seen.setdefault(a[0], []).append((k, a, False))
-        for a in o["wr"]:
-            seen.setdefault(a[0], []).append((k, a, True))
-    succ = [[] for _ in range(n)]
-    for k in range(n):
-        for j in deps[k]:
-            succ[j].append(k)
-    base = [0.0] * n
-    for k in range(n - 1, -1, -1):
-        base[k] = ops[k]["cost"] + ops[k]["lat"] + max([base[s] + WAKE for s in succ[k]] + [0.0])
-    dl = []
+                elif a[0][:2] == "ps" and o["eng"] == "p":
+                    deps[k].setdefault(j, False)
+        for a, wr in [(a, False) for a in o["rd"]] + [(a, True) for a in o["wr"]]:
+            s = seen.setdefault(a[0], [])
+            if a[0][:2] == "ps" and s and ops[s[-1][0]]["eng"] != o["eng"]:
+                s[:] = [x for i, x in enumerate(s) if all(ops[y[0]]["eng"] == ops[s[-1][0]]["eng"] for y in s[i:])]
+            s.append((k, a, wr))
+    dl, pre, suc, rsuc = [], [], [[] for _ in range(n)], [[] for _ in range(n)]
     for k in range(n):
         dl.append([(j, w) for j, w in deps[k].items() if not (w and any(deps[i].get(j) for i in deps[k] if i > j))])
-    best = place(ops, deps, succ, base)
-    score = sum(replay(ops, dl, best[0], k, w, x) for k, w, x in VIEWS)
+        pre.append([(j, ops[j]["cost"] + (ops[j]["lat"] + WAKE if w else ops[j]["lat"] - 1.8 if ops[k]["eng"] == "s" else 0.0)) for j, w in dl[k]])
+        for j, lag in pre[k]:
+            suc[j].append((k, lag))
+            rsuc[k].append((j, lag + ops[k]["cost"] - ops[j]["cost"]))
+    tail = [0.0] * n
+    for k in range(n - 1, -1, -1):
+        tail[k] = max([ops[k]["cost"] + ops[k]["lat"]] + [tail[s] + lag for s, lag in suc[k]])
+
+    def weigh(st):
+        order = sorted(range(n), key=lambda k: (st[k], k))
+        return sum(replay(ops, dl, order, k, w, x) for k, w, x in VIEWS), order
+    best = justify(ops, suc, rsuc, [(-tail[k], k) for k in range(n)])
+    score, order = weigh(best)
     seed = 12345
     for it in range(TRIES):
-        pr = list(base)
-        for r in range(3):
+        key = list(best)
+        seed = (seed * 1103515245 + 12345) % 2147483648
+        lo = (seed >> 8) % 1000 / 1000.0 * max(best)
+        seed = (seed * 1103515245 + 12345) % 2147483648
+        amp = SHAKE * ((seed >> 8) % 1000 / 1000.0) ** 2
+        for k in range(n):
+            if lo <= best[k] < lo + SPAN:
+                seed = (seed * 1103515245 + 12345) % 2147483648
+                key[k] += amp * ((seed >> 8) % 2001 - 1000) / 1000.0
+        for k in range(n):
+            for j, lag in pre[k]:
+                if key[j] > key[k]:
+                    key[k] = key[j]
+        near = [k for k in range(n) if "alt" in ops[k] and lo <= best[k] < lo + SPAN]
+        flip = []
+        for r in range(it % 3 if near else 0):
             seed = (seed * 1103515245 + 12345) % 2147483648
-            lo = (seed >> 8) % n
-            seed = (seed * 1103515245 + 12345) % 2147483648
-            w = 1 + (seed >> 8) % 12
-            seed = (seed * 1103515245 + 12345) % 2147483648
-            dv = ((seed >> 8) % 2001 - 1000) / 1000.0
-            for k in range(lo, min(n, lo + w)):
-                pr[k] += 6.0 * dv * dv * dv
-        got = place(ops, deps, succ, pr)
-        sc = sum(replay(ops, dl, got[0], k, w, x) for k, w, x in VIEWS)
+            flip.append(near[(seed >> 8) % len(near)])
+            swap(ops[flip[-1]])
+        got = justify(ops, suc, rsuc, [(key[k], k) for k in range(n)])
+        sc, od = weigh(got)
         if sc <= score:
-            best, base, score = got, pr, sc
-    return best[0], deps, best[1], best[2]
+            best, score, order = got, sc, od
+        else:
+            for k in flip:
+                swap(ops[k])
+    return order, deps, best, [best[k] + ops[k]["cost"] + ops[k]["lat"] for k in range(n)], [o["eng"] for o in ops]
 
 
 def rank_program(g, core, T, topo):
@@ -628,7 +656,10 @@ def rank_program(g, core, T, topo):
     ops = build(g, T, topo.addr(nxt), topo.mask(core, nxt), neng)
     if "plan" not in PLAN:
         PLAN["plan"] = schedule(ops)
-    order, deps, start, done = PLAN["plan"]
+    order, deps, start, done, engs = PLAN["plan"]
+    for o, e in zip(ops, engs):
+        if o["eng"] != e:
+            swap(o)
     queue = {"v": g.vector, "a": g.scalar, "p": g.tensor, "g": g, "s": g.sync}
     total, mark, clock = {}, {}, {}
     known = {e: {} for e in queue}

@@ -7,17 +7,18 @@ for _t in range(ST):
     NB.append(NB[-1] + 16 + CW[_t] + 4096)
 MAGIC = 12582912.0
 MAGIC16 = 201326592.0
-HOW = ("sfss", "sfss", "sfss")
+HOW = ("sfff", "sfff", "sfff")
 XV = ("avav", "avav", "avav")
 PMV = (1, 1, 1)
 STAGES = ((0, 64), (64, 64))
 PARTS = (2, 1, 1)
-CH = ("sfff", "ssff", "ssff")
+CH = ("sfff", "sfff", "sfff")
 LG = ("cccg", "cccg", "cccg")
 LASTPN = 1
+SL, SH = (1, 1, 1), (1, 1, 1)
 SPLIT = 2
-WAKE, TRIES, SHAKE, SPAN = 0.14, 5000, 2.0, 6.0
-VIEWS = (((1.0, 1.0, 1.0, 1.0), 0.14, 0.0), ((0.88, 0.88, 0.74, 1.1), 0.2, 0.5), ((1.16, 1.2, 1.45, 1.16), 0.15, 0.4), ((0.9, 0.9, 0.8, 0.9), 0.3, 0.4))
+WAKE, TRIES, SHAKE, SPAN = 0.2, 5000, 2.0, 6.0
+VIEWS = (((1.0, 1.0, 1.0, 1.0), 0.2, 0.0), ((1.14, 1.2, 1.5, 1.14), 0.15, 0.6), ((0.92, 0.85, 0.7, 1.1), 0.25, 0.0), ((1.3, 1.5, 2.0, 1.3), 0.2, 1.5))
 NDMA = 8
 
 SCRATCH = {
@@ -45,8 +46,9 @@ SEMAPHORES = (["cv", "ca", "cp", "cg", "sent"] + ["d%d" % k for k in range(NDMA)
 
 A = AluOpType
 ACT = ActivationFunctionType
-CY = 0.83e-3 * 1.25
-PC = 0.42e-3 * 1.25
+CY = 0.83e-3 * 1.1
+PC = 0.42e-3 * 1.1
+GA, SC = 1.3 * 0.83e-3, 2.5 * 0.83e-3
 WIDE2 = ("G", "TB", "HI", "LO", "WB", "U")
 REC = ("G", 0, V + H, 1)
 PLAN = {}
@@ -132,7 +134,7 @@ def build(g, T, nxt_addr, nxt_mask, neng):
         return R(win).indirect(R(off))
 
     def agat(o, win, off, rd=None):
-        k = op("a", lambda: g.scalar.activation(R(o), IND(win, off), ACT.Copy), (rd or [win]) + [off], [o], 0.065 + 1.6 * 0.83e-3 * o[2])
+        k = op("a", lambda: g.scalar.activation(R(o), IND(win, off), ACT.Copy), (rd or [win]) + [off], [o], 0.065 + GA * o[2])
         ops[k]["alt"] = lambda: g.vector.tensor_copy(R(o), IND(win, off))
         return o
 
@@ -142,12 +144,12 @@ def build(g, T, nxt_addr, nxt_mask, neng):
         return o
 
     def fused(o, win, off, b, alu):
-        op("v", lambda: g.vector.tensor_tensor(R(o), IND(win, off), R(b), alu), [win, off, b], [o], 0.05 + 1.6 * 0.83e-3 * o[2])
+        op("v", lambda: g.vector.tensor_tensor(R(o), IND(win, off), R(b), alu), [win, off, b], [o], 0.05 + GA * o[2])
         return o
 
     def scat(off, src, add=None):
         n = H // SPLIT
-        c = 0.05 + 3.8 * 0.83e-3 * n
+        c = 0.05 + SC * n
         for k in range(SPLIT):
             o2, s2 = sub(off, k * n // 16, n // 16), sub(src, k * n, n)
             if add is None:
@@ -186,12 +188,12 @@ def build(g, T, nxt_addr, nxt_mask, neng):
         name = "d%d" % fill["d"]
         fill["d"] += 1
         e = g.sync if q == "s" else g.scalar
-        return op(q, lambda: e.dma_start(out, in_), rd, wr, 0.06, lat=1.8 + nbytes / 180e3, sem=(name, 16), after=after)
+        return op(q, lambda: e.dma_start(out, in_), rd, wr, 0.06, lat=1.2 + nbytes / 300e3, sem=(name, 16), after=after)
 
     def send(dst, src, sem, nbytes):
         k = op("g", lambda: g.remote_dma(R(dst), R(src), T.sem[sem], T.sem.sent, nxt_addr[1], nxt_addr[0], nxt_mask),
                [src], [], 0.4, sem=("", 0))
-        op("x", None, [], [dst], 0.0, lat=2.2 + nbytes / 60e3, sem=(sem, neng), after=[k])
+        op("x", None, [], [dst], 0.0, lat=1.6 + nbytes / 70e3, sem=(sem, neng), after=[k])
 
     dma("a", T.RT[:], T.rt[:], [], [("RT", 0, 160, 1)], 80e3)
     big = dma("s", T.G[:, 0:V], T.rec[:], [], [("G", 0, V, 1)], 1050e3)
@@ -220,6 +222,7 @@ def build(g, T, nxt_addr, nxt_mask, neng):
         s = f(2 * n)
         op("v", lambda: g.vector.tensor_tensor_scan(R(s), R(sub(RS, 0, 2 * n)), R(o), 0.0, A.add, A.max), [RS, o], [s], CY * 64)
         return sub(s, 1, n, 2)
+    E16 = {False: summing(1.0 / 32, False), True: summing(1.0 / 64, False)} if any(SL + SH) else None
     EB = {False: summing(1.0 / 32), True: summing(1.0 / 64)}
     ID = iota(new("WB", 128), [[0, 128]], 1, 0)
     asel(ID, [[-1, 128]], A.is_equal, 0.0, 0, 1)
@@ -288,8 +291,17 @@ def build(g, T, nxt_addr, nxt_mask, neng):
     dma("s", T.TB[0:128:4, :], T.HI[:], [hi], [TBW[0]], 260e3)
     dma("s", T.TB[1:128:4, :], T.LO[:], [lo], [TBW[1]], 260e3)
 
-    def count(bank, cmpt, signed, p, w, th, c0=0):
+    def count(bank, cmpt, signed, p, w, th, c0=0, wide=0, lk=None):
         n = p[2]
+        if wide:
+            o = (bank, 0, n, 1)
+            mm(o, [(ID, sub(C32, c0, n)), (I((-0.5 if signed else -8.5) / 32 + (9.0 / 32 if lk else 0.0)), sub(ONE, 0, n))]
+               + ([(I(-9.0 / 32), lk)] if lk else []), True, False)
+            mm(o, [(sub(E16[signed], 16 - r, 128), sub(cmpt, r, n, 16)) for r in range(16)], False, True)
+            if p[0] == "U":
+                ts(p, o, PQ, A.add)
+            tt(w, o, sub(C32, c0, n), A.is_gt)
+            return o
         o = wrap(bank, EB[signed], cmpt, n, [(ID, sub(C64, 2 * c0, 2 * n)), (ID, sub(OUTS[signed], 0, 2 * n))])
         if p[0] == "U":
             ts(p, o, PQ, A.add)
@@ -326,7 +338,7 @@ def build(g, T, nxt_addr, nxt_mask, neng):
                 d = mm((("ps5", "ps2")[k], 0, n, 1), [(IDN, ak), (ID, sub(C[o], 2 * n * k, n, 2))], True, True)
                 act(ck, d, ACT.Sign, bias=-0.5)
             c0, cn = n // 16 * k, n // 16
-            count(("ps1", "ps0")[k], ck, signed, sub(p2, c0, cn), sub(w, c0, cn), sub(C32, c0, cn), c0)
+            count(("ps1", "ps0")[k], ck, signed, sub(p2, c0, cn), sub(w, c0, cn), sub(C32, c0, cn), c0, SH[t])
         u = tt(f(), w, sub(AC, 32 * o, 32), A.mult)
         old = st["cur"]
         st["cur"] = tt(f(), u, old, A.max)
@@ -390,7 +402,7 @@ def build(g, T, nxt_addr, nxt_mask, neng):
         j2 = ts(new("IP", 4), j1, 4, A.arith_shift_right, 31, A.bitwise_and)
         off = sub(cp(new("U", 4), j2), 0, 3)
         if PMV[t]:
-            PM = ts(f(256), J, tt(f(1), sb, f16, A.subtract), A.is_equal)
+            PM = ts(f(256), J, f16, A.add, sb, A.is_equal)
         else:
             PM = act(f(256), act(f(256), J, ACT.Abs, bias=tt(f(1), f16, sb, A.subtract)), ACT.Relu, bias=1.0, scale=-1.0)
         rw = f(128)
@@ -432,7 +444,8 @@ def build(g, T, nxt_addr, nxt_mask, neng):
                 tt(sub(ACk, lo, n), tk, sub(ACa, lo, n), A.min)
                 nd = mm(vp(352, n), [(ID, DC), (ID, DR), (I(-8192.0), lk1)], True, True)
                 tt(sub(xd, lo, n), nd, sub(xi, lo, n), A.max)
-                mm(vp(160 + lo, n), [(ID, C32M), (I(4096.0), lk1)], True, True)
+                if not SL[t]:
+                    mm(vp(160 + lo, n), [(ID, C32M), (I(4096.0), lk1)], True, True)
             if not last:
                 pre = [(ID, sub(HY, lo, n)), (ID, sub(LY, lo, n))] if lo < 128 else [(I(2.0), LR)]
                 t2 = mm(("ps7", 0, n, 1), pre + [(I(16384.0), lk0), (I(-16384.0), lk1)], True, True)
@@ -473,7 +486,7 @@ def build(g, T, nxt_addr, nxt_mask, neng):
                 dd = mm(("ps6", 0, H, 1), [(ID, X[o]), (IDN, Y[o])], True, True)
                 cm = act(new("WB", H), dd, ACT.Sign, bias=-0.5)
             p, w = new("U", 32) if o < 3 or (last and LASTPN) else f(), f()
-            sc = count("ps0", cm, how == "s", p, w, vp(160 + 32 * o, 32))
+            sc = count("ps0", cm, how == "s", p, w, vp(160 + 32 * o, 32), 0, SL[t], sub(LK, 32 * o + 32, 32))
             if o == 3 and not last:
                 cp(sub(a16, 128, 32), tt(f(), t1, tt(f(), sc, r2, A.add), A.max))
             q16.append(cp(new("U", 32), tt(f(), CQ, sc, A.subtract)) if LG[t][o] == "g" and not (last and o == 3 and LASTPN) else None)
@@ -564,7 +577,7 @@ def replay(ops, dl, order, k, wake, far):
         e = o["eng"]
         t = free[e]
         for j, w in dl[c]:
-            x = done[j] + wake if w else (done[j] - 1.8 if e == "s" else fr[j])
+            x = done[j] + wake if w else (done[j] - 1.2 if e == "s" else fr[j])
             if x > t:
                 t = x
         fr[c] = t + k[o["kind"]] * o["cost"]
@@ -603,7 +616,7 @@ def schedule(ops):
     dl, pre, suc, rsuc = [], [], [[] for _ in range(n)], [[] for _ in range(n)]
     for k in range(n):
         dl.append([(j, w) for j, w in deps[k].items() if not (w and any(deps[i].get(j) for i in deps[k] if i > j))])
-        pre.append([(j, ops[j]["cost"] + (ops[j]["lat"] + WAKE if w else ops[j]["lat"] - 1.8 if ops[k]["eng"] == "s" else 0.0)) for j, w in dl[k]])
+        pre.append([(j, ops[j]["cost"] + (ops[j]["lat"] + WAKE if w else ops[j]["lat"] - 1.2 if ops[k]["eng"] == "s" else 0.0)) for j, w in dl[k]])
         for j, lag in pre[k]:
             suc[j].append((k, lag))
             rsuc[k].append((j, lag + ops[k]["cost"] - ops[j]["cost"]))

@@ -1,24 +1,21 @@
 from concourse.mybir import AluOpType, ActivationFunctionType
 
 V, H, ST = 4096, 512, 3
-CW = [4096, 4096, 4096]
-NB = [V + H]
-for _t in range(ST):
-    NB.append(NB[-1] + 16 + CW[_t] + 4096)
+CW = 4096
+NB = [V + H + (16 + CW + 4096) * _t for _t in range(ST + 1)]
 MAGIC = 12582912.0
 MAGIC16 = 201326592.0
-HOW = ("sfff", "sfff", "sfff")
-XV = ("avav", "avav", "avav")
-PMV = (1, 1, 1)
-STAGES = ((0, 64), (64, 64))
 PARTS = (2, 1, 1)
-CH = ("sfff", "sfff", "sfff")
-LG = ("cccg", "cccg", "cccg")
-LASTPN = 1
-SL, SH = (1, 1, 1), (1, 1, 1)
+LG = ("cccg", "cccg", "ccpn")
+PAIR = ((0, 2), (0, 2), ())
+STAGES = ((0, 64), (64, 64))
 SPLIT = 2
-WAKE, TRIES, SHAKE, SPAN = 0.2, 5000, 2.0, 6.0
-VIEWS = (((1.0, 1.0, 1.0, 1.0), 0.2, 0.0), ((1.14, 1.2, 1.5, 1.14), 0.15, 0.6), ((0.92, 0.85, 0.7, 1.1), 0.25, 0.0), ((1.3, 1.5, 2.0, 1.3), 0.2, 1.5))
+HELD = 2
+WAKE, TRIES, SHAKE, SPAN, MOVES, MORE, COOL, SEEDS = 0.2, 500, 2.0, 6.0, 7000, 30000, 1.0, (3,)
+LAST = 22000
+VIEWS = (((1.0, 1.0, 1.0, 1.0), 0.2, 0.0), ((1.14, 1.2, 1.5, 1.14), 0.25, 0.8), ((1.25, 1.0, 1.0, 1.25), 0.2, 1.5),
+         ((1.0, 1.4, 2.0, 1.0), 0.2, 0.8), ((1.0, 1.0, 1.0, 1.0), 0.22, 0.4))
+FAR = (((1.25, 1.45, 2.2, 1.25), 0.2, 6.0), ((1.1, 1.0, 1.0, 1.1), 0.2, 3.5))
 NDMA = 8
 
 SCRATCH = {
@@ -31,14 +28,14 @@ SCRATCH = {
     "YR": ("sbuf", [128, 160], "float32"),
     "WB": ("sbuf", [128, 36864], "bfloat16"),
     "F": ("sbuf", [128, 14336], "float32"),
-    "IP": ("sbuf", [128, 2048], "int32"),
+    "IP": ("sbuf", [128, 3072], "int32"),
     "U": ("sbuf", [128, 3072], "uint16"),
 }
 for _t in range(ST):
     SCRATCH["Z%d" % _t] = ("sbuf", [128, H], "bfloat16")
     SCRATCH["W%d" % _t] = ("sbuf", [128, H], "bfloat16")
-    SCRATCH["ZT%d" % _t] = ("sbuf", [128, 16], "bfloat16")
-    SCRATCH["WT%d" % _t] = ("sbuf", [128, 16], "bfloat16")
+    SCRATCH["ZT%d" % _t] = ("sbuf", [128, 8], "float32")
+    SCRATCH["WT%d" % _t] = ("sbuf", [128, 8], "float32")
 for _b in range(8):
     SCRATCH["ps%d" % _b] = ("psum", [128, 512], "float32")
 SEMAPHORES = (["cv", "ca", "cp", "cg", "sent"] + ["d%d" % k for k in range(NDMA)]
@@ -49,7 +46,7 @@ ACT = ActivationFunctionType
 CY = 0.83e-3 * 1.1
 PC = 0.42e-3 * 1.1
 GA, SC = 1.3 * 0.83e-3, 2.5 * 0.83e-3
-WIDE2 = ("G", "TB", "HI", "LO", "WB", "U")
+WIDE2 = ("G", "TB", "HI", "LO", "WB", "U", "Z0", "Z1", "Z2", "W0", "W1", "W2")
 REC = ("G", 0, V + H, 1)
 PLAN = {}
 
@@ -67,7 +64,7 @@ def meet(a, b):
 
 
 def two(a):
-    return a[0] in WIDE2 or a[0][0] in "ZW"
+    return a[0] in WIDE2
 
 
 def swap(o):
@@ -75,7 +72,7 @@ def swap(o):
 
 
 def build(g, T, nxt_addr, nxt_mask, neng):
-    ops = []
+    ops, held, made = [], {}, {}
     fill = {"WB": 0, "F": 0, "IP": 0, "U": 0, "d": 0}
 
     def R(a):
@@ -130,6 +127,11 @@ def build(g, T, nxt_addr, nxt_mask, neng):
         op("a", lambda: g.scalar.activation(R(o), R(i), fn, bias=S(bias), scale=S(scale)), aps(i, bias, scale), [o], CY * max(64, o[2]))
         return o
 
+    def aff(o, i, scale, bias=0.0):
+        act(o, i, ACT.Identity, bias, scale)
+        ops[-1]["alt"] = lambda: g.vector.tensor_scalar(R(o), R(i), S(scale), S(bias), A.mult, A.add)
+        return o
+
     def IND(win, off):
         return R(win).indirect(R(off))
 
@@ -147,7 +149,10 @@ def build(g, T, nxt_addr, nxt_mask, neng):
         op("v", lambda: g.vector.tensor_tensor(R(o), IND(win, off), R(b), alu), [win, off, b], [o], 0.05 + GA * o[2])
         return o
 
-    def scat(off, src, add=None):
+    def scat(off, src, add=None, tag=None):
+        if tag is not None and tag[1] >= HELD and tag[0] < ST - 1 and tag not in held:
+            held[tag] = (off, src, add, tag)
+            return
         n = H // SPLIT
         c = 0.05 + SC * n
         for k in range(SPLIT):
@@ -157,8 +162,9 @@ def build(g, T, nxt_addr, nxt_mask, neng):
             else:
                 a2 = sub(add, k * n, n)
                 op("v", lambda o2=o2, s2=s2, a2=a2: g.vector.tensor_tensor(IND(REC, o2), R(s2), R(a2), A.add), [o2, s2, a2], [REC], c)
+            made.setdefault(tag, []).append(len(ops) - 1)
 
-    def mm(o, terms, start, stop):
+    def mm(o, terms, start=True, stop=True):
         if len(terms) > 1 and o[2] >= 256:
             for k, x in enumerate(terms):
                 mm(o, [x], start and k == 0, stop and k == len(terms) - 1)
@@ -200,29 +206,16 @@ def build(g, T, nxt_addr, nxt_mask, neng):
     dma("s", T.CHI[:], T.ch[:], [], [("CHI", 0, 1024, 1)], 520e3, after=[big])
     pi = iota(new("IP", 1), [[0, 1]], 0, 1)
     ri = ts(new("IP", 1), pi, 15, A.bitwise_and)
-    RF = cp(f(1), ri)
     RF2 = ts(f(1), ri, 2.0, A.mult)
-    RF16 = ts(f(1), ri, 16.0, A.mult, 7.5, A.add)
-    PQ = ts(f(1), ri, 2.0, A.mult, 0.5, A.add)
+    PQ = aff(f(1), RF2, 1.0, 0.5)
     E8 = iota(f(8), [[0, 8]], 1, 0)
     asel(E8, [[-16, 8]], A.is_ge, 0.0, 0, 1)
     asel(E8, [[16, 8]], A.is_ge, 0.0, 15, -1)
 
-    def summing(scale, twice=True):
+    def summing(scale):
         k = mset(new("WB", 144), 0.0)
-        ts(sub(k, 16, 8, 16), E8, scale, A.mult)
-        if twice:
-            ts(sub(k, 24, 8, 16), E8, scale, A.mult)
+        aff(sub(k, 16, 8, 16), E8, scale)
         return k
-
-    def wrap(bank, lhs, tile, n, pre):
-        o = (bank, 0, 2 * n, 1)
-        mm(o, pre, True, False)
-        mm(o, [(sub(lhs, 16 - r, 128), sub(tile, r, 2 * n, 8)) for r in range(8)], False, True)
-        s = f(2 * n)
-        op("v", lambda: g.vector.tensor_tensor_scan(R(s), R(sub(RS, 0, 2 * n)), R(o), 0.0, A.add, A.max), [RS, o], [s], CY * 64)
-        return sub(s, 1, n, 2)
-    E16 = {False: summing(1.0 / 32, False), True: summing(1.0 / 64, False)} if any(SL + SH) else None
     EB = {False: summing(1.0 / 32), True: summing(1.0 / 64)}
     ID = iota(new("WB", 128), [[0, 128]], 1, 0)
     asel(ID, [[-1, 128]], A.is_equal, 0.0, 0, 1)
@@ -230,125 +223,126 @@ def build(g, T, nxt_addr, nxt_mask, neng):
 
     def I(x):
         if x not in ids:
-            ids[x] = ts(new("WB", 128), ID, x, A.mult)
+            ids[x] = aff(new("WB", 128), ID, x)
         return ids[x]
     IDN = I(-1.0)
     C32 = iota(new("WB", 32), [[32, 32]], 0, 0)
-    C64 = iota(new("WB", 64), [[32, 32], [0, 2]], 0, 0)
-    RS = mset(f(64), 0.0)
-    mset(sub(RS, 0, 32, 2), -2.0 ** 50)
     ONE = mset(new("WB", 160), 1.0)
-    OUT = new("WB", 64)
-    ts(sub(OUT, 0, 32, 2), sub(ONE, 0, 32), ts(f(1), ri, 7.5, A.is_gt), A.mult)
-    ts(sub(OUT, 1, 32, 2), sub(ONE, 0, 32), ts(f(1), ri, 7.5, A.is_lt), A.mult)
-    OUTS = {False: ts(new("WB", 64), OUT, -4096.0, A.mult, -8.5 / 32, A.add), True: ts(new("WB", 64), OUT, -4096.0, A.mult, -0.5 / 32, A.add)}
-    CQ = ts(f(), C32, 2.0, A.mult, PQ, A.add)
-    C32M = iota(new("WB", 64), [[0, 2], [32, 32]], -4096, 0)
+    CQ = aff(f(), C32, 2.0, PQ)
     DC = iota(new("WB", 64), [[0, 2], [1, 32]], 0, 0)
-    DR = ts(new("WB", 64), sub(ONE, 0, 64), ts(f(1), ri, 32.0, A.mult, 4096.0, A.add), A.mult)
+    DR = aff(new("WB", 64), sub(ONE, 0, 64), aff(f(1), RF2, 16.0, 4096.0))
     mset(("G", V, H, 1), 0.0)
     for t in range(ST):
-        mset(("G", NB[t], 16, 1), 256.0)
+        aff(("G", NB[t], 16, 1), sub(ONE, 0, 16), 256.0)
+        aff(("ZT%d" % t, 0, 8, 1), sub(ONE, 0, 8), 1.0)
     KO = iota(new("WB", 256), [[1, 8], [0, 32]], 1, 0)
-    LR = ts(new("WB", 32), sub(ONE, 0, 32), RF, A.mult)
-    KE = []
-    for o in range(4):
-        m1 = ts(f(1), ri, 4 * o + 0.5, A.subtract)
-        KE.append(summing(ts(f(1), tt(f(1), m1, m1, A.mult), 0.5, A.is_lt), False))
+    KE = [summing(act(f(1), act(f(1), RF2, ACT.Abs, bias=-8.0 * o - 1), ACT.Relu, bias=1.5, scale=-0.5)) for o in range(4)]
     BD = iota(new("WB", 128), [[0, 128]], 1, 0)
     asel(BD, [[-16, 8], [0, 16]], A.is_ge, 0.0, 0, 1)
     asel(BD, [[16, 8], [0, 16]], A.is_ge, 0.0, 15, -1)
-    J = iota(f(256), [[16, 2], [-16, 8], [-1, 16]], 0, 1)
-    asel(J, [[0, 2], [-16, 8], [0, 16]], A.is_ge, 999.0, 0, 1)
-    asel(J, [[0, 2], [16, 8], [0, 16]], A.is_ge, 999.0, 15, -1)
-    ts(J, J, 7.5, A.subtract)
-    J16 = ts(f(4), iota(f(4), [[256, 4]], 0, 0), RF16, A.add)
+    BDN = aff(new("WB", 128), BD, -1.0)
+    TT = iota(f(512), [[0, 512]], 1, 0)
+    asel(TT, [[16, 2], [-16, 8], [-1, 32]], A.is_equal, 0.0, 0, 1)
+    asel(TT, [[0, 2], [-16, 8], [0, 32]], A.is_ge, 0.0, 0, 1)
+    asel(TT, [[0, 2], [16, 8], [0, 32]], A.is_ge, 0.0, 15, -1)
+    JC = aff(f(16), iota(f(16), [[32, 16]], 0, 0), 1.0, aff(f(1), RF2, 0.5, 7.5))
+    J16 = aff(f(4), iota(f(4), [[256, 4]], 0, 0), 1.0, aff(f(1), RF2, 8.0, 7.5))
     NH = mset(new("WB", H), -0.5)
-    M75 = mset(new("WB", 2), -7.5)
-    IF8 = ts(f(128), ID, -8192.0, A.mult)
-    HA0, LA0, HY, LY = new("WB", 160), new("WB", 160), new("WB", 160), new("WB", 160)
-    iota(sub(HA0, 0, 32), [[32, 32]], 0, 0)
-    iota(sub(HA0, 32, 128), [[1024, 4], [32, 32]], 0, 0)
-    iota(sub(HY, 0, 128), [[1024, 4], [32, 32]], 0, 0)
-    ts(sub(LA0, 0, 32), sub(ONE, 0, 32), RF2, A.mult, 16.0, A.add)
-    ts(sub(LA0, 32, 128), sub(ONE, 0, 128), RF2, A.mult, 17.0, A.add)
-    ts(sub(LY, 0, 128), sub(ONE, 0, 128), RF2, A.mult, 17.0, A.add)
-    HA, LA = [HA0] * ST, [LA0] * ST
-    APA = [act(f(128), mm(("ps7", 0, 128, 1), [(ID, sub(HA[t], 0, 128)), (ID, sub(LA[t], 0, 128))], True, True), ACT.Identity,
-               bias=float(NB[t])) for t in range(ST)]
+    M75 = aff(new("WB", 2), sub(ONE, 0, 2), -7.5)
+    M85 = aff(new("WB", 2), sub(ONE, 0, 2), -8.5)
+    IF8 = aff(f(128), ID, -8192.0)
+    HA, LA, HB, LY = new("WB", 128), new("WB", 160), new("WB", 160), new("WB", 160)
+    iota(sub(HA, 0, 32), [[32, 32]], 0, 0)
+    iota(sub(HA, 32, 96), [[1024, 3], [32, 32]], 0, 0)
+    iota(sub(HB, 0, 32), [[32, 32]], 0, 0)
+    iota(sub(HB, 32, 128), [[1024, 4], [0, 32]], 0, 0)
+    aff(sub(LA, 0, 32), sub(ONE, 0, 32), RF2, 16.0)
+    aff(sub(LA, 32, 128), sub(ONE, 0, 128), RF2, 17.0)
+    aff(sub(LY, 0, 32), sub(ONE, 0, 32), RF2, 17.0)
+    aff(sub(LY, 32, 128), sub(ONE, 0, 128), RF2, 16.5)
+    ap = mm(("ps7", 0, 128, 1), [(ID, HA), (ID, sub(LA, 0, 128))])
+    APA = [act(f(128), ap, ACT.Identity, bias=float(NB[t])) for t in range(ST)]
     LKS = [new("WB", 192) for t in range(ST)]
     SGS = [new("WB", 192) for t in range(ST)]
     for t in range(ST):
-        mset(sub(LKS[t], 0, 32), 1.0)
-        mset(sub(SGS[t], 0, 32), 1.0)
-        mset(sub(SGS[t], 160, 32), -1.0)
+        aff(sub(LKS[t], 0, 32), sub(ONE, 0, 32), 1.0)
+        aff(sub(SGS[t], 0, 32), sub(ONE, 0, 32), 1.0)
+        aff(sub(SGS[t], 160, 32), sub(ONE, 0, 32), -1.0)
     hi, lo, chi = ("HI", 0, 1024, 1), ("LO", 0, 1024, 1), ("CHI", 0, 1024, 1)
     for k in range(4):
         h = cp(sub(hi, 256 * k, 256), sub(chi, 256 * k, 256))
-        tt(sub(lo, 256 * k, 256), mm(("ps%d" % (6, 4)[k % 2], 0, 256, 1), [(IDN, h)], True, True), sub(chi, 256 * k, 256), A.add)
+        tt(sub(lo, 256 * k, 256), mm(("ps%d" % (7, 4)[k % 2], 0, 256, 1), [(IDN, h)]), sub(chi, 256 * k, 256), A.add)
     TBW = [("TB0", 0, 1, 1), ("TB1", 0, 1, 1)]
     op("v", lambda: g.vector.memset(T.TB[:], 0.0), [], TBW, CY * V / 2)
     dma("s", T.TB[0:128:4, :], T.HI[:], [hi], [TBW[0]], 260e3)
     dma("s", T.TB[1:128:4, :], T.LO[:], [lo], [TBW[1]], 260e3)
 
-    def count(bank, cmpt, signed, p, w, th, c0=0, wide=0, lk=None):
-        n = p[2]
-        if wide:
-            o = (bank, 0, n, 1)
-            mm(o, [(ID, sub(C32, c0, n)), (I((-0.5 if signed else -8.5) / 32 + (9.0 / 32 if lk else 0.0)), sub(ONE, 0, n))]
-               + ([(I(-9.0 / 32), lk)] if lk else []), True, False)
-            mm(o, [(sub(E16[signed], 16 - r, 128), sub(cmpt, r, n, 16)) for r in range(16)], False, True)
-            if p[0] == "U":
-                ts(p, o, PQ, A.add)
-            tt(w, o, sub(C32, c0, n), A.is_gt)
-            return o
-        o = wrap(bank, EB[signed], cmpt, n, [(ID, sub(C64, 2 * c0, 2 * n)), (ID, sub(OUTS[signed], 0, 2 * n))])
-        if p[0] == "U":
+    def count(bank, cmpt, signed, p, w, c0=0, lk=None):
+        n = w[2]
+        o = (bank, 0, n, 1)
+        mm(o, [(ID, sub(C32, c0, n)), (I((-0.5 if signed else -8.5) / 32 + (9.0 / 32 if lk else 0.0)), sub(ONE, 0, n))]
+           + ([(I(-9.0 / 32), lk)] if lk else []), True, False)
+        mm(o, [(sub(EB[signed], 16 - r, 128), sub(cmpt, r, n, 16)) for r in range(16)], False, True)
+        if p:
             ts(p, o, PQ, A.add)
-        tt(w, o, th, A.is_gt)
+        tt(w, o, sub(C32, c0, n), A.is_gt)
         return o
 
     def rotate(out, win, off, PM):
         rg = agat(f(48), win, off)
-        return mm(out, [(sub(PM, 0, 128), sub(rg, 0, 32)), (sub(PM, 128, 128), sub(rg, 1, 32))], True, True)
+        return mm(out, [(sub(PM, 0, 128), sub(rg, 0, 32)), (sub(PM, 128, 128), sub(rg, 1, 32))])
 
     def regions(t):
-        p0 = NB[t] + 16 + CW[t]
+        p0 = NB[t] + 16 + CW
         P = [("G", p0 + 1024 * o, 1024, 1) for o in range(4)]
         X = [sub(p, 0, H, 2) for p in P]
         Y = [sub(p, 1, H, 2) for p in P]
         AA = [("G", NB[t] + 16, H, 2)] + [("G", NB[t] + 17 + 1024 * o, H, 2) for o in range(4)]
         return NB[t], P, X, Y, AA
 
-    def champion_level(t, o, st, AC):
+    def champion_level(t, o, st, AC, src=None):
         nb, P, X, Y, AA = regions(t)
         C = [None] + [("G", nb + 16 + 1024 * k, 1024, 1) for k in range(4)]
         p2, w, cm = new("U", 32), f(), new("WB", H)
         parts = PARTS[t]
         n = H // parts
+        if o == 4:
+            zc = vgat(new("WB", 16), sub(C[3], 0, 32), sub(st["p16"], 0, 1))
+            r4, s3 = sub(AA[4], 0, 1), ("ps6", 0, 3, 1)
+            c0 = tt(new("WB", 1), sub(zc, 0, 1), r4, A.is_gt)
+            mm(sub(s3, 1, 1), [(ID, sub(M75, 0, 1)), (BD, sub(zc, 0, 1))])
+            mm(sub(s3, 2, 1), [(BD, r4), (BDN, sub(zc, 0, 1))])
+            mm(sub(s3, 0, 1), [(ID, sub(M85, 0, 1)), (BD, c0)])
+            ZT = ("ZT%d" % t, 0, 8, 1)
+            ts(sub(ZT, 0, 1), ts(f(1), sub(s3, 0, 1), 0.0, A.is_gt, sub(s3, 2, 1), A.mult), sub(s3, 1, 1), A.add)
+            send(("WT%d" % t, 0, 8, 1), ZT, "at%d" % t, 30e3)
         for k in range(parts):
             ck, ak = sub(cm, n * k, n), sub(AA[o], n * k, n)
-            signed = CH[t][o - 1] == "s"
+            signed = o == 1 and t == 0
             if o > 1:
                 wk, pk = sub(C[o - 1], 0, 2 * n * (k + 1)), sub(st["p16"], n // 16 * k, n // 16)
-                if not signed:
-                    fused(ck, wk, pk, ak, A.is_gt)
+                fused(ck, wk, pk, ak, A.is_gt)
                 agat(sub(C[o], 2 * n * k, n, 2), wk, pk)
-            if signed:
-                d = mm((("ps5", "ps2")[k], 0, n, 1), [(IDN, ak), (ID, sub(C[o], 2 * n * k, n, 2))], True, True)
+            elif signed:
+                d = mm((("ps5", "ps2")[k], 0, n, 1), [(IDN, ak), (ID, sub(C[o], 2 * n * k, n, 2))])
                 act(ck, d, ACT.Sign, bias=-0.5)
+            else:
+                fused(ck, src[0], src[1], AA[0], A.is_lt)
             c0, cn = n // 16 * k, n // 16
-            count(("ps1", "ps0")[k], ck, signed, sub(p2, c0, cn), sub(w, c0, cn), sub(C32, c0, cn), c0, SH[t])
+            count(("ps1", "ps0")[k], ck, signed, sub(p2, c0, cn), sub(w, c0, cn), c0)
         u = tt(f(), w, sub(AC, 32 * o, 32), A.mult)
         old = st["cur"]
-        st["cur"] = tt(f(), u, old, A.max)
+        st["cur"] = tt(new("IP", 32) if o == 3 else f(), u, old, A.max)
         if o == 4:
-            st["curi"] = tt(new("IP", 32), u, old, A.max)
+            m3 = ts(new("IP", 32), old, 4095, A.bitwise_and)
+            d = tt(f(), aff(f(), sub(AC, 128, 32), 1.0, -20480.0), m3, A.subtract)
+            st["ky"] = f(160)
+            st["m"] = tt(sub(st["ky"], 0, 32), tt(f(), w, d, A.mult), m3, A.add)
         st["p16"], st["win"] = p2, C[o]
 
     rt = ("RT", 0, 160, 1)
     r16 = cp(new("U", 160), tt(f(160), ts(vp(0, 160), rt, 0.5, A.is_lt, float(NB[0]), A.mult), rt, A.add))
-    AC = tt(f(160), mm(vp(160, 160), [(I(4096.0), sub(KO, 0, 160))], True, True), rt, A.add)
+    AC = tt(f(160), mm(vp(160, 160), [(I(4096.0), sub(KO, 0, 160))]), rt, A.add)
     nb, P, X, Y, AA = regions(0)
     for o in range(5):
         for k in range(2):
@@ -362,98 +356,100 @@ def build(g, T, nxt_addr, nxt_mask, neng):
         nb, P, X, Y, AA = regions(t)
         last = t == ST - 1
         Z, W = ("Z%d" % t, 0, H, 1), ("W%d" % t, 0, H, 1)
-        ZT, WT = ("ZT%d" % t, 0, 16, 1), ("WT%d" % t, 0, 16, 1)
-        cur = st["cur"]
-        agat(ZT, sub(st["win"], 0, 32), sub(st["p16"], 0, 1))
-        send(WT, ZT, "at%d" % t, 30e3)
+        cur, m, ky, ls = st["cur"], st["m"], st["ky"], f(128)
         agat(Z, st["win"], st["p16"])
         send(W, Z, "aw%d" % t, 131e3)
-        ky, ls = f(160), f(128)
-        m = ts(new("IP", 32), st["curi"], 4095, A.bitwise_and)
         m16 = cp(new("U", 32), m)
         G1 = agat(new("WB", H), ("TB", 0, V, 1), m16, TBW)
         MB = ("ps1", 0, H, 1)
         mm(MB, [(I(0.5), NH), (I(0.5), Z)], True, False)
-        SG, LK = SGS[t], LKS[t]
-        for o in range(1, 5):
-            act(sub(SG, 32 * o, 32), cur, ACT.Sign, bias=-4096.0 * (o + 1))
-        Ta = mm(vp(288, 160), [(I(4096.0), sub(KO, 64, 160)), (I(-4096.0), sub(SG, 0, 160)), (I(4096.0), sub(SG, 32, 160))], True, True)
-        ACa = tt(new("IP", 160), Ta, AC, A.min)
-        xi = new("IP", 160)
-        ts(sub(xi, 128, 32), sub(ACa, 128, 32), 4095, A.bitwise_and)
 
         def found(e, ks):
             for o in range(e[2] // 32):
                 tt(sub(e, 32 * o, 32), sub(ks, 32 * o, 32), m, A.is_equal)
             return e
-        el = None
+        el = ef = None
         if t == 1:
-            el = tt(f(128), found(vp(0, 128), keys[0]), losers[0], A.mult)
+            el = ef = tt(f(128), found(vp(0, 128), keys[0]), losers[0], A.mult)
         if t == 2:
-            lb = tt(vp(128, 128), found(vp(0, 128), keys[0]), losers[0], A.mult)
-            lc = tt(f(96), found(vp(256, 96), sub(rotd, 0, 96)), sub(rotd, 96, 96), A.mult)
-            tt(sub(lb, 0, 96), sub(lb, 0, 96), lc, A.max)
-            ea = found(vp(0, 128), keys[1])
-            el = tt(f(128), lb, tt(f(128), ea, tt(f(128), losers[1], lb, A.subtract), A.mult), A.add)
-        sb = ("ps5", 0, 1, 1)
-        mm(sb, [(ID, sub(M75, 0, 1)), (BD, sub(WT, 0, 1))], True, True)
+            la = tt(f(128), found(vp(0, 128), keys[1]), aff(f(128), losers[1], 1.0, 8192.0), A.mult)
+            lb = tt(vp(128, 128), found(vp(128, 128), keys[0]), losers[0], A.mult)
+            lc = tt(vp(256, 96), found(vp(256, 96), sub(rotd, 0, 96)), sub(rotd, 96, 96), A.mult)
+            ef = tt(f(128), lb, la, A.max)
+            tt(sub(ef, 0, 96), lc, sub(ef, 0, 96), A.max)
+            el = ts(new("IP", 128), cp(new("IP", 128), ef), 8191, A.bitwise_and)
+        SG, LK = SGS[t], LKS[t]
+        for o in range(1, 5):
+            act(sub(SG, 32 * o, 32), cur, ACT.Sign, bias=-4096.0 * (o + 1))
+        Ta = mm(vp(288, 160), [(I(4096.0), sub(KO, 64, 160)), (I(-4096.0), sub(SG, 0, 160)), (I(4096.0), sub(SG, 32, 160))])
+        ACk, xi = new("IP", 160), new("IP", 160)
+        ACa = tt(f(128), sub(Ta, 0, 128), sub(AC, 0, 128), A.min)
+        tt(sub(ACk, 128, 32), sub(Ta, 128, 32), sub(AC, 128, 32), A.min)
+        ts(sub(xi, 128, 32), sub(ACk, 128, 32), 4095, A.bitwise_and)
+        sb = ("WT%d" % t, 0, 1, 1)
         j1 = ts(new("IP", 4), J16, sb, A.add)
         f16 = ts(f(1), sb, MAGIC16, A.add, MAGIC16, A.subtract)
         j2 = ts(new("IP", 4), j1, 4, A.arith_shift_right, 31, A.bitwise_and)
         off = sub(cp(new("U", 4), j2), 0, 3)
-        if PMV[t]:
-            PM = ts(f(256), J, f16, A.add, sb, A.is_equal)
-        else:
-            PM = act(f(256), act(f(256), J, ACT.Abs, bias=tt(f(1), f16, sb, A.subtract)), ACT.Relu, bias=1.0, scale=-1.0)
+        PM = agat(f(256), TT, ts(new("U", 16), JC, sb, A.add, f16, A.subtract))
         rw = f(128)
-        for o in range(4):
-            kd = (("ps6", "ps0")[o // 2], 32 * (o % 2), 32, 1)
-            pre = [(I(2.0 ** 26), sub(ONE, 0, 32)), (I(-2.0 ** 26), sub(SG, 32 * o + 32, 32))]
-            mm(kd, pre + ([(IF8, sub(el, 32 * o, 32))] if el else []) + [(sub(KE[o], 16 - r, 128), sub(G1, r, 32, 16)) for r in range(16)], True, True)
-            if o % 2 and el:
-                tt(sub(rw, 32 * o - 32, 64), (kd[0], 0, 64, 1), sub(el, 32 * o - 32, 64), A.max)
-            elif o % 2:
-                act(sub(rw, 32 * o - 32, 64), (kd[0], 0, 64, 1), ACT.Copy)
-        x16, xa, bp = new("U", 128), new("IP", 128), new("WB", 128)
-        US, ACk, xd, a16 = vp(0, 160), f(160), f(128), new("U", 160)
         for lo, n in STAGES:
-            rb = ("ps7", lo, n, 1)
+            kd = (("ps6", "ps0")[lo > 0], 0, n, 1)
+            for o in range(lo // 32, (lo + n) // 32):
+                pre = [(I(2.0 ** 26), sub(ONE, 0, 32)), (I(-2.0 ** 26), sub(SG, 32 * o + 32, 32))] + ([(IF8, sub(ef, 32 * o, 32))] if el else [])
+                if 32 * o == lo:
+                    mm(sub(kd, 0, 32), pre, True, False)
+                mm(sub(kd, 32 * o - lo, 32), (pre if 32 * o > lo else []) + [(sub(KE[o], 16 - r, 128), sub(G1, r, 32, 16)) for r in range(16)], 32 * o > lo)
+            if el:
+                tt(sub(rw, lo, n), kd, sub(el, lo, n), A.max)
+            else:
+                act(sub(rw, lo, n), kd, ACT.Copy)
+        x16, xa, bp = new("U", 128), new("IP", 128), new("WB", 128)
+        US, xd, a16, BA = vp(0, 160), f(128), new("U", 160), f(160)
+        for lo, n in STAGES:
+            rb = (("ps7", "ps6")[lo > 0], lo, n, 1)
             for o in range(lo // 32, (lo + n) // 32):
                 rotate(sub(rb, 32 * o - lo, 32), sub(rw, 32 * o, 32), off, PM)
-            cp(sub(x16, lo, n), tt(f(n), rb, sub(APA[t], lo, n), A.min))
+            xp = tt(f(n), rb, sub(APA[t], lo, n), A.min)
+            cp(sub(x16, lo, n), xp)
             tt(sub(xa, lo, n), rb, sub(ACa, lo, n), A.min)
-            act(sub(bp, lo, n), rb, ACT.Sign, bias=8192.0, scale=-1.0)
+            act(sub(bp, lo, n), xp, ACT.Sign, bias=4300.0, scale=-1.0)
             ts(sub(xi, lo, n), sub(xa, lo, n), 4095, A.bitwise_and)
             for o in range(lo // 32, (lo + n) // 32):
-                (vgat if XV[t][o] == "v" else agat)(X[o], ("G", 0, nb + 16 + CW[t], 1), sub(x16, 32 * o, 32))
+                if (t - 1, o) in held:
+                    scat(*held[t - 1, o])
+                (vgat if o % 2 else agat)(X[o], ("G", 0, nb + 16 + CW, 1), sub(x16, 32 * o, 32))
+                ops[-1]["free"] = made.get((t - 1, o), [])
                 tt(sub(LK, 32 * o + 32, 32), sub(xi, 32 * o, 32), sub(LK, 32 * o, 32), A.min)
                 if o == 0:
-                    D0 = ("ps5", 0, H, 1)
-                    mm(D0, [(ID, Z), (ID, W), (I(-2.0), X[0])], True, True)
+                    I2, D0, end = I(-2.0), mm(("ps5", 0, H, 1), [(ID, Z)], True, False), [0]
+                    for k, (l, r) in enumerate(((ID, W), (I2, X[0]))):
+                        mm(D0, [(l, r)], False, False)
+                        ops[-1]["fn"] = lambda k=k, l=l, r=r, end=end, D0=D0: g.tensor.matmul(R(D0), R(l), R(r), False, end[0] == k)
+                        ops[-1]["end"] = (end, k)
                     mm(MB, [(I(0.5), W), (I(-2 * MAGIC), NH)], False, True)
                     cm0 = act(new("WB", H), D0, ACT.Sign, bias=-0.5, scale=-1.0)
                     act(Y[0], MB, ACT.Identity, bias=-MAGIC)
         tt(sub(LK, 160, 32), sub(xi, 128, 32), sub(LK, 128, 32), A.min)
         for lo, n in ((0, 64), (64, 64), (128, 32)):
-            lk0, lk1, one = sub(LK, lo, n), sub(LK, lo + 32, n), sub(ONE, 0, n)
-            mm(sub(US, lo, n), [(ID, lk0), (IDN, lk1)], True, True)
-            gone = []
-            if lo < 128:
-                gone = [(I(-8192.0), lk1), (I(4096.0), sub(bp, lo, n))]
-                tk = mm(vp(288, n), [(I(4096.0), sub(KO, 96 + lo, n))] + gone, True, True)
-                tt(sub(ACk, lo, n), tk, sub(ACa, lo, n), A.min)
-                nd = mm(vp(352, n), [(ID, DC), (ID, DR), (I(-8192.0), lk1)], True, True)
-                tt(sub(xd, lo, n), nd, sub(xi, lo, n), A.max)
-                if not SL[t]:
-                    mm(vp(160 + lo, n), [(ID, C32M), (I(4096.0), lk1)], True, True)
+            lk0, lk1 = sub(LK, lo, n), sub(LK, lo + 32, n)
+            gone = [(I(-8192.0), lk1), (I(4096.0), sub(bp, lo, n))] if lo < 128 else []
             if not last:
-                pre = [(ID, sub(HY, lo, n)), (ID, sub(LY, lo, n))] if lo < 128 else [(I(2.0), LR)]
-                t2 = mm(("ps7", 0, n, 1), pre + [(I(16384.0), lk0), (I(-16384.0), lk1)], True, True)
-                r2 = act(f(n), t2, ACT.Identity, bias=CW[t] - 16384.0 + (-4096.0 if lo < 128 else 16.5 + 3072))
-                t1 = mm(vp(416, n), [(ID, sub(HA[t], lo, n)), (ID, sub(LA[t], lo, n)), (I(-4096.0), sub(SG, lo, n)),
-                                     (I(4096.0), sub(SG, lo + 32, n))] + gone, True, True)
-                if lo < 128:
-                    ts(sub(a16, lo, n), tt(f(n), t1, r2, A.max), 4096.0, A.add)
+                t2 = mm(("ps6", 0, n, 1), [(ID, sub(HB, lo, n)), (ID, sub(LY, lo, n)), (I(16384.0), lk0), (I(-16384.0), lk1)])
+                r2 = act(f(n), t2, ACT.Identity, bias=CW - 16384.0 + 9.0 / 32 - (4096.0 if lo < 128 else 0.0))
+                t1 = mm(vp(288, n), [(ID, sub(HB, lo, n)), (ID, sub(LA, lo, n)), (I(-4096.0), sub(SG, lo, n)),
+                                     (I(4096.0), sub(SG, lo + 32, n)), (I(9.0 / 32), lk0)] + gone)
+            if lo < 128:
+                nd = mm(vp(224, n), [(ID, DC), (ID, DR), (I(-8192.0), lk1)])
+                tk = mm(vp(160, n), [(I(4096.0), sub(KO, 96 + lo, n))] + gone)
+            mm(sub(US, lo, n), [(ID, lk0), (IDN, lk1)])
+            if not last:
+                tt(sub(BA, lo, n), t1, r2, A.max)
+                if lo == 0:
+                    ts(sub(a16, 0, 32), sub(BA, 0, 32), 4096.0 - 9.0 / 32, A.add)
+            if lo < 128:
+                tt(sub(xd, lo, n), nd, sub(xi, lo, n), A.max)
+                tt(sub(ACk, lo, n), tk, sub(ACa, lo, n), A.min)
         if t == 1:
             rotd = f(192)
             for k, src in enumerate((keys[0], losers[0])):
@@ -465,71 +461,61 @@ def build(g, T, nxt_addr, nxt_mask, neng):
 
         def root(o, y):
             if not last:
-                tt(sub(AN, 32 * o, 32), tt(f(), sub(US, 32 * o, 32), y, A.mult), sub(ACk if o < 4 else ACa, 32 * o, 32), A.add)
-                agat(regions(t + 1)[4][o], ("G", nb, 16 + CW[t] + 1024 * min(o + 1, 4), 1), sub(a16, 32 * o, 32))
+                tt(sub(AN, 32 * o, 32), tt(f(), sub(US, 32 * o, 32), y, A.mult), sub(ACk, 32 * o, 32), A.add)
+                src = (("G", nb, 16 + CW + 1024 * max(o, 1), 1), sub(a16, 32 * o, 32))
+                agat(regions(t + 1)[4][o], *src)
                 if o >= 1:
-                    champion_level(t + 1, o, st2, AN)
+                    champion_level(t + 1, o, st2, AN, src)
 
         scat(m16, Y[0])
-        y = cp(sub(ky, 0, 32), m) if last else m
+        y = m
         p = None
         pend, q16 = [], []
         for o in range(4):
-            how = HOW[t][o]
-            if o == 0:
-                cm = cm0
-            elif how == "f":
+            cm = cm0
+            if o > 0:
                 cm = fused(new("WB", H), P[o - 1], p, X[o], A.is_lt)
                 agat(Y[o], P[o - 1], p)
-            else:
-                agat(Y[o], P[o - 1], p)
-                dd = mm(("ps6", 0, H, 1), [(ID, X[o]), (IDN, Y[o])], True, True)
-                cm = act(new("WB", H), dd, ACT.Sign, bias=-0.5)
-            p, w = new("U", 32) if o < 3 or (last and LASTPN) else f(), f()
-            sc = count("ps0", cm, how == "s", p, w, vp(160 + 32 * o, 32), 0, SL[t], sub(LK, 32 * o + 32, 32))
-            if o == 3 and not last:
-                cp(sub(a16, 128, 32), tt(f(), t1, tt(f(), sc, r2, A.add), A.max))
-            q16.append(cp(new("U", 32), tt(f(), CQ, sc, A.subtract)) if LG[t][o] == "g" and not (last and o == 3 and LASTPN) else None)
+            p, w = new("U", 32) if o < 3 or LG[t][o] == "n" else None, f()
+            sc = count("ps0", cm, o == 0, p, w, 0, sub(LK, 32 * o + 32, 32))
+            if not last:
+                ts(sub(a16, 32 * o + 32, 32), tt(f(), sc, sub(BA, 32 * o + 32, 32), A.add), (4096.0 if o < 3 else 0.0) - 9.0 / 32, A.add)
+            q16.append(cp(new("U", 32), tt(f(), CQ, sc, A.subtract)) if LG[t][o] == "g" else None)
             root(o, y)
             d = tt(f(), y, sub(xd, 32 * o, 32), A.subtract)
             x = tt(f(), w, d, A.mult)
-            lsr = tt(sub(ls, 32 * o, 32), y, x, A.subtract)
+            tt(sub(ls, 32 * o, 32), y, x, A.subtract)
             y = tt(sub(ky, 32 * o + 32, 32), sub(xd, 32 * o, 32), x, A.add)
-            pend.append(cp(new("U", 32), lsr))
+            if o not in PAIR[t]:
+                k0 = len(pend)
+                both = cp(new("U", 32 * (o + 1 - k0)), sub(ls, 32 * k0, 32 * (o + 1 - k0)))
+                pend += [sub(both, 32 * k, 32) for k in range(o + 1 - k0)]
         root(4, y)
         if last:
-            cp(sub(ACk, 128, 32), sub(ACa, 128, 32))
-            rk = tt(f(160), ACk, mm(("ps1", 0, 160, 1), [(I(4096.0), sub(KO, 0, 160))], True, True), A.subtract)
+            rk = tt(f(160), ACk, mm(("ps1", 0, 160, 1), [(I(4096.0), sub(KO, 0, 160))]), A.subtract)
             tt(("YR", 0, 160, 1), tt(US, US, ky, A.mult), rk, A.add)
         for o in range(4):
-            b1, b2 = (("ps2", "ps4")[o % 2], 0, H, 1), ("ps5", 0, H, 1)
-            if last and o == 3 and LASTPN:
+            b1 = (("ps2", "ps4")[o % 2], 0, H, 1)
+            if LG[t][o] == "n":
                 pn, nw = new("WB", 2 * H), new("WB", H)
-                mm(b1, [(ID, Y[o]), (IDN, X[o])], True, True)
-                sg = act(new("WB", H), b1, ACT.Sign)
-                act(sub(pn, 0, H, 2), mm(b2, [(ID, Y[o]), (IDN, sg)], True, True), ACT.Copy)
-                act(sub(pn, 1, H, 2), mm(("ps7", 0, H, 1), [(ID, X[o]), (ID, sg)], True, True), ACT.Copy)
+                sg = act(new("WB", H), mm(b1, [(ID, Y[o]), (IDN, X[o])]), ACT.Sign)
+                act(sub(pn, 0, H, 2), mm(("ps5", 0, H, 1), [(ID, Y[o]), (IDN, sg)]), ACT.Copy)
+                act(sub(pn, 1, H, 2), mm(("ps7", 0, H, 1), [(ID, X[o]), (ID, sg)]), ACT.Copy)
                 for k in range(2):
                     agat(sub(nw, 256 * k, 256), pn, sub(p, 16 * k, 16))
                 scat(pend[o], nw)
+            elif LG[t][o] == "p":
+                mm(b1, [(ID, X[o]), (ID, Y[o]), (IDN, Y[o + 1])])
+                b2 = mm(("ps6", 0, H, 1), [(ID, X[o]), (ID, Y[o]), (I(-2.0), Y[o + 1])])
+                scat(pend[o], act(new("WB", H), b1, ACT.Copy), act(new("WB", H), b2, ACT.Sign, scale=-1.0), (t, o))
             elif LG[t][o] == "g":
-                old, sg = new("WB", H), new("WB", H)
-                parts = 2 if last and o == 3 else 1
-                n = H // parts
-                for k in range(parts):
-                    bk, ok = ((b1[0], b2[0])[k], 0, n, 1), sub(old, n * k, n)
-                    agat(ok, P[o], sub(q16[o], n // 16 * k, n // 16))
-                    if o < 3:
-                        mm(bk, [(ID, Y[o + 1]), (IDN, ok)], True, True)
-                    else:
-                        mm(bk, [(ID, sub(X[o], n * k, n)), (ID, sub(Y[o], n * k, n)), (I(-2.0), ok)], True, True)
-                    act(sub(sg, n * k, n), bk, ACT.Sign)
-                scat(pend[o], old, sg)
+                old = agat(new("WB", H), P[o], q16[o])
+                mm(b1, [(ID, Y[o + 1]), (IDN, old)] if o < 3 else [(ID, X[o]), (ID, Y[o]), (I(-2.0), old)])
+                scat(pend[o], old, act(new("WB", H), b1, ACT.Sign), (t, o))
             else:
-                mm(b1, [(ID, X[o]), (ID, Y[o]), (IDN, Y[o + 1])], True, True)
-                old = act(new("WB", H), b1, ACT.Copy)
-                mm(b1, [(IDN, Y[o + 1]), (ID, old)], True, True)
-                scat(pend[o], old, act(new("WB", H), b1, ACT.Sign, scale=-1.0))
+                old = act(new("WB", H), mm(b1, [(ID, X[o]), (ID, Y[o]), (IDN, Y[o + 1])]), ACT.Copy)
+                mm(b1, [(IDN, Y[o + 1]), (ID, old)])
+                scat(pend[o], old, act(new("WB", H), b1, ACT.Sign, scale=-1.0), (t, o))
         keys.append(sub(ky, 32, 128))
         losers.append(ls)
         st, AC = st2, AN
@@ -587,6 +573,140 @@ def replay(ops, dl, order, k, wake, far):
     return max(done)
 
 
+def refine(ops, dl, order, engs, moves, cool, VIEWS):
+    n = len(ops)
+    eng = ["vapgsx".index(e) for e in engs]
+    cost = [[k[o["kind"]] * o["cost"] for o in ops] for k, w, x in VIEWS]
+    late = [[o["lat"] + (x if o["eng"] == "x" else 0.0) for o in ops] for k, w, x in VIEWS]
+    cls = [1 if o["kind"] == 2 else 2 if "free" in o else 0 for o in ops]
+    hard = [[j for j, w in d if w] for d in dl]
+    soft = [[j for j, w in d if not w] for d in dl]
+    near = [set(j for j, w in d) for d in dl]
+
+    def play(order, v, lo=0, base=None):
+        cs, lt, wake = cost[v], late[v], VIEWS[v][1]
+        free, who = [0.0] * 6, [-1] * 6
+        done, fr, by = ([0.0] * n, [0.0] * n, [-1] * n) if base is None else (base[1][:], base[3][:], base[2][:])
+        turn = [-1, []]
+        for c in order[:lo]:
+            who[eng[c]] = c
+            if cls[c] == 1:
+                turn[0] = c
+            elif cls[c] == 2:
+                turn[1].append(c)
+        for e in range(5):
+            if who[e] >= 0:
+                free[e] = fr[who[e]]
+        who[5] = -1
+        for c in order[lo:]:
+            e = eng[c]
+            t, b = free[e], -2 - who[e]
+            for j in hard[c]:
+                x = done[j] + wake
+                if x > t:
+                    t, b = x, j
+            for j in soft[c]:
+                x = done[j] - 1.2 if e == 4 else fr[j]
+                if x > t:
+                    t, b = x, j
+            if cls[c] == 2:
+                j = turn[0]
+                if j >= 0 and done[j] + wake > t:
+                    t, b = done[j] + wake, (j if j in near[c] else -2 - j)
+                turn[1].append(c)
+            elif cls[c] == 1:
+                for j in turn[1][-4:]:
+                    if done[j] + wake > t:
+                        t, b = done[j] + wake, (j if j in near[c] else -2 - j)
+                turn[0] = c
+            t += cs[c]
+            fr[c], done[c], by[c] = t, t + lt[c], b
+            if e != 5:
+                free[e], who[e] = t, c
+        return max(done), done, by, fr
+
+    def chain(done, by):
+        c, out = done.index(max(done)), []
+        while c >= 0:
+            b = by[c]
+            if b < -1:
+                out.append((-2 - b, c))
+                b = -2 - b
+            c = b
+        return out
+    got = [play(order, v) for v in range(len(VIEWS))]
+    score = sum(x[0] for x in got)
+    top = (score, order, list(eng))
+    links = [chain(x[1], x[2]) for x in got]
+    seed = 4321
+    for it in range(moves):
+        seed = (seed * 1103515245 + 12345) % 2147483648
+        ln = links[(seed >> 8) % len(links)]
+        seed = (seed * 1103515245 + 12345) % 2147483648
+        a, b = ln[(seed >> 8) % len(ln)]
+        seed = (seed * 1103515245 + 12345) % 2147483648
+        kind = (seed >> 8) % 8
+        flip = -1
+        if kind < 2:
+            flip = (a, b)[kind]
+            if "alt" not in ops[flip]:
+                continue
+            eng[flip] = 1 - eng[flip]
+            new, ia = order, order.index(flip)
+        else:
+            ia, ib = order.index(a), order.index(b)
+            for r in range(kind - 2 if kind < 5 else 0):
+                k = ia - 1
+                while k >= 0 and eng[order[k]] != eng[b]:
+                    k -= 1
+                if k >= 0:
+                    ia, a = k, order[k]
+            seg = order[ia:ib + 1]
+            if kind < 5:
+                mark, need, es = {b}, set(near[b]), set()
+                for x in seg[-2:0:-1]:
+                    if x in need or eng[x] in es:
+                        mark.add(x)
+                        need |= near[x]
+                        if eng[x] != 5:
+                            es.add(eng[x])
+                if a in need or eng[a] in es:
+                    continue
+                new = order[:ia] + [x for x in seg if x in mark] + [x for x in seg if x not in mark] + order[ib + 1:]
+            else:
+                more = kind - 5
+                while more and ib + 1 < n:
+                    ib += 1
+                    more -= eng[order[ib]] == eng[a]
+                seg = order[ia:ib + 1]
+                mark, es = {a}, set()
+                for x in seg[1:]:
+                    if not mark.isdisjoint(near[x]) or eng[x] in es:
+                        mark.add(x)
+                        if eng[x] != 5:
+                            es.add(eng[x])
+                if b in mark:
+                    continue
+                new = order[:ia] + [x for x in seg if x not in mark] + [x for x in seg if x in mark] + order[ib + 1:]
+        seed = (seed * 1103515245 + 12345) % 2147483648
+        bound = score + cool * (1.0 - it / moves) * ((seed >> 8) % 1000 / 1000.0) ** 3
+        tried, sc = [], 0.0
+        for v in range(len(VIEWS)):
+            tried.append(play(new, v, ia, got[v]))
+            sc += tried[-1][0] - got[v][0]
+            if score + sc > bound + 1.0:
+                break
+        if score + sc <= bound and len(tried) == len(VIEWS):
+            order, got, score = new, tried, score + sc
+            links = [chain(x[1], x[2]) for x in got]
+            if score < top[0]:
+                top = (score, order, list(eng))
+        elif flip >= 0:
+            eng[flip] = 1 - eng[flip]
+    eng[:] = top[2]
+    return top[1], play(top[1], 0)[1], ["vapgsx"[e] for e in eng], top[0]
+
+
 def schedule(ops):
     n = len(ops)
     deps = [dict() for _ in range(n)]
@@ -613,11 +733,13 @@ def schedule(ops):
             if a[0][:2] == "ps" and s and ops[s[-1][0]]["eng"] != o["eng"]:
                 s[:] = [x for i, x in enumerate(s) if all(ops[y[0]]["eng"] == ops[s[-1][0]]["eng"] for y in s[i:])]
             s.append((k, a, wr))
-    dl, pre, suc, rsuc = [], [], [[] for _ in range(n)], [[] for _ in range(n)]
+
+    def lean():
+        return [[(j, w) for j, w in deps[k].items() if not (w and any(deps[i].get(j) for i in deps[k] if i > j))] for k in range(n)]
+    dl, suc, rsuc = lean(), [[] for _ in range(n)], [[] for _ in range(n)]
     for k in range(n):
-        dl.append([(j, w) for j, w in deps[k].items() if not (w and any(deps[i].get(j) for i in deps[k] if i > j))])
-        pre.append([(j, ops[j]["cost"] + (ops[j]["lat"] + WAKE if w else ops[j]["lat"] - 1.2 if ops[k]["eng"] == "s" else 0.0)) for j, w in dl[k]])
-        for j, lag in pre[k]:
+        for j, w in dl[k]:
+            lag = ops[j]["cost"] + (ops[j]["lat"] + WAKE if w else ops[j]["lat"] - 1.2 if ops[k]["eng"] == "s" else 0.0)
             suc[j].append((k, lag))
             rsuc[k].append((j, lag + ops[k]["cost"] - ops[j]["cost"]))
     tail = [0.0] * n
@@ -627,37 +749,59 @@ def schedule(ops):
     def weigh(st):
         order = sorted(range(n), key=lambda k: (st[k], k))
         return sum(replay(ops, dl, order, k, w, x) for k, w, x in VIEWS), order
-    best = justify(ops, suc, rsuc, [(-tail[k], k) for k in range(n)])
-    score, order = weigh(best)
-    seed = 12345
-    for it in range(TRIES):
-        key = list(best)
-        seed = (seed * 1103515245 + 12345) % 2147483648
-        lo = (seed >> 8) % 1000 / 1000.0 * max(best)
-        seed = (seed * 1103515245 + 12345) % 2147483648
-        amp = SHAKE * ((seed >> 8) % 1000 / 1000.0) ** 2
-        for k in range(n):
-            if lo <= best[k] < lo + SPAN:
-                seed = (seed * 1103515245 + 12345) % 2147483648
-                key[k] += amp * ((seed >> 8) % 2001 - 1000) / 1000.0
-        for k in range(n):
-            for j, lag in pre[k]:
-                if key[j] > key[k]:
-                    key[k] = key[j]
-        near = [k for k in range(n) if "alt" in ops[k] and lo <= best[k] < lo + SPAN]
-        flip = []
-        for r in range(it % 3 if near else 0):
+    for k, o in enumerate(ops):
+        for j in list(deps[k]):
+            if (o["kind"] == 2 and "free" in ops[j]) or (ops[j]["kind"] == 2 and j not in o.get("free", [j])):
+                del deps[k][j]
+    dl2 = lean()
+    for k, o in enumerate(ops):
+        if "end" in o and "end" in ops[k - 1]:
+            del deps[k][k - 1]
+    dl3 = lean()
+    top = None
+    for seed in SEEDS:
+        best = justify(ops, suc, rsuc, [(-tail[k], k) for k in range(n)])
+        score, order = weigh(best)
+        for it in range(TRIES):
+            key = list(best)
             seed = (seed * 1103515245 + 12345) % 2147483648
-            flip.append(near[(seed >> 8) % len(near)])
-            swap(ops[flip[-1]])
-        got = justify(ops, suc, rsuc, [(key[k], k) for k in range(n)])
-        sc, od = weigh(got)
-        if sc <= score:
-            best, score, order = got, sc, od
-        else:
-            for k in flip:
-                swap(ops[k])
-    return order, deps, best, [best[k] + ops[k]["cost"] + ops[k]["lat"] for k in range(n)], [o["eng"] for o in ops]
+            lo = (seed >> 8) % 1000 / 1000.0 * max(best)
+            seed = (seed * 1103515245 + 12345) % 2147483648
+            amp = SHAKE * ((seed >> 8) % 1000 / 1000.0) ** 2
+            for k in range(n):
+                if lo <= best[k] < lo + SPAN:
+                    seed = (seed * 1103515245 + 12345) % 2147483648
+                    key[k] += amp * ((seed >> 8) % 2001 - 1000) / 1000.0
+            for k in range(n):
+                for j, w in dl[k]:
+                    if key[j] > key[k]:
+                        key[k] = key[j]
+            near = [k for k in range(n) if "alt" in ops[k] and lo <= best[k] < lo + SPAN]
+            flip = []
+            for r in range(it % 3 if near else 0):
+                seed = (seed * 1103515245 + 12345) % 2147483648
+                flip.append(near[(seed >> 8) % len(near)])
+                swap(ops[flip[-1]])
+            got = justify(ops, suc, rsuc, [(key[k], k) for k in range(n)])
+            sc, od = weigh(got)
+            if sc <= score:
+                best, score, order = got, sc, od
+            else:
+                for k in flip:
+                    swap(ops[k])
+        got = refine(ops, dl2, order, [o["eng"] for o in ops], MOVES, COOL, VIEWS)
+        if top is None or got[3] < top[3]:
+            top = got
+    order, done, engs = refine(ops, dl2, top[0], top[2], MORE, COOL, VIEWS + FAR)[:3]
+    order, done, engs = refine(ops, dl3, order, engs, LAST, COOL / 2, VIEWS + FAR + (((1.35, 1.6, 2.4, 1.35), 0.2, 3.0),) * 2)[:3]
+    turns = []
+    for k in order:
+        if ops[k]["kind"] == 2 or "free" in ops[k]:
+            for j in turns:
+                if (ops[j]["kind"] == 2) != (ops[k]["kind"] == 2):
+                    deps[k][j] = True
+            turns.append(k)
+    return order, deps, [done[k] - ops[k]["cost"] - ops[k]["lat"] for k in range(n)], done, engs
 
 
 def rank_program(g, core, T, topo):
@@ -673,6 +817,9 @@ def rank_program(g, core, T, topo):
     for o, e in zip(ops, engs):
         if o["eng"] != e:
             swap(o)
+    for k in order:
+        if "end" in ops[k]:
+            ops[k]["end"][0][0] = ops[k]["end"][1]
     queue = {"v": g.vector, "a": g.scalar, "p": g.tensor, "g": g, "s": g.sync}
     total, mark, clock = {}, {}, {}
     known = {e: {} for e in queue}

from concourse.mybir import AluOpType, ActivationFunctionType

V, H, ST = 4096, 512, 3
CW = 4096
NB = [V + H + (16 + CW + 4096) * _t for _t in range(ST + 1)]
MAGIC = 12582912.0
MAGIC16 = 201326592.0
PARTS = (2, 1, 1)
LG = ("cccg", "cccg", "ccpn")
PAIR = ((0, 2), (0, 2), ())
STAGES = ((0, 64), (64, 64))
SPLIT = 2
HELD = 2
WAKE, TRIES, SHAKE, SPAN, MOVES, MORE, COOL, SEEDS = 0.2, 500, 2.0, 6.0, 7000, 30000, 1.0, (3,)
LAST = 22000
VIEWS = (((1.0, 1.0, 1.0, 1.0), 0.2, 0.0), ((1.14, 1.2, 1.5, 1.14), 0.25, 0.8), ((1.25, 1.0, 1.0, 1.25), 0.2, 1.5),
         ((1.0, 1.4, 2.0, 1.0), 0.2, 0.8), ((1.0, 1.0, 1.0, 1.0), 0.22, 0.4))
FAR = (((1.25, 1.45, 2.2, 1.25), 0.2, 6.0), ((1.1, 1.0, 1.0, 1.1), 0.2, 3.5))
NDMA = 8

SCRATCH = {
    "G": ("sbuf", [128, NB[ST]], "bfloat16"),
    "TB": ("sbuf", [128, V], "bfloat16"),
    "CHI": ("sbuf", [128, 1024], "int32"),
    "HI": ("sbuf", [128, 1024], "bfloat16"),
    "LO": ("sbuf", [128, 1024], "bfloat16"),
    "RT": ("sbuf", [128, 160], "int32"),
    "YR": ("sbuf", [128, 160], "float32"),
    "WB": ("sbuf", [128, 36864], "bfloat16"),
    "F": ("sbuf", [128, 14336], "float32"),
    "IP": ("sbuf", [128, 3072], "int32"),
    "U": ("sbuf", [128, 3072], "uint16"),
}
for _t in range(ST):
    SCRATCH["Z%d" % _t] = ("sbuf", [128, H], "bfloat16")
    SCRATCH["W%d" % _t] = ("sbuf", [128, H], "bfloat16")
    SCRATCH["ZT%d" % _t] = ("sbuf", [128, 8], "float32")
    SCRATCH["WT%d" % _t] = ("sbuf", [128, 8], "float32")
for _b in range(8):
    SCRATCH["ps%d" % _b] = ("psum", [128, 512], "float32")
SEMAPHORES = (["cv", "ca", "cp", "cg", "sent"] + ["d%d" % k for k in range(NDMA)]
              + ["aw%d" % k for k in range(ST)] + ["at%d" % k for k in range(ST)])

A = AluOpType
ACT = ActivationFunctionType
CY = 0.83e-3 * 1.1
PC = 0.42e-3 * 1.1
GA, SC = 1.3 * 0.83e-3, 2.5 * 0.83e-3
WIDE2 = ("G", "TB", "HI", "LO", "WB", "U", "Z0", "Z1", "Z2", "W0", "W1", "W2")
REC = ("G", 0, V + H, 1)
PLAN = {}


def sub(a, lo, n, st=1):
    return (a[0], a[1] + lo * a[3], n, a[3] * st)


def meet(a, b):
    alo, ahi = a[1], a[1] + (a[2] - 1) * a[3]
    blo, bhi = b[1], b[1] + (b[2] - 1) * b[3]
    if ahi < blo or bhi < alo:
        return False
    return not (a[3] == b[3] and a[3] > 1 and (alo - blo) % a[3] != 0)


def two(a):
    return a[0] in WIDE2


def swap(o):
    o["eng"], o["fn"], o["alt"] = "v" if o["eng"] == "a" else "a", o["alt"], o["fn"]


def build(g, T, nxt_addr, nxt_mask, neng):
    ops, held, made = [], {}, {}
    fill = {"WB": 0, "F": 0, "IP": 0, "U": 0, "d": 0}

    def R(a):
        if a[3] == 1:
            return T[a[0]][:, a[1]:a[1] + a[2]]
        return T[a[0]][:, a[1]:a[1] + (a[2] - 1) * a[3] + 1:a[3]]

    def new(pool, n):
        lo = fill[pool]
        fill[pool] = lo + (n + 15) // 16 * 16
        return (pool, lo, n, 1)

    def f(n=32):
        return new("F", n)

    def vp(lo, n):
        return ("ps3", lo, n, 1)

    def op(eng, fn, rd, wr, cost, lat=0.0, sem=None, acc=False, after=()):
        ops.append({"eng": eng, "fn": fn, "rd": rd, "wr": wr, "cost": cost, "lat": lat, "sem": sem, "acc": acc, "after": list(after),
                    "kind": 3 if eng == "p" else 0 if not any(a[0] == "U" for a in rd) else 2 if wr[0] == REC else 1})
        return len(ops) - 1

    def S(x):
        return R(x) if isinstance(x, tuple) else x

    def aps(*xs):
        return [x for x in xs if isinstance(x, tuple)]

    def cp(o, i):
        op("v", lambda: g.vector.tensor_copy(R(o), R(i)), [i], [o], CY * max(64, o[2] * (0.5 if two(o) and two(i) else 1)))
        return o

    def ts(o, i, s1, o0, s2=None, o1=None):
        c = CY * max(64, o[2] * (0.5 if two(o) and two(i) else 1))
        if o1 is None:
            op("v", lambda: g.vector.tensor_scalar(R(o), R(i), S(s1), None, o0), aps(i, s1), [o], c)
        else:
            op("v", lambda: g.vector.tensor_scalar(R(o), R(i), S(s1), S(s2), o0, o1), aps(i, s1, s2), [o], c)
        return o

    def tt(o, a, b, alu):
        k = 1 if a[0][:2] == "ps" or b[0][:2] == "ps" else 2
        op("v", lambda: g.vector.tensor_tensor(R(o), R(a), R(b), alu), [a, b], [o], CY * max(64, o[2] * k))
        return o

    def mset(o, c):
        op("v", lambda: g.vector.memset(R(o), c), [], [o], CY * max(64, o[2] * (0.5 if two(o) else 1)))
        return o

    def act(o, i, fn, bias=0.0, scale=1.0):
        op("a", lambda: g.scalar.activation(R(o), R(i), fn, bias=S(bias), scale=S(scale)), aps(i, bias, scale), [o], CY * max(64, o[2]))
        return o

    def aff(o, i, scale, bias=0.0):
        act(o, i, ACT.Identity, bias, scale)
        ops[-1]["alt"] = lambda: g.vector.tensor_scalar(R(o), R(i), S(scale), S(bias), A.mult, A.add)
        return o

    def IND(win, off):
        return R(win).indirect(R(off))

    def agat(o, win, off, rd=None):
        k = op("a", lambda: g.scalar.activation(R(o), IND(win, off), ACT.Copy), (rd or [win]) + [off], [o], 0.065 + GA * o[2])
        ops[k]["alt"] = lambda: g.vector.tensor_copy(R(o), IND(win, off))
        return o

    def vgat(o, win, off):
        agat(o, win, off)
        swap(ops[-1])
        return o

    def fused(o, win, off, b, alu):
        op("v", lambda: g.vector.tensor_tensor(R(o), IND(win, off), R(b), alu), [win, off, b], [o], 0.05 + GA * o[2])
        return o

    def scat(off, src, add=None, tag=None):
        if tag is not None and tag[1] >= HELD and tag[0] < ST - 1 and tag not in held:
            held[tag] = (off, src, add, tag)
            return
        n = H // SPLIT
        c = 0.05 + SC * n
        for k in range(SPLIT):
            o2, s2 = sub(off, k * n // 16, n // 16), sub(src, k * n, n)
            if add is None:
                op("v", lambda o2=o2, s2=s2: g.vector.tensor_copy(IND(REC, o2), R(s2)), [o2, s2], [REC], c)
            else:
                a2 = sub(add, k * n, n)
                op("v", lambda o2=o2, s2=s2, a2=a2: g.vector.tensor_tensor(IND(REC, o2), R(s2), R(a2), A.add), [o2, s2, a2], [REC], c)
            made.setdefault(tag, []).append(len(ops) - 1)

    def mm(o, terms, start=True, stop=True):
        if len(terms) > 1 and o[2] >= 256:
            for k, x in enumerate(terms):
                mm(o, [x], start and k == 0, stop and k == len(terms) - 1)
            return o

        def fn():
            last = None
            for k, (l, r) in enumerate(terms):
                last = g.tensor.matmul(R(o), R(l), R(r), start and k == 0, stop and k == len(terms) - 1)
            return last
        c = sum(PC * max(64, r[2]) * (4 if r[0] == "F" else 1) for l, r in terms)
        op("p", fn, [x for t in terms for x in t], [o], c, lat=0.05, acc=not start)
        return o

    def iota(o, pat, base, cm):
        if o[0] == "IP":
            op("g", lambda: g.iota(R(o), pat, base, cm), [], [o], 0.13 + 2 * CY * o[2])
        else:
            op("g", lambda: g.iota(R(o), pat, base, cm, allow_small_or_imprecise_dtypes=True), [], [o], 0.13 + 2 * CY * o[2])
        return o

    def asel(o, pat, cmp, fl, base, cm):
        op("g", lambda: g.affine_select(R(o), R(o), pat, cmp, fl, base, cm), [o], [o], 0.17 + 2 * CY * o[2])
        return o

    def dma(q, out, in_, rd, wr, nbytes, after=()):
        name = "d%d" % fill["d"]
        fill["d"] += 1
        e = g.sync if q == "s" else g.scalar
        return op(q, lambda: e.dma_start(out, in_), rd, wr, 0.06, lat=1.2 + nbytes / 300e3, sem=(name, 16), after=after)

    def send(dst, src, sem, nbytes):
        k = op("g", lambda: g.remote_dma(R(dst), R(src), T.sem[sem], T.sem.sent, nxt_addr[1], nxt_addr[0], nxt_mask),
               [src], [], 0.4, sem=("", 0))
        op("x", None, [], [dst], 0.0, lat=1.6 + nbytes / 70e3, sem=(sem, neng), after=[k])

    dma("a", T.RT[:], T.rt[:], [], [("RT", 0, 160, 1)], 80e3)
    big = dma("s", T.G[:, 0:V], T.rec[:], [], [("G", 0, V, 1)], 1050e3)
    dma("s", T.CHI[:], T.ch[:], [], [("CHI", 0, 1024, 1)], 520e3, after=[big])
    pi = iota(new("IP", 1), [[0, 1]], 0, 1)
    ri = ts(new("IP", 1), pi, 15, A.bitwise_and)
    RF2 = ts(f(1), ri, 2.0, A.mult)
    PQ = aff(f(1), RF2, 1.0, 0.5)
    E8 = iota(f(8), [[0, 8]], 1, 0)
    asel(E8, [[-16, 8]], A.is_ge, 0.0, 0, 1)
    asel(E8, [[16, 8]], A.is_ge, 0.0, 15, -1)

    def summing(scale):
        k = mset(new("WB", 144), 0.0)
        aff(sub(k, 16, 8, 16), E8, scale)
        return k
    EB = {False: summing(1.0 / 32), True: summing(1.0 / 64)}
    ID = iota(new("WB", 128), [[0, 128]], 1, 0)
    asel(ID, [[-1, 128]], A.is_equal, 0.0, 0, 1)
    ids = {1.0: ID}

    def I(x):
        if x not in ids:
            ids[x] = aff(new("WB", 128), ID, x)
        return ids[x]
    IDN = I(-1.0)
    C32 = iota(new("WB", 32), [[32, 32]], 0, 0)
    ONE = mset(new("WB", 160), 1.0)
    CQ = aff(f(), C32, 2.0, PQ)
    DC = iota(new("WB", 64), [[0, 2], [1, 32]], 0, 0)
    DR = aff(new("WB", 64), sub(ONE, 0, 64), aff(f(1), RF2, 16.0, 4096.0))
    mset(("G", V, H, 1), 0.0)
    for t in range(ST):
        aff(("G", NB[t], 16, 1), sub(ONE, 0, 16), 256.0)
        aff(("ZT%d" % t, 0, 8, 1), sub(ONE, 0, 8), 1.0)
    KO = iota(new("WB", 256), [[1, 8], [0, 32]], 1, 0)
    KE = [summing(act(f(1), act(f(1), RF2, ACT.Abs, bias=-8.0 * o - 1), ACT.Relu, bias=1.5, scale=-0.5)) for o in range(4)]
    BD = iota(new("WB", 128), [[0, 128]], 1, 0)
    asel(BD, [[-16, 8], [0, 16]], A.is_ge, 0.0, 0, 1)
    asel(BD, [[16, 8], [0, 16]], A.is_ge, 0.0, 15, -1)
    BDN = aff(new("WB", 128), BD, -1.0)
    TT = iota(f(512), [[0, 512]], 1, 0)
    asel(TT, [[16, 2], [-16, 8], [-1, 32]], A.is_equal, 0.0, 0, 1)
    asel(TT, [[0, 2], [-16, 8], [0, 32]], A.is_ge, 0.0, 0, 1)
    asel(TT, [[0, 2], [16, 8], [0, 32]], A.is_ge, 0.0, 15, -1)
    JC = aff(f(16), iota(f(16), [[32, 16]], 0, 0), 1.0, aff(f(1), RF2, 0.5, 7.5))
    J16 = aff(f(4), iota(f(4), [[256, 4]], 0, 0), 1.0, aff(f(1), RF2, 8.0, 7.5))
    NH = mset(new("WB", H), -0.5)
    M75 = aff(new("WB", 2), sub(ONE, 0, 2), -7.5)
    M85 = aff(new("WB", 2), sub(ONE, 0, 2), -8.5)
    IF8 = aff(f(128), ID, -8192.0)
    HA, LA, HB, LY = new("WB", 128), new("WB", 160), new("WB", 160), new("WB", 160)
    iota(sub(HA, 0, 32), [[32, 32]], 0, 0)
    iota(sub(HA, 32, 96), [[1024, 3], [32, 32]], 0, 0)
    iota(sub(HB, 0, 32), [[32, 32]], 0, 0)
    iota(sub(HB, 32, 128), [[1024, 4], [0, 32]], 0, 0)
    aff(sub(LA, 0, 32), sub(ONE, 0, 32), RF2, 16.0)
    aff(sub(LA, 32, 128), sub(ONE, 0, 128), RF2, 17.0)
    aff(sub(LY, 0, 32), sub(ONE, 0, 32), RF2, 17.0)
    aff(sub(LY, 32, 128), sub(ONE, 0, 128), RF2, 16.5)
    ap = mm(("ps7", 0, 128, 1), [(ID, HA), (ID, sub(LA, 0, 128))])
    APA = [act(f(128), ap, ACT.Identity, bias=float(NB[t])) for t in range(ST)]
    LKS = [new("WB", 192) for t in range(ST)]
    SGS = [new("WB", 192) for t in range(ST)]
    for t in range(ST):
        aff(sub(LKS[t], 0, 32), sub(ONE, 0, 32), 1.0)
        aff(sub(SGS[t], 0, 32), sub(ONE, 0, 32), 1.0)
        aff(sub(SGS[t], 160, 32), sub(ONE, 0, 32), -1.0)
    hi, lo, chi = ("HI", 0, 1024, 1), ("LO", 0, 1024, 1), ("CHI", 0, 1024, 1)
    for k in range(4):
        h = cp(sub(hi, 256 * k, 256), sub(chi, 256 * k, 256))
        tt(sub(lo, 256 * k, 256), mm(("ps%d" % (7, 4)[k % 2], 0, 256, 1), [(IDN, h)]), sub(chi, 256 * k, 256), A.add)
    TBW = [("TB0", 0, 1, 1), ("TB1", 0, 1, 1)]
    op("v", lambda: g.vector.memset(T.TB[:], 0.0), [], TBW, CY * V / 2)
    dma("s", T.TB[0:128:4, :], T.HI[:], [hi], [TBW[0]], 260e3)
    dma("s", T.TB[1:128:4, :], T.LO[:], [lo], [TBW[1]], 260e3)

    def count(bank, cmpt, signed, p, w, c0=0, lk=None):
        n = w[2]
        o = (bank, 0, n, 1)
        mm(o, [(ID, sub(C32, c0, n)), (I((-0.5 if signed else -8.5) / 32 + (9.0 / 32 if lk else 0.0)), sub(ONE, 0, n))]
           + ([(I(-9.0 / 32), lk)] if lk else []), True, False)
        mm(o, [(sub(EB[signed], 16 - r, 128), sub(cmpt, r, n, 16)) for r in range(16)], False, True)
        if p:
            ts(p, o, PQ, A.add)
        tt(w, o, sub(C32, c0, n), A.is_gt)
        return o

    def rotate(out, win, off, PM):
        rg = agat(f(48), win, off)
        return mm(out, [(sub(PM, 0, 128), sub(rg, 0, 32)), (sub(PM, 128, 128), sub(rg, 1, 32))])

    def regions(t):
        p0 = NB[t] + 16 + CW
        P = [("G", p0 + 1024 * o, 1024, 1) for o in range(4)]
        X = [sub(p, 0, H, 2) for p in P]
        Y = [sub(p, 1, H, 2) for p in P]
        AA = [("G", NB[t] + 16, H, 2)] + [("G", NB[t] + 17 + 1024 * o, H, 2) for o in range(4)]
        return NB[t], P, X, Y, AA

    def champion_level(t, o, st, AC, src=None):
        nb, P, X, Y, AA = regions(t)
        C = [None] + [("G", nb + 16 + 1024 * k, 1024, 1) for k in range(4)]
        p2, w, cm = new("U", 32), f(), new("WB", H)
        parts = PARTS[t]
        n = H // parts
        if o == 4:
            zc = vgat(new("WB", 16), sub(C[3], 0, 32), sub(st["p16"], 0, 1))
            r4, s3 = sub(AA[4], 0, 1), ("ps6", 0, 3, 1)
            c0 = tt(new("WB", 1), sub(zc, 0, 1), r4, A.is_gt)
            mm(sub(s3, 1, 1), [(ID, sub(M75, 0, 1)), (BD, sub(zc, 0, 1))])
            mm(sub(s3, 2, 1), [(BD, r4), (BDN, sub(zc, 0, 1))])
            mm(sub(s3, 0, 1), [(ID, sub(M85, 0, 1)), (BD, c0)])
            ZT = ("ZT%d" % t, 0, 8, 1)
            ts(sub(ZT, 0, 1), ts(f(1), sub(s3, 0, 1), 0.0, A.is_gt, sub(s3, 2, 1), A.mult), sub(s3, 1, 1), A.add)
            send(("WT%d" % t, 0, 8, 1), ZT, "at%d" % t, 30e3)
        for k in range(parts):
            ck, ak = sub(cm, n * k, n), sub(AA[o], n * k, n)
            signed = o == 1 and t == 0
            if o > 1:
                wk, pk = sub(C[o - 1], 0, 2 * n * (k + 1)), sub(st["p16"], n // 16 * k, n // 16)
                fused(ck, wk, pk, ak, A.is_gt)
                agat(sub(C[o], 2 * n * k, n, 2), wk, pk)
            elif signed:
                d = mm((("ps5", "ps2")[k], 0, n, 1), [(IDN, ak), (ID, sub(C[o], 2 * n * k, n, 2))])
                act(ck, d, ACT.Sign, bias=-0.5)
            else:
                fused(ck, src[0], src[1], AA[0], A.is_lt)
            c0, cn = n // 16 * k, n // 16
            count(("ps1", "ps0")[k], ck, signed, sub(p2, c0, cn), sub(w, c0, cn), c0)
        u = tt(f(), w, sub(AC, 32 * o, 32), A.mult)
        old = st["cur"]
        st["cur"] = tt(new("IP", 32) if o == 3 else f(), u, old, A.max)
        if o == 4:
            m3 = ts(new("IP", 32), old, 4095, A.bitwise_and)
            d = tt(f(), aff(f(), sub(AC, 128, 32), 1.0, -20480.0), m3, A.subtract)
            st["ky"] = f(160)
            st["m"] = tt(sub(st["ky"], 0, 32), tt(f(), w, d, A.mult), m3, A.add)
        st["p16"], st["win"] = p2, C[o]

    rt = ("RT", 0, 160, 1)
    r16 = cp(new("U", 160), tt(f(160), ts(vp(0, 160), rt, 0.5, A.is_lt, float(NB[0]), A.mult), rt, A.add))
    AC = tt(f(160), mm(vp(160, 160), [(I(4096.0), sub(KO, 0, 160))]), rt, A.add)
    nb, P, X, Y, AA = regions(0)
    for o in range(5):
        for k in range(2):
            (vgat if o in (0, 2) else agat)(sub(AA[o], 256 * k, 256), ("G", 0, NB[0] + 16, 1), sub(r16, 32 * o + 16 * k, 16))
    st = {"cur": sub(AC, 0, 32)}
    for o in range(1, 5):
        champion_level(0, o, st, AC)

    keys, losers, rotd = [], [], None
    for t in range(ST):
        nb, P, X, Y, AA = regions(t)
        last = t == ST - 1
        Z, W = ("Z%d" % t, 0, H, 1), ("W%d" % t, 0, H, 1)
        cur, m, ky, ls = st["cur"], st["m"], st["ky"], f(128)
        agat(Z, st["win"], st["p16"])
        send(W, Z, "aw%d" % t, 131e3)
        m16 = cp(new("U", 32), m)
        G1 = agat(new("WB", H), ("TB", 0, V, 1), m16, TBW)
        MB = ("ps1", 0, H, 1)
        mm(MB, [(I(0.5), NH), (I(0.5), Z)], True, False)

        def found(e, ks):
            for o in range(e[2] // 32):
                tt(sub(e, 32 * o, 32), sub(ks, 32 * o, 32), m, A.is_equal)
            return e
        el = ef = None
        if t == 1:
            el = ef = tt(f(128), found(vp(0, 128), keys[0]), losers[0], A.mult)
        if t == 2:
            la = tt(f(128), found(vp(0, 128), keys[1]), aff(f(128), losers[1], 1.0, 8192.0), A.mult)
            lb = tt(vp(128, 128), found(vp(128, 128), keys[0]), losers[0], A.mult)
            lc = tt(vp(256, 96), found(vp(256, 96), sub(rotd, 0, 96)), sub(rotd, 96, 96), A.mult)
            ef = tt(f(128), lb, la, A.max)
            tt(sub(ef, 0, 96), lc, sub(ef, 0, 96), A.max)
            el = ts(new("IP", 128), cp(new("IP", 128), ef), 8191, A.bitwise_and)
        SG, LK = SGS[t], LKS[t]
        for o in range(1, 5):
            act(sub(SG, 32 * o, 32), cur, ACT.Sign, bias=-4096.0 * (o + 1))
        Ta = mm(vp(288, 160), [(I(4096.0), sub(KO, 64, 160)), (I(-4096.0), sub(SG, 0, 160)), (I(4096.0), sub(SG, 32, 160))])
        ACk, xi = new("IP", 160), new("IP", 160)
        ACa = tt(f(128), sub(Ta, 0, 128), sub(AC, 0, 128), A.min)
        tt(sub(ACk, 128, 32), sub(Ta, 128, 32), sub(AC, 128, 32), A.min)
        ts(sub(xi, 128, 32), sub(ACk, 128, 32), 4095, A.bitwise_and)
        sb = ("WT%d" % t, 0, 1, 1)
        j1 = ts(new("IP", 4), J16, sb, A.add)
        f16 = ts(f(1), sb, MAGIC16, A.add, MAGIC16, A.subtract)
        j2 = ts(new("IP", 4), j1, 4, A.arith_shift_right, 31, A.bitwise_and)
        off = sub(cp(new("U", 4), j2), 0, 3)
        PM = agat(f(256), TT, ts(new("U", 16), JC, sb, A.add, f16, A.subtract))
        rw = f(128)
        for lo, n in STAGES:
            kd = (("ps6", "ps0")[lo > 0], 0, n, 1)
            for o in range(lo // 32, (lo + n) // 32):
                pre = [(I(2.0 ** 26), sub(ONE, 0, 32)), (I(-2.0 ** 26), sub(SG, 32 * o + 32, 32))] + ([(IF8, sub(ef, 32 * o, 32))] if el else [])
                if 32 * o == lo:
                    mm(sub(kd, 0, 32), pre, True, False)
                mm(sub(kd, 32 * o - lo, 32), (pre if 32 * o > lo else []) + [(sub(KE[o], 16 - r, 128), sub(G1, r, 32, 16)) for r in range(16)], 32 * o > lo)
            if el:
                tt(sub(rw, lo, n), kd, sub(el, lo, n), A.max)
            else:
                act(sub(rw, lo, n), kd, ACT.Copy)
        x16, xa, bp = new("U", 128), new("IP", 128), new("WB", 128)
        US, xd, a16, BA = vp(0, 160), f(128), new("U", 160), f(160)
        for lo, n in STAGES:
            rb = (("ps7", "ps6")[lo > 0], lo, n, 1)
            for o in range(lo // 32, (lo + n) // 32):
                rotate(sub(rb, 32 * o - lo, 32), sub(rw, 32 * o, 32), off, PM)
            xp = tt(f(n), rb, sub(APA[t], lo, n), A.min)
            cp(sub(x16, lo, n), xp)
            tt(sub(xa, lo, n), rb, sub(ACa, lo, n), A.min)
            act(sub(bp, lo, n), xp, ACT.Sign, bias=4300.0, scale=-1.0)
            ts(sub(xi, lo, n), sub(xa, lo, n), 4095, A.bitwise_and)
            for o in range(lo // 32, (lo + n) // 32):
                if (t - 1, o) in held:
                    scat(*held[t - 1, o])
                (vgat if o % 2 else agat)(X[o], ("G", 0, nb + 16 + CW, 1), sub(x16, 32 * o, 32))
                ops[-1]["free"] = made.get((t - 1, o), [])
                tt(sub(LK, 32 * o + 32, 32), sub(xi, 32 * o, 32), sub(LK, 32 * o, 32), A.min)
                if o == 0:
                    I2, D0, end = I(-2.0), mm(("ps5", 0, H, 1), [(ID, Z)], True, False), [0]
                    for k, (l, r) in enumerate(((ID, W), (I2, X[0]))):
                        mm(D0, [(l, r)], False, False)
                        ops[-1]["fn"] = lambda k=k, l=l, r=r, end=end, D0=D0: g.tensor.matmul(R(D0), R(l), R(r), False, end[0] == k)
                        ops[-1]["end"] = (end, k)
                    mm(MB, [(I(0.5), W), (I(-2 * MAGIC), NH)], False, True)
                    cm0 = act(new("WB", H), D0, ACT.Sign, bias=-0.5, scale=-1.0)
                    act(Y[0], MB, ACT.Identity, bias=-MAGIC)
        tt(sub(LK, 160, 32), sub(xi, 128, 32), sub(LK, 128, 32), A.min)
        for lo, n in ((0, 64), (64, 64), (128, 32)):
            lk0, lk1 = sub(LK, lo, n), sub(LK, lo + 32, n)
            gone = [(I(-8192.0), lk1), (I(4096.0), sub(bp, lo, n))] if lo < 128 else []
            if not last:
                t2 = mm(("ps6", 0, n, 1), [(ID, sub(HB, lo, n)), (ID, sub(LY, lo, n)), (I(16384.0), lk0), (I(-16384.0), lk1)])
                r2 = act(f(n), t2, ACT.Identity, bias=CW - 16384.0 + 9.0 / 32 - (4096.0 if lo < 128 else 0.0))
                t1 = mm(vp(288, n), [(ID, sub(HB, lo, n)), (ID, sub(LA, lo, n)), (I(-4096.0), sub(SG, lo, n)),
                                     (I(4096.0), sub(SG, lo + 32, n)), (I(9.0 / 32), lk0)] + gone)
            if lo < 128:
                nd = mm(vp(224, n), [(ID, DC), (ID, DR), (I(-8192.0), lk1)])
                tk = mm(vp(160, n), [(I(4096.0), sub(KO, 96 + lo, n))] + gone)
            mm(sub(US, lo, n), [(ID, lk0), (IDN, lk1)])
            if not last:
                tt(sub(BA, lo, n), t1, r2, A.max)
                if lo == 0:
                    ts(sub(a16, 0, 32), sub(BA, 0, 32), 4096.0 - 9.0 / 32, A.add)
            if lo < 128:
                tt(sub(xd, lo, n), nd, sub(xi, lo, n), A.max)
                tt(sub(ACk, lo, n), tk, sub(ACa, lo, n), A.min)
        if t == 1:
            rotd = f(192)
            for k, src in enumerate((keys[0], losers[0])):
                for o in range(3):
                    rotate(("ps7", 32 * o, 32, 1), sub(src, 32 * o, 32), off, PM)
                act(sub(rotd, 96 * k, 96), ("ps7", 0, 96, 1), ACT.Copy)
        AN = f(160)
        st2 = {"cur": sub(AN, 0, 32)}

        def root(o, y):
            if not last:
                tt(sub(AN, 32 * o, 32), tt(f(), sub(US, 32 * o, 32), y, A.mult), sub(ACk, 32 * o, 32), A.add)
                src = (("G", nb, 16 + CW + 1024 * max(o, 1), 1), sub(a16, 32 * o, 32))
                agat(regions(t + 1)[4][o], *src)
                if o >= 1:
                    champion_level(t + 1, o, st2, AN, src)

        scat(m16, Y[0])
        y = m
        p = None
        pend, q16 = [], []
        for o in range(4):
            cm = cm0
            if o > 0:
                cm = fused(new("WB", H), P[o - 1], p, X[o], A.is_lt)
                agat(Y[o], P[o - 1], p)
            p, w = new("U", 32) if o < 3 or LG[t][o] == "n" else None, f()
            sc = count("ps0", cm, o == 0, p, w, 0, sub(LK, 32 * o + 32, 32))
            if not last:
                ts(sub(a16, 32 * o + 32, 32), tt(f(), sc, sub(BA, 32 * o + 32, 32), A.add), (4096.0 if o < 3 else 0.0) - 9.0 / 32, A.add)
            q16.append(cp(new("U", 32), tt(f(), CQ, sc, A.subtract)) if LG[t][o] == "g" else None)
            root(o, y)
            d = tt(f(), y, sub(xd, 32 * o, 32), A.subtract)
            x = tt(f(), w, d, A.mult)
            tt(sub(ls, 32 * o, 32), y, x, A.subtract)
            y = tt(sub(ky, 32 * o + 32, 32), sub(xd, 32 * o, 32), x, A.add)
            if o not in PAIR[t]:
                k0 = len(pend)
                both = cp(new("U", 32 * (o + 1 - k0)), sub(ls, 32 * k0, 32 * (o + 1 - k0)))
                pend += [sub(both, 32 * k, 32) for k in range(o + 1 - k0)]
        root(4, y)
        if last:
            rk = tt(f(160), ACk, mm(("ps1", 0, 160, 1), [(I(4096.0), sub(KO, 0, 160))]), A.subtract)
            tt(("YR", 0, 160, 1), tt(US, US, ky, A.mult), rk, A.add)
        for o in range(4):
            b1 = (("ps2", "ps4")[o % 2], 0, H, 1)
            if LG[t][o] == "n":
                pn, nw = new("WB", 2 * H), new("WB", H)
                sg = act(new("WB", H), mm(b1, [(ID, Y[o]), (IDN, X[o])]), ACT.Sign)
                act(sub(pn, 0, H, 2), mm(("ps5", 0, H, 1), [(ID, Y[o]), (IDN, sg)]), ACT.Copy)
                act(sub(pn, 1, H, 2), mm(("ps7", 0, H, 1), [(ID, X[o]), (ID, sg)]), ACT.Copy)
                for k in range(2):
                    agat(sub(nw, 256 * k, 256), pn, sub(p, 16 * k, 16))
                scat(pend[o], nw)
            elif LG[t][o] == "p":
                mm(b1, [(ID, X[o]), (ID, Y[o]), (IDN, Y[o + 1])])
                b2 = mm(("ps6", 0, H, 1), [(ID, X[o]), (ID, Y[o]), (I(-2.0), Y[o + 1])])
                scat(pend[o], act(new("WB", H), b1, ACT.Copy), act(new("WB", H), b2, ACT.Sign, scale=-1.0), (t, o))
            elif LG[t][o] == "g":
                old = agat(new("WB", H), P[o], q16[o])
                mm(b1, [(ID, Y[o + 1]), (IDN, old)] if o < 3 else [(ID, X[o]), (ID, Y[o]), (I(-2.0), old)])
                scat(pend[o], old, act(new("WB", H), b1, ACT.Sign), (t, o))
            else:
                old = act(new("WB", H), mm(b1, [(ID, X[o]), (ID, Y[o]), (IDN, Y[o + 1])]), ACT.Copy)
                mm(b1, [(IDN, Y[o + 1]), (ID, old)])
                scat(pend[o], old, act(new("WB", H), b1, ACT.Sign, scale=-1.0), (t, o))
        keys.append(sub(ky, 32, 128))
        losers.append(ls)
        st, AC = st2, AN
    dma("a", T.yrt[:], T.YR[:], [("YR", 0, 160, 1)], [], 80e3)
    dma("s", T.yrec[:], T.G[:, 0:V], [("G", 0, V, 1)], [], 1050e3)
    return ops


def sweep(ops, after, key, first):
    n = len(ops)
    rdy = list(first)
    start = [0.0] * n
    busy = {e: [] for e in "vapgs"}
    for k in sorted(range(n), key=lambda k: key[k]):
        t, c, e = rdy[k], ops[k]["cost"], ops[k]["eng"]
        if e != "x":
            b = busy[e]
            i = len(b)
            while i > 0 and b[i - 1][1] > t:
                i -= 1
            while i < len(b) and b[i][0] < t + c - 1e-9:
                t = max(t, b[i][1])
                i += 1
            b.insert(i, (t, t + c))
        start[k] = t
        for s, lag in after[k]:
            if t + lag > rdy[s]:
                rdy[s] = t + lag
    return start


def justify(ops, suc, rsuc, key):
    n = len(ops)
    fw = sweep(ops, suc, key, [0.0] * n)
    bw = sweep(ops, rsuc, [(-fw[k] - ops[k]["cost"], -k) for k in range(n)], [o["lat"] for o in ops])
    return sweep(ops, suc, [(-bw[k] - ops[k]["cost"], k) for k in range(n)], [0.0] * n)


def replay(ops, dl, order, k, wake, far):
    free = {e: 0.0 for e in "vapgsx"}
    n = len(ops)
    done, fr = [0.0] * n, [0.0] * n
    for c in order:
        o = ops[c]
        e = o["eng"]
        t = free[e]
        for j, w in dl[c]:
            x = done[j] + wake if w else (done[j] - 1.2 if e == "s" else fr[j])
            if x > t:
                t = x
        fr[c] = t + k[o["kind"]] * o["cost"]
        done[c] = fr[c] + o["lat"] + (far if e == "x" else 0.0)
        if e != "x":
            free[e] = fr[c]
    return max(done)


def refine(ops, dl, order, engs, moves, cool, VIEWS):
    n = len(ops)
    eng = ["vapgsx".index(e) for e in engs]
    cost = [[k[o["kind"]] * o["cost"] for o in ops] for k, w, x in VIEWS]
    late = [[o["lat"] + (x if o["eng"] == "x" else 0.0) for o in ops] for k, w, x in VIEWS]
    cls = [1 if o["kind"] == 2 else 2 if "free" in o else 0 for o in ops]
    hard = [[j for j, w in d if w] for d in dl]
    soft = [[j for j, w in d if not w] for d in dl]
    near = [set(j for j, w in d) for d in dl]

    def play(order, v, lo=0, base=None):
        cs, lt, wake = cost[v], late[v], VIEWS[v][1]
        free, who = [0.0] * 6, [-1] * 6
        done, fr, by = ([0.0] * n, [0.0] * n, [-1] * n) if base is None else (base[1][:], base[3][:], base[2][:])
        turn = [-1, []]
        for c in order[:lo]:
            who[eng[c]] = c
            if cls[c] == 1:
                turn[0] = c
            elif cls[c] == 2:
                turn[1].append(c)
        for e in range(5):
            if who[e] >= 0:
                free[e] = fr[who[e]]
        who[5] = -1
        for c in order[lo:]:
            e = eng[c]
            t, b = free[e], -2 - who[e]
            for j in hard[c]:
                x = done[j] + wake
                if x > t:
                    t, b = x, j
            for j in soft[c]:
                x = done[j] - 1.2 if e == 4 else fr[j]
                if x > t:
                    t, b = x, j
            if cls[c] == 2:
                j = turn[0]
                if j >= 0 and done[j] + wake > t:
                    t, b = done[j] + wake, (j if j in near[c] else -2 - j)
                turn[1].append(c)
            elif cls[c] == 1:
                for j in turn[1][-4:]:
                    if done[j] + wake > t:
                        t, b = done[j] + wake, (j if j in near[c] else -2 - j)
                turn[0] = c
            t += cs[c]
            fr[c], done[c], by[c] = t, t + lt[c], b
            if e != 5:
                free[e], who[e] = t, c
        return max(done), done, by, fr

    def chain(done, by):
        c, out = done.index(max(done)), []
        while c >= 0:
            b = by[c]
            if b < -1:
                out.append((-2 - b, c))
                b = -2 - b
            c = b
        return out
    got = [play(order, v) for v in range(len(VIEWS))]
    score = sum(x[0] for x in got)
    top = (score, order, list(eng))
    links = [chain(x[1], x[2]) for x in got]
    seed = 4321
    for it in range(moves):
        seed = (seed * 1103515245 + 12345) % 2147483648
        ln = links[(seed >> 8) % len(links)]
        seed = (seed * 1103515245 + 12345) % 2147483648
        a, b = ln[(seed >> 8) % len(ln)]
        seed = (seed * 1103515245 + 12345) % 2147483648
        kind = (seed >> 8) % 8
        flip = -1
        if kind < 2:
            flip = (a, b)[kind]
            if "alt" not in ops[flip]:
                continue
            eng[flip] = 1 - eng[flip]
            new, ia = order, order.index(flip)
        else:
            ia, ib = order.index(a), order.index(b)
            for r in range(kind - 2 if kind < 5 else 0):
                k = ia - 1
                while k >= 0 and eng[order[k]] != eng[b]:
                    k -= 1
                if k >= 0:
                    ia, a = k, order[k]
            seg = order[ia:ib + 1]
            if kind < 5:
                mark, need, es = {b}, set(near[b]), set()
                for x in seg[-2:0:-1]:
                    if x in need or eng[x] in es:
                        mark.add(x)
                        need |= near[x]
                        if eng[x] != 5:
                            es.add(eng[x])
                if a in need or eng[a] in es:
                    continue
                new = order[:ia] + [x for x in seg if x in mark] + [x for x in seg if x not in mark] + order[ib + 1:]
            else:
                more = kind - 5
                while more and ib + 1 < n:
                    ib += 1
                    more -= eng[order[ib]] == eng[a]
                seg = order[ia:ib + 1]
                mark, es = {a}, set()
                for x in seg[1:]:
                    if not mark.isdisjoint(near[x]) or eng[x] in es:
                        mark.add(x)
                        if eng[x] != 5:
                            es.add(eng[x])
                if b in mark:
                    continue
                new = order[:ia] + [x for x in seg if x not in mark] + [x for x in seg if x in mark] + order[ib + 1:]
        seed = (seed * 1103515245 + 12345) % 2147483648
        bound = score + cool * (1.0 - it / moves) * ((seed >> 8) % 1000 / 1000.0) ** 3
        tried, sc = [], 0.0
        for v in range(len(VIEWS)):
            tried.append(play(new, v, ia, got[v]))
            sc += tried[-1][0] - got[v][0]
            if score + sc > bound + 1.0:
                break
        if score + sc <= bound and len(tried) == len(VIEWS):
            order, got, score = new, tried, score + sc
            links = [chain(x[1], x[2]) for x in got]
            if score < top[0]:
                top = (score, order, list(eng))
        elif flip >= 0:
            eng[flip] = 1 - eng[flip]
    eng[:] = top[2]
    return top[1], play(top[1], 0)[1], ["vapgsx"[e] for e in eng], top[0]


def schedule(ops):
    n = len(ops)
    deps = [dict() for _ in range(n)]
    seen = {}
    for k, o in enumerate(ops):
        for j in o["after"]:
            deps[k][j] = o["eng"] != ops[j]["eng"] and o["eng"] != "x"
        for a, wr in [(a, False) for a in o["rd"]] + [(a, True) for a in o["wr"]]:
            for j, b, bw in seen.get(a[0], []):
                if j == k:
                    continue
                other = ops[j]["eng"] != o["eng"]
                if a[0][:2] == "ps" and other:
                    deps[k][j] = True
                elif (wr or bw) and meet(a, b):
                    if o["acc"] and not other and a[0][:2] == "ps":
                        deps[k].setdefault(j, False)
                    else:
                        deps[k][j] = True
                elif a[0][:2] == "ps" and o["eng"] == "p":
                    deps[k].setdefault(j, False)
        for a, wr in [(a, False) for a in o["rd"]] + [(a, True) for a in o["wr"]]:
            s = seen.setdefault(a[0], [])
            if a[0][:2] == "ps" and s and ops[s[-1][0]]["eng"] != o["eng"]:
                s[:] = [x for i, x in enumerate(s) if all(ops[y[0]]["eng"] == ops[s[-1][0]]["eng"] for y in s[i:])]
            s.append((k, a, wr))

    def lean():
        return [[(j, w) for j, w in deps[k].items() if not (w and any(deps[i].get(j) for i in deps[k] if i > j))] for k in range(n)]
    dl, suc, rsuc = lean(), [[] for _ in range(n)], [[] for _ in range(n)]
    for k in range(n):
        for j, w in dl[k]:
            lag = ops[j]["cost"] + (ops[j]["lat"] + WAKE if w else ops[j]["lat"] - 1.2 if ops[k]["eng"] == "s" else 0.0)
            suc[j].append((k, lag))
            rsuc[k].append((j, lag + ops[k]["cost"] - ops[j]["cost"]))
    tail = [0.0] * n
    for k in range(n - 1, -1, -1):
        tail[k] = max([ops[k]["cost"] + ops[k]["lat"]] + [tail[s] + lag for s, lag in suc[k]])

    def weigh(st):
        order = sorted(range(n), key=lambda k: (st[k], k))
        return sum(replay(ops, dl, order, k, w, x) for k, w, x in VIEWS), order
    for k, o in enumerate(ops):
        for j in list(deps[k]):
            if (o["kind"] == 2 and "free" in ops[j]) or (ops[j]["kind"] == 2 and j not in o.get("free", [j])):
                del deps[k][j]
    dl2 = lean()
    for k, o in enumerate(ops):
        if "end" in o and "end" in ops[k - 1]:
            del deps[k][k - 1]
    dl3 = lean()
    top = None
    for seed in SEEDS:
        best = justify(ops, suc, rsuc, [(-tail[k], k) for k in range(n)])
        score, order = weigh(best)
        for it in range(TRIES):
            key = list(best)
            seed = (seed * 1103515245 + 12345) % 2147483648
            lo = (seed >> 8) % 1000 / 1000.0 * max(best)
            seed = (seed * 1103515245 + 12345) % 2147483648
            amp = SHAKE * ((seed >> 8) % 1000 / 1000.0) ** 2
            for k in range(n):
                if lo <= best[k] < lo + SPAN:
                    seed = (seed * 1103515245 + 12345) % 2147483648
                    key[k] += amp * ((seed >> 8) % 2001 - 1000) / 1000.0
            for k in range(n):
                for j, w in dl[k]:
                    if key[j] > key[k]:
                        key[k] = key[j]
            near = [k for k in range(n) if "alt" in ops[k] and lo <= best[k] < lo + SPAN]
            flip = []
            for r in range(it % 3 if near else 0):
                seed = (seed * 1103515245 + 12345) % 2147483648
                flip.append(near[(seed >> 8) % len(near)])
                swap(ops[flip[-1]])
            got = justify(ops, suc, rsuc, [(key[k], k) for k in range(n)])
            sc, od = weigh(got)
            if sc <= score:
                best, score, order = got, sc, od
            else:
                for k in flip:
                    swap(ops[k])
        got = refine(ops, dl2, order, [o["eng"] for o in ops], MOVES, COOL, VIEWS)
        if top is None or got[3] < top[3]:
            top = got
    order, done, engs = refine(ops, dl2, top[0], top[2], MORE, COOL, VIEWS + FAR)[:3]
    order, done, engs = refine(ops, dl3, order, engs, LAST, COOL / 2, VIEWS + FAR + (((1.35, 1.6, 2.4, 1.35), 0.2, 3.0),) * 2)[:3]
    turns = []
    for k in order:
        if ops[k]["kind"] == 2 or "free" in ops[k]:
            for j in turns:
                if (ops[j]["kind"] == 2) != (ops[k]["kind"] == 2):
                    deps[k][j] = True
            turns.append(k)
    return order, deps, [done[k] - ops[k]["cost"] - ops[k]["lat"] for k in range(n)], done, engs


def rank_program(g, core, T, topo):
    rank = T.rank_of(core)
    if rank is None:
        return
    nxt = T.cores[(rank + 1) % len(T.cores)]
    neng = len(topo.engines(core, nxt))
    ops = build(g, T, topo.addr(nxt), topo.mask(core, nxt), neng)
    if "plan" not in PLAN:
        PLAN["plan"] = schedule(ops)
    order, deps, start, done, engs = PLAN["plan"]
    for o, e in zip(ops, engs):
        if o["eng"] != e:
            swap(o)
    for k in order:
        if "end" in ops[k]:
            ops[k]["end"][0][0] = ops[k]["end"][1]
    queue = {"v": g.vector, "a": g.scalar, "p": g.tensor, "g": g, "s": g.sync}
    total, mark, clock = {}, {}, {}
    known = {e: {} for e in queue}
    sends = 0
    for k in order:
        o = ops[k]
        e = o["eng"]
        if e == "x":
            mark[k] = o["sem"]
            clock[k] = {o["sem"][0]: o["sem"][1]}
            total[o["sem"][0]] = o["sem"][1]
            continue
        need = {}
        for j in deps[k]:
            if deps[k][j]:
                s, c = mark[j]
                if c > need.get(s, (0, 0))[0]:
                    need[s] = (c, j)
        for s, (c, j) in sorted(need.items(), key=lambda x: -done[x[1][1]]):
            if known[e].get(s, 0) < c:
                queue[e].wait_ge(T.sem[s], c)
                for s2, c2 in clock[j].items():
                    known[e][s2] = max(known[e].get(s2, 0), c2)
        ins = o["fn"]()
        if o["sem"] is None:
            s = "c" + e
            total[s] = total.get(s, 0) + 1
            ins.then_inc(T.sem[s], 1)
            mark[k] = (s, total[s])
        elif o["sem"][0] == "":
            sends += neng
            continue
        else:
            s = o["sem"][0]
            ins.then_inc(T.sem[s], 16)
            total[s] = 16
            mark[k] = (s, 16)
        clock[k] = dict(known[e])
        clock[k][s] = total[s]
    total["sent"] = sends
    for s in total:
        g.wait_ge(T.sem[s], total[s])
